import numpy as np
import ml_dtypes


def mxq(x, axis, fmt="e4m3"):
    dtype, down = {"e4m3": (ml_dtypes.float8_e4m3fn, 7), "e5m2": (ml_dtypes.float8_e5m2, 14)}[fmt]
    v = np.moveaxis(np.asarray(x, np.float32).astype(ml_dtypes.bfloat16).astype(np.float64), axis, -1)
    blocks = v.reshape(v.shape[:-1] + (-1, 32))
    amax = np.abs(blocks).max(-1, keepdims=True)
    byte = np.maximum(np.where(amax > 0, np.frexp(amax)[1] - 1 + 127, 0) - down, 1)
    scale = np.exp2(byte - 127.0)
    codes = (blocks / scale).astype(np.float32).astype(dtype).astype(np.float64)
    return np.moveaxis((codes * scale).reshape(v.shape), -1, axis)


WIDE = False


def mx_kscale(k):
    if not WIDE:
        return np.ones(k)
    levels = np.array([10, -10, 5, -5, 0])
    if k % 512:
        return np.exp2(np.random.permutation(np.resize(levels, k // 32))).repeat(32)
    a = np.empty((k // 512, 16))
    for p in range(k // 512):
        a[p, :8] = np.random.permutation(np.resize(levels, 8))
        for g in range(8):
            far = levels[np.abs(levels - a[p, g]) >= 10]
            a[p, g + 8] = far[np.random.randint(len(far))]
    return np.exp2(a.ravel()).repeat(32)


def f64(x):
    return np.asarray(x).astype(np.float64)


def striped(idx):
    return np.tile(idx.reshape(-1, 16).T, (8, 1)).astype(np.uint16)


def unstriped(offs):
    return offs[:16].T.reshape(-1).astype(np.int64)


E2M1 = np.array([0.0, 0.5, 1.0, 1.5, 2.0, 3.0, 4.0, 6.0, -0.0, -0.5, -1.0, -1.5, -2.0, -3.0, -4.0, -6.0])


def pack_weight(w, fmt):
    k, n = w.shape
    w = f64(np.asarray(w, np.float32).astype(ml_dtypes.bfloat16)).reshape(k // 32, 32, n)
    amax = np.abs(w).max(1)
    if fmt == "e4m3":
        byte = np.frexp(amax)[1] - 1 + 127 - 7
    else:
        mant, ex = np.frexp(amax / 6.0)
        byte = np.where(mant > 0.5, ex, ex - 1) + 127
    byte = np.clip(np.where(amax > 0, byte, 1), 1, 254)
    scaled = (w * np.exp2(127.0 - byte)[:, None, :]).reshape(k, n).astype(np.float32)
    by_word = np.ascontiguousarray(scaled.reshape(k // 512, 128, 4, n).transpose(0, 1, 3, 2))
    if fmt == "e4m3":
        words = by_word.astype(ml_dtypes.float8_e4m3fn).view(np.uint8)
    else:
        c = by_word.astype(ml_dtypes.float4_e2m1fn).view(np.uint8) & 0xF
        words = (c[..., 0::2] | (c[..., 1::2] << 4)).reshape(k // 512, 128, 2 * n)
    return np.ascontiguousarray(words), np.ascontiguousarray(byte.astype(np.uint8).reshape(k // 512, 16, n))


def unpack_weight(words, scales, fmt):
    g, _, n = scales.shape
    words = np.ascontiguousarray(words).reshape(g, 128, n, -1)
    if fmt == "e4m3":
        vals = words.view(ml_dtypes.float8_e4m3fn).astype(np.float64)
    else:
        nib = np.empty((g, 128, n, 4), np.uint8)
        nib[..., 0::2] = words & 0xF
        nib[..., 1::2] = words >> 4
        vals = E2M1[nib]
    vals = vals * np.repeat(np.exp2(scales.astype(np.float64) - 127.0), 8, axis=1)[..., None]
    return vals.transpose(0, 1, 3, 2).reshape(g * 512, n)


def gelu(v):
    return 0.5 * v * (1.0 + np.tanh(np.sqrt(2.0 / np.pi) * (v + 0.044715 * v**3)))


K, H, T, S, P = 1024, 1024, 4096, 1024, 512

def setup_inputs():
    n = np.random.standard_normal
    s = mx_kscale(K)[:, None]
    u = mx_kscale(H)[:, None]
    tab_words, tab_scales = pack_weight(n((K, T)) * s, "e4m3")
    w1_words, w1_scales = pack_weight(n((K, H)) / np.sqrt(K) / s, "e2m1")
    return {
        "tab_words": tab_words, "tab_scales": tab_scales,
        "offs": striped(np.random.permutation(T)[:S]),
        "w1_words": w1_words, "w1_scales": w1_scales,
        "b1": (0.4 * n(H)).astype(np.float32),
        "pos1": striped(np.random.permutation(S)[:P]),
        "gain": (np.exp(0.3 * n(H)) * u[:, 0]).astype(np.float32),
        "w2": (1.4 * n((H, H)) / np.sqrt(H) / u).astype(np.float32),
        "b2": (0.4 * n(H)).astype(np.float32),
        "pos2": striped(np.random.permutation(S)[:P]),
        "skip": np.exp(0.3 * n(H)).astype(np.float32),
    }

def reference(tab_words, tab_scales, offs, w1_words, w1_scales, b1, pos1, gain, w2, b2, pos2, skip):
    v = unpack_weight(tab_words, tab_scales, "e4m3")[:, unstriped(offs)]
    w1 = unpack_weight(w1_words, w1_scales, "e2m1")
    h = (w1.T @ v) + f64(b1)[:, None]
    x = f64(gain)[:, None] * np.tanh(h[:, unstriped(pos1)])
    y = (mxq(f64(w2), 0, "e4m3").T @ mxq(x, 0, "e4m3")) + f64(b2)[:, None]
    enc = f64(skip)[:, None] * h[:, unstriped(pos2)]
    return np.maximum(y, enc)

@@ -1,0 +1,222 @@
+from contextlib import ExitStack
+
+import concourse.mybir as mybir
+from concourse.masks import make_identity
+
+K, H, T, S, M = 1024, 1024, 4096, 1024, 512
+FLOPS = 2 * K * H * S + 2 * H * H * M
+
+F32 = mybir.dt.float32
+BF16 = mybir.dt.bfloat16
+I32 = mybir.dt.int32
+U32 = mybir.dt.uint32
+U16 = mybir.dt.uint16
+U8 = mybir.dt.uint8
+FP8X4 = mybir.dt.float8_e4m3fn_x4
+FP4X4 = mybir.dt.float4_e2m1fn_x4
+ALU = mybir.AluOpType
+ACT = mybir.ActivationFunctionType
+
+P = 128
+N = 512
+GAIN, B2, SKIP = 0, 1, 2
+
+
+def tile_list_dental_unet_skip_kernel(
+    tc, tab_words, tab_scales, offs, w1_words, w1_scales, b1, pos1, gain, w2, b2, pos2, skip, out
+):
+    nc = tc.nc
+    with ExitStack() as ctx:
+        keep = ctx.enter_context(tc.tile_pool(name="keep", bufs=1))
+        head = ctx.enter_context(tc.tile_pool(name="head", bufs=1))
+        psum = ctx.enter_context(tc.psum_pool(name="psum", bufs=4))
+
+        offs_sb = keep.tile([P, S // 16], U16, name="offs_sb")
+        pos1_sb = keep.tile([P, M // 16], U16, name="pos1_sb")
+        pos2_sb = keep.tile([P, M // 16], U16, name="pos2_sb")
+        nc.sync.dma_start(offs_sb[:], offs)
+        nc.sync.dma_start(pos1_sb[:], pos1)
+        nc.sync.dma_start(pos2_sb[:], pos2)
+
+        tab_s = head.tile([P, T], U8, name="tab_s", align_bytes=64, offset=2048)
+        nc.vector.memset(tab_s[:].bitcast(I32), 0)
+        for q in range(4):
+            nc.gpsimd.dma_start(
+                tab_s[32 * q : 32 * q + 8, :].bitcast(I32), tab_scales[:, 4 * q : 4 * q + 4, :].bitcast(I32)
+            )
+
+        tab_w = [keep.tile([P, T], I32, name="tab_w%d" % a, tag="stage%d" % a, align_bytes=64) for a in range(2)]
+        w1w_raw = keep.tile([P, 2 * 512], I32, name="w1w_raw", align_bytes=64)
+        nc.sync.dma_start(tab_w[0][:], tab_words[0].rearrange("p n t -> p (n t)").bitcast(I32))
+        nc.sync.dma_start(
+            w1w_raw[:].rearrange("p (a n) -> p a n", a=2), w1_words.rearrange("a p n -> p a n").bitcast(I32)
+        )
+        nc.sync.dma_start(tab_w[1][:], tab_words[1].rearrange("p n t -> p (n t)").bitcast(I32))
+
+        w1s_raw = keep.tile([P, 2 * 256], I32, name="w1s_raw", align_bytes=64)
+        nc.vector.memset(w1s_raw[:], 0)
+        for q in range(4):
+            nc.scalar.dma_start(
+                w1s_raw[32 * q : 32 * q + 4, :].rearrange("r (a n) -> r a n", a=2),
+                w1_scales[:, 4 * q : 4 * q + 4, :].rearrange("a r n -> r a n").bitcast(I32),
+            )
+
+        def load_rows(name, vecs, queue):
+            rows = keep.tile([P, 2 * P], F32, name=name)
+            nc.vector.memset(rows[:], 0.0)
+            for v, vec in enumerate(vecs):
+                queue.dma_start(
+                    rows[4 * v : 4 * v + 4, :].rearrange("t (g i) -> t g i", i=8),
+                    vec.rearrange("(g t i) -> t g i", t=4, i=8),
+                )
+            return rows
+
+        b1_rows = load_rows("b1_rows", (b1,), nc.scalar)
+        late_rows = load_rows("late_rows", (gain, b2, skip), nc.gpsimd)
+        ident = keep.tile([P, P], F32, name="ident")
+        make_identity(nc, ident[:])
+
+        zero_in = keep.tile([P, 8], F32, name="zero_in")
+        zero = keep.tile([P, 8], F32, name="zero")
+        nc.vector.memset(zero_in[:], 0.0)
+        nc.scalar.activation(zero[:, 0:1], zero_in[:, 0:1], ACT.Tanh)
+
+        v_s1 = keep.tile([P, S], U8, name="v_s1", align_bytes=64)
+        nc.vector.memset(v_s1[:].bitcast(I32), 0)
+
+        v_s0 = keep.tile([P, S], U8, name="v_s0", align_bytes=64)
+        nc.vector.tensor_copy(v_s0[:], tab_s[:].indirect(offs_sb[:]))
+        nc.scalar.dma_start(v_s1[0:112, :].bitcast(I32), v_s0[4:116, :].bitcast(I32))
+        v_s = (v_s0, v_s1)
+
+        v_w0 = head.tile([P, S], I32, name="v_w0", align_bytes=64, offset=0)
+        nc.vector.tensor_copy(v_w0[:].bitcast(U32), tab_w[0][:].bitcast(U32).indirect(offs_sb[:]))
+
+        w1w = head.tile([P, 2 * 512], I32, name="w1w", align_bytes=64, offset=4096)
+        nc.vector.tensor_copy(
+            w1w[:].rearrange("p (c t g q) -> p c t g q", c=4, t=4, g=16),
+            w1w_raw[:].rearrange("p (c g t q) -> p c t g q", c=4, t=4, g=16),
+        )
+        w1s = keep.tile([P, 2 * 256], I32, name="w1s", align_bytes=64)
+        nc.vector.tensor_copy(
+            w1s[:].rearrange("p (c t g q) -> p c t g q", c=4, t=4, g=16),
+            w1s_raw[:].rearrange("p (c g t q) -> p c t g q", c=4, t=4, g=16),
+        )
+
+        def turn(name, rows, count):
+            turned = psum.tile([P, N], F32, name="turned", tag="dec_bank")
+            for b in range(2):
+                nc.tensor.transpose(turned[:, b * P : (b + 1) * P], rows[:, b * P : (b + 1) * P], ident[:])
+            cols = keep.tile([P, 2, 4 * count], F32, name=name)
+            nc.scalar.copy(cols[:], turned[:, 0 : 2 * P].rearrange("p (b r) -> p b r", b=2)[:, :, 0 : 4 * count])
+            return cols
+
+        def col(cols, v, j):
+            return cols[:, j // 4, 4 * v + j % 4 : 4 * v + j % 4 + 1]
+
+        b1_cols = turn("b1_cols", b1_rows, 1)
+
+        v_w1 = [keep.tile([P, N], I32, name="v_w1_%d" % half, align_bytes=64) for half in range(2)]
+        for half in range(2):
+            nc.vector.tensor_copy(
+                v_w1[half][:].bitcast(U32),
+                tab_w[1][:].bitcast(U32).indirect(offs_sb[:, 32 * half : 32 * half + 32]),
+            )
+
+        w2_raw = [keep.tile([P, 4 * H], F32, name="w2_raw%d" % b, tag="stage%d" % b, align_bytes=64) for b in range(2)]
+        w2_rows = w2.rearrange("(b g t i) n -> b t g i n", b=2, t=4, i=8)
+        for b in range(2):
+            for t in range(4):
+                nc.sync.dma_start(w2_raw[b][:, t * H : (t + 1) * H], w2_rows[b, t])
+
+        h = [keep.tile([P, S], F32, name="h%d" % j) for j in range(8)]
+        g1 = [keep.tile([P, M], F32, name="g1_%d" % j, tag="g1_%d" % j) for j in range(8)]
+        g2 = {}
+        res = [keep.tile([P, M], F32, name="res%d" % j) for j in range(8)]
+        enc = [keep.tile([P, M], F32, name="enc%d" % j) for j in range(8)]
+        th = [keep.tile([P, 4 * M], F32, name="th%d" % b, tag="th%d" % b) for b in range(2)]
+        x_bf = [keep.tile([P, 4 * M], BF16, name="x_bf%d" % b, align_bytes=64) for b in range(2)]
+        x_w = [keep.tile([P, M], U32, name="x_w%d" % b, align_bytes=64) for b in range(2)]
+        x_s = [keep.tile([P, M], U8, name="x_s%d" % b, align_bytes=64) for b in range(2)]
+        w2_bf = [keep.tile([P, 4 * N], BF16, name="w2_bf%d" % c, align_bytes=64) for c in range(4)]
+        w2_w = [keep.tile([P, N], U32, name="w2_w%d" % c, align_bytes=64) for c in range(4)]
+        w2_s = [keep.tile([P, N], U8, name="w2_s%d" % c, align_bytes=64) for c in range(4)]
+
+        def encode(j):
+            for half in range(2):
+                acc = psum.tile([P, N], F32, name="acc", tag="enc_bank")
+                cols = slice(half * N, (half + 1) * N)
+                for a in range(2):
+                    words = v_w0[:, cols] if a == 0 else v_w1[half][:]
+                    nc.tensor.matmul_mx(
+                        out=acc[:],
+                        lhsT=w1w[:, 512 * a + 64 * j : 512 * a + 64 * (j + 1)].bitcast(FP4X4),
+                        lhsT_scale=w1s[:, 256 * a + 32 * j : 256 * a + 32 * (j + 1)].bitcast(U8),
+                        rhs=words.bitcast(FP8X4),
+                        rhs_scale=v_s[a][:, cols],
+                        start=(a == 0),
+                        stop=(a == 1),
+                    )
+                nc.scalar.activation(h[j][:, cols], acc[:], ACT.Identity, bias=col(b1_cols, 0, j))
+            nc.vector.tensor_copy(g1[j][:], h[j][:].indirect(pos1_sb[:]))
+
+        def pick_skip(j, tag):
+            g2[j] = keep.tile([P, M], F32, name="g2_%d" % j, tag=tag)
+            nc.vector.tensor_copy(g2[j][:], h[j][:].indirect(pos2_sb[:]))
+
+        def squash(j):
+            b, t = divmod(j, 4)
+            nc.scalar.activation(th[b][:, t * M : (t + 1) * M], g1[j][:], ACT.Tanh, bias=zero[:, 0:1])
+            if t == 3:
+                nc.vector.tensor_tensor(
+                    x_bf[b][:].rearrange("p (c i t) -> p c t i", i=4, t=4),
+                    th[b][:].rearrange("p (t c i) -> p c t i", i=4, t=4),
+                    late_cols[:, b, 4 * GAIN : 4 * GAIN + 4].unsqueeze(1).unsqueeze(3).broadcast_to([P, M // 4, 4, 4]),
+                    ALU.mult,
+                )
+                nc.vector.quantize_mx(out=x_w[b][:].bitcast(FP8X4), scales=x_s[b][:], in_=x_bf[b][:])
+
+        def quantize_w2(c):
+            b, nb = divmod(c, 2)
+            src = w2_raw[b][:].rearrange("p (r nb g t i) -> p nb t g r i", r=4, nb=2, t=4, i=8)[:, nb]
+            nc.scalar.copy(w2_bf[c][:].rearrange("p (t g i r) -> p t g r i", t=4, i=8, r=4), src)
+            nc.vector.quantize_mx(out=w2_w[c][:].bitcast(FP8X4), scales=w2_s[c][:], in_=w2_bf[c][:])
+
+        out_rows = out.rearrange("(b g t i) m -> b t g i m", b=2, t=4, i=8)
+
+        def decode(j):
+            nb, t = divmod(j, 4)
+            acc = psum.tile([P, N], F32, name="acc", tag="dec_bank")
+            for b in range(2):
+                c = 2 * b + nb
+                nc.tensor.matmul_mx(
+                    out=acc[:],
+                    lhsT=w2_w[c][:, t * P : (t + 1) * P].bitcast(FP8X4),
+                    lhsT_scale=w2_s[c][:, t * P : (t + 1) * P],
+                    rhs=x_w[b][:].bitcast(FP8X4),
+                    rhs_scale=x_s[b][:],
+                    start=(b == 0),
+                    stop=(b == 1),
+                )
+            nc.scalar.activation(enc[j][:], g2[j][:], ACT.Copy, scale=col(late_cols, SKIP, j))
+            nc.vector.scalar_tensor_tensor(res[j][:], acc[:], col(late_cols, B2, j), enc[j][:], ALU.add, ALU.max)
+            nc.sync.dma_start(out_rows[nb, t], res[j][:])
+
+        encode(0)
+        pick_skip(0, "g2_0")
+        encode(1)
+        pick_skip(1, "g2_1")
+        late_cols = turn("late_cols", late_rows, 3)
+        for j in range(2, 8):
+            encode(j)
+            if j < 6:
+                pick_skip(j, "g2_%d" % j)
+            squash(j - 2)
+            if 3 <= j <= 6:
+                quantize_w2(j - 3)
+        pick_skip(6, "g1_5")
+        squash(6)
+        squash(7)
+        pick_skip(7, "th1")
+        for j in range(8):
+            decode(j)

@@ -1,7 +1,6 @@
 from contextlib import ExitStack
 
 import concourse.mybir as mybir
-from concourse.masks import make_identity
 
 K, H, T, S, M = 1024, 1024, 4096, 1024, 512
 FLOPS = 2 * K * H * S + 2 * H * H * M
@@ -19,7 +18,6 @@ ACT = mybir.ActivationFunctionType
 
 P = 128
 N = 512
-GAIN, B2, SKIP = 0, 1, 2
 
 
 def tile_list_dental_unet_skip_kernel(
@@ -34,24 +32,38 @@ def tile_list_dental_unet_skip_kernel(
         offs_sb = keep.tile([P, S // 16], U16, name="offs_sb")
         pos1_sb = keep.tile([P, M // 16], U16, name="pos1_sb")
         pos2_sb = keep.tile([P, M // 16], U16, name="pos2_sb")
+
+        def load_channels(queue, tile, vec):
+            queue.dma_start(tile[:, :, 0:4], vec.rearrange("(b p t) -> p b t", b=2, t=4))
+
+        def col(cols, j):
+            return cols[:, j // 4, j % 4 : j % 4 + 1]
+
+        tab_s = head.tile([P, T], U8, name="tab_s", align_bytes=64, offset=0)
+        nc.sync.dma_start(tab_s[0:32, :].bitcast(I32), tab_scales.rearrange("a q n -> (a q) n").bitcast(I32))
         nc.sync.dma_start(offs_sb[:], offs)
         nc.sync.dma_start(pos1_sb[:], pos1)
         nc.sync.dma_start(pos2_sb[:], pos2)
-
-        tab_s = head.tile([P, T], U8, name="tab_s", align_bytes=64, offset=2048)
-        nc.vector.memset(tab_s[:].bitcast(I32), 0)
-        for q in range(4):
-            nc.gpsimd.dma_start(
-                tab_s[32 * q : 32 * q + 8, :].bitcast(I32), tab_scales[:, 4 * q : 4 * q + 4, :].bitcast(I32)
-            )
-
-        tab_w = [keep.tile([P, T], I32, name="tab_w%d" % a, tag="stage%d" % a, align_bytes=64) for a in range(2)]
+        b1_cols = keep.tile([P, 2, 8], F32, name="b1_cols")
+        load_channels(nc.scalar, b1_cols, b1)
         w1w_raw = keep.tile([P, 2 * 512], I32, name="w1w_raw", align_bytes=64)
-        nc.sync.dma_start(tab_w[0][:], tab_words[0].rearrange("p n t -> p (n t)").bitcast(I32))
         nc.sync.dma_start(
             w1w_raw[:].rearrange("p (a n) -> p a n", a=2), w1_words.rearrange("a p n -> p a n").bitcast(I32)
         )
-        nc.sync.dma_start(tab_w[1][:], tab_words[1].rearrange("p n t -> p (n t)").bitcast(I32))
+        tab_w0 = keep.tile([P, T], I32, name="tab_w0", tag="stage0", align_bytes=64)
+        nc.sync.dma_start(tab_w0[:], tab_words[0].rearrange("p n t -> p (n t)").bitcast(I32))
+
+        nc.vector.memset(tab_s[32:64, :].bitcast(I32), 0)
+        nc.vector.memset(tab_s[64:128, :].bitcast(I32), 0)
+
+        zero_in = keep.tile([P, 8], F32, name="zero_in")
+        zero = keep.tile([P, 8], F32, name="zero")
+        nc.vector.memset(zero_in[:], 0.0)
+        nc.scalar.activation(zero[:, 0:1], zero_in[:, 0:1], ACT.Tanh)
+
+        v_s = [keep.tile([P, S], U8, name="v_s%d" % a, align_bytes=64) for a in range(2)]
+        for a in range(2):
+            nc.vector.memset(v_s[a][:].bitcast(I32), 0)
 
         w1s_raw = keep.tile([P, 2 * 256], I32, name="w1s_raw", align_bytes=64)
         nc.vector.memset(w1s_raw[:], 0)
@@ -61,73 +73,54 @@ def tile_list_dental_unet_skip_kernel(
                 w1_scales[:, 4 * q : 4 * q + 4, :].rearrange("a r n -> r a n").bitcast(I32),
             )
 
-        def load_rows(name, vecs, queue):
-            rows = keep.tile([P, 2 * P], F32, name=name)
-            nc.vector.memset(rows[:], 0.0)
-            for v, vec in enumerate(vecs):
-                queue.dma_start(
-                    rows[4 * v : 4 * v + 4, :].rearrange("t (g i) -> t g i", i=8),
-                    vec.rearrange("(g t i) -> t g i", t=4, i=8),
-                )
-            return rows
+        picked_s = keep.tile([P, S], U8, name="picked_s", align_bytes=64)
+        nc.vector.tensor_copy(picked_s[:], tab_s[:].indirect(offs_sb[:]))
 
-        b1_rows = load_rows("b1_rows", (b1,), nc.scalar)
-        late_rows = load_rows("late_rows", (gain, b2, skip), nc.gpsimd)
-        ident = keep.tile([P, P], F32, name="ident")
-        make_identity(nc, ident[:])
+        def move_scales(queue, a, q):
+            row = 16 * a + 4 * q
+            queue.dma_start(v_s[a][32 * q : 32 * q + 4, :].bitcast(I32), picked_s[row : row + 4, :].bitcast(I32))
 
-        zero_in = keep.tile([P, 8], F32, name="zero_in")
-        zero = keep.tile([P, 8], F32, name="zero")
-        nc.vector.memset(zero_in[:], 0.0)
-        nc.scalar.activation(zero[:, 0:1], zero_in[:, 0:1], ACT.Tanh)
+        moves = [(a, q) for a in range(2) for q in range(4)]
+        for a, q in moves[:2]:
+            move_scales(nc.sync, a, q)
+        tab_w1 = head.tile([P, T], I32, name="tab_w1", align_bytes=64, offset=0)
+        nc.sync.dma_start(tab_w1[:], tab_words[1].rearrange("p n t -> p (n t)").bitcast(I32))
+        for a, q in moves[2:]:
+            move_scales(nc.scalar, a, q)
 
-        v_s1 = keep.tile([P, S], U8, name="v_s1", align_bytes=64)
-        nc.vector.memset(v_s1[:].bitcast(I32), 0)
-
-        v_s0 = keep.tile([P, S], U8, name="v_s0", align_bytes=64)
-        nc.vector.tensor_copy(v_s0[:], tab_s[:].indirect(offs_sb[:]))
-        nc.scalar.dma_start(v_s1[0:112, :].bitcast(I32), v_s0[4:116, :].bitcast(I32))
-        v_s = (v_s0, v_s1)
-
-        v_w0 = head.tile([P, S], I32, name="v_w0", align_bytes=64, offset=0)
-        nc.vector.tensor_copy(v_w0[:].bitcast(U32), tab_w[0][:].bitcast(U32).indirect(offs_sb[:]))
-
-        w1w = head.tile([P, 2 * 512], I32, name="w1w", align_bytes=64, offset=4096)
+        w1w = keep.tile([P, 2 * 512], I32, name="w1w", align_bytes=64)
         nc.vector.tensor_copy(
-            w1w[:].rearrange("p (c t g q) -> p c t g q", c=4, t=4, g=16),
-            w1w_raw[:].rearrange("p (c g t q) -> p c t g q", c=4, t=4, g=16),
+            w1w[:].bitcast(U16).rearrange("p (c t m) -> p c t m", c=4, t=4),
+            w1w_raw[:].bitcast(U16).rearrange("p (c m t) -> p c t m", c=4, t=4),
         )
         w1s = keep.tile([P, 2 * 256], I32, name="w1s", align_bytes=64)
         nc.vector.tensor_copy(
-            w1s[:].rearrange("p (c t g q) -> p c t g q", c=4, t=4, g=16),
-            w1s_raw[:].rearrange("p (c g t q) -> p c t g q", c=4, t=4, g=16),
+            w1s[:].bitcast(U8).rearrange("p (c t m) -> p c t m", c=4, t=4),
+            w1s_raw[:].bitcast(U8).rearrange("p (c m t) -> p c t m", c=4, t=4),
         )
 
-        def turn(name, rows, count):
-            turned = psum.tile([P, N], F32, name="turned", tag="dec_bank")
-            for b in range(2):
-                nc.tensor.transpose(turned[:, b * P : (b + 1) * P], rows[:, b * P : (b + 1) * P], ident[:])
-            cols = keep.tile([P, 2, 4 * count], F32, name=name)
-            nc.scalar.copy(cols[:], turned[:, 0 : 2 * P].rearrange("p (b r) -> p b r", b=2)[:, :, 0 : 4 * count])
-            return cols
-
-        def col(cols, v, j):
-            return cols[:, j // 4, 4 * v + j % 4 : 4 * v + j % 4 + 1]
-
-        b1_cols = turn("b1_cols", b1_rows, 1)
-
+        v_w0 = keep.tile([P, S], I32, name="v_w0", align_bytes=64)
+        nc.vector.tensor_copy(v_w0[:].bitcast(U32), tab_w0[:].bitcast(U32).indirect(offs_sb[:]))
         v_w1 = [keep.tile([P, N], I32, name="v_w1_%d" % half, align_bytes=64) for half in range(2)]
         for half in range(2):
             nc.vector.tensor_copy(
                 v_w1[half][:].bitcast(U32),
-                tab_w[1][:].bitcast(U32).indirect(offs_sb[:, 32 * half : 32 * half + 32]),
+                tab_w1[:].bitcast(U32).indirect(offs_sb[:, 32 * half : 32 * half + 32]),
             )
 
-        w2_raw = [keep.tile([P, 4 * H], F32, name="w2_raw%d" % b, tag="stage%d" % b, align_bytes=64) for b in range(2)]
-        w2_rows = w2.rearrange("(b g t i) n -> b t g i n", b=2, t=4, i=8)
-        for b in range(2):
-            for t in range(4):
-                nc.sync.dma_start(w2_raw[b][:, t * H : (t + 1) * H], w2_rows[b, t])
+        w2_raw = [
+            keep.tile([P, 4 * H], F32, name="w2_raw0", tag="stage0", align_bytes=64),
+            head.tile([P, 4 * H], F32, name="w2_raw1", align_bytes=64, offset=256),
+        ]
+        w2_rows = w2.rearrange("(b p r) n -> b p (r n)", b=2, r=4)
+        nc.sync.dma_start(w2_raw[0][:], w2_rows[0])
+        gain_cols = head.tile([P, 2, 8], F32, name="gain_cols", align_bytes=64, offset=0)
+        skip_cols = head.tile([P, 2, 8], F32, name="skip_cols", align_bytes=64, offset=64)
+        b2_cols = head.tile([P, 2, 8], F32, name="b2_cols", align_bytes=64, offset=128)
+        load_channels(nc.sync, gain_cols, gain)
+        load_channels(nc.sync, skip_cols, skip)
+        load_channels(nc.sync, b2_cols, b2)
+        nc.sync.dma_start(w2_raw[1][:], w2_rows[1])
 
         h = [keep.tile([P, S], F32, name="h%d" % j) for j in range(8)]
         g1 = [keep.tile([P, M], F32, name="g1_%d" % j, tag="g1_%d" % j) for j in range(8)]
@@ -157,7 +150,7 @@ def tile_list_dental_unet_skip_kernel(
                         start=(a == 0),
                         stop=(a == 1),
                     )
-                nc.scalar.activation(h[j][:, cols], acc[:], ACT.Identity, bias=col(b1_cols, 0, j))
+                nc.scalar.activation(h[j][:, cols], acc[:], ACT.Identity, bias=col(b1_cols, j))
             nc.vector.tensor_copy(g1[j][:], h[j][:].indirect(pos1_sb[:]))
 
         def pick_skip(j, tag):
@@ -171,22 +164,25 @@ def tile_list_dental_unet_skip_kernel(
                 nc.vector.tensor_tensor(
                     x_bf[b][:].rearrange("p (c i t) -> p c t i", i=4, t=4),
                     th[b][:].rearrange("p (t c i) -> p c t i", i=4, t=4),
-                    late_cols[:, b, 4 * GAIN : 4 * GAIN + 4].unsqueeze(1).unsqueeze(3).broadcast_to([P, M // 4, 4, 4]),
+                    gain_cols[:, b, 0:4].unsqueeze(1).unsqueeze(3).broadcast_to([P, M // 4, 4, 4]),
                     ALU.mult,
                 )
                 nc.vector.quantize_mx(out=x_w[b][:].bitcast(FP8X4), scales=x_s[b][:], in_=x_bf[b][:])
 
+        def scale_skip(j):
+            nc.scalar.activation(enc[j][:], g2[j][:], ACT.Copy, scale=col(skip_cols, j))
+
         def quantize_w2(c):
             b, nb = divmod(c, 2)
-            src = w2_raw[b][:].rearrange("p (r nb g t i) -> p nb t g r i", r=4, nb=2, t=4, i=8)[:, nb]
-            nc.scalar.copy(w2_bf[c][:].rearrange("p (t g i r) -> p t g r i", t=4, i=8, r=4), src)
+            src = w2_raw[b][:].rearrange("p (r nb m t) -> p nb m t r", r=4, nb=2, t=4)[:, nb]
+            nc.scalar.copy(w2_bf[c][:].rearrange("p (t m r) -> p m t r", t=4, r=4), src)
             nc.vector.quantize_mx(out=w2_w[c][:].bitcast(FP8X4), scales=w2_s[c][:], in_=w2_bf[c][:])
 
-        out_rows = out.rearrange("(b g t i) m -> b t g i m", b=2, t=4, i=8)
+        out_rows = out.rearrange("(b p t) m -> b t p m", b=2, t=4)
 
         def decode(j):
             nb, t = divmod(j, 4)
-            acc = psum.tile([P, N], F32, name="acc", tag="dec_bank")
+            acc = psum.tile([P, N], F32, name="acc", tag="dec_bank" if j < 4 else "enc_bank")
             for b in range(2):
                 c = 2 * b + nb
                 nc.tensor.matmul_mx(
@@ -198,25 +194,36 @@ def tile_list_dental_unet_skip_kernel(
                     start=(b == 0),
                     stop=(b == 1),
                 )
-            nc.scalar.activation(enc[j][:], g2[j][:], ACT.Copy, scale=col(late_cols, SKIP, j))
-            nc.vector.scalar_tensor_tensor(res[j][:], acc[:], col(late_cols, B2, j), enc[j][:], ALU.add, ALU.max)
+            nc.vector.scalar_tensor_tensor(res[j][:], acc[:], col(b2_cols, j), enc[j][:], ALU.add, ALU.max)
             nc.sync.dma_start(out_rows[nb, t], res[j][:])
 
-        encode(0)
-        pick_skip(0, "g2_0")
-        encode(1)
-        pick_skip(1, "g2_1")
-        late_cols = turn("late_cols", late_rows, 3)
-        for j in range(2, 8):
+        for j in range(3):
             encode(j)
-            if j < 6:
-                pick_skip(j, "g2_%d" % j)
-            squash(j - 2)
-            if 3 <= j <= 6:
-                quantize_w2(j - 3)
+            pick_skip(j, "g2_%d" % j)
+        quantize_w2(0)
+        encode(3)
+        pick_skip(3, "g2_3")
+        squash(0)
+        encode(4)
+        pick_skip(4, "g2_4")
+        squash(1)
+        squash(2)
+        encode(5)
+        pick_skip(5, "g2_5")
+        squash(3)
+        quantize_w2(1)
+        encode(6)
+        squash(4)
+        encode(7)
+        squash(5)
         pick_skip(6, "g1_5")
+        quantize_w2(2)
         squash(6)
         squash(7)
         pick_skip(7, "th1")
+        scale_skip(0)
+        quantize_w2(3)
         for j in range(8):
+            if j > 0:
+                scale_skip(j)
             decode(j)

@@ -46,6 +46,8 @@ def tile_list_dental_unet_skip_kernel(
         nc.sync.dma_start(pos2_sb[:], pos2)
         b1_cols = keep.tile([P, 2, 8], F32, name="b1_cols")
         load_channels(nc.scalar, b1_cols, b1)
+        skip_cols = keep.tile([P, 2, 8], F32, name="skip_cols")
+        load_channels(nc.gpsimd, skip_cols, skip)
         w1w_raw = keep.tile([P, 2 * 512], I32, name="w1w_raw", align_bytes=64)
         nc.sync.dma_start(
             w1w_raw[:].rearrange("p (a n) -> p a n", a=2), w1_words.rearrange("a p n -> p a n").bitcast(I32)
@@ -108,6 +110,10 @@ def tile_list_dental_unet_skip_kernel(
                 tab_w1[:].bitcast(U32).indirect(offs_sb[:, 32 * half : 32 * half + 32]),
             )
 
+        skip_wide = [keep.tile([P, M], F32, name="skip_wide%d" % j) for j in range(8)]
+        for j in range(8):
+            nc.scalar.activation(skip_wide[j][:], col(skip_cols, j).to_broadcast([P, M]), ACT.Copy)
+
         w2_raw = [
             keep.tile([P, 4 * H], F32, name="w2_raw0", tag="stage0", align_bytes=64),
             head.tile([P, 4 * H], F32, name="w2_raw1", align_bytes=64, offset=256),
@@ -115,18 +121,15 @@ def tile_list_dental_unet_skip_kernel(
         w2_rows = w2.rearrange("(b p r) n -> b p (r n)", b=2, r=4)
         nc.sync.dma_start(w2_raw[0][:], w2_rows[0])
         gain_cols = head.tile([P, 2, 8], F32, name="gain_cols", align_bytes=64, offset=0)
-        skip_cols = head.tile([P, 2, 8], F32, name="skip_cols", align_bytes=64, offset=64)
         b2_cols = head.tile([P, 2, 8], F32, name="b2_cols", align_bytes=64, offset=128)
         load_channels(nc.sync, gain_cols, gain)
-        load_channels(nc.sync, skip_cols, skip)
         load_channels(nc.sync, b2_cols, b2)
         nc.sync.dma_start(w2_raw[1][:], w2_rows[1])
 
         h = [keep.tile([P, S], F32, name="h%d" % j) for j in range(8)]
         g1 = [keep.tile([P, M], F32, name="g1_%d" % j, tag="g1_%d" % j) for j in range(8)]
-        g2 = {}
+        enc = {}
         res = [keep.tile([P, M], F32, name="res%d" % j) for j in range(8)]
-        enc = [keep.tile([P, M], F32, name="enc%d" % j) for j in range(8)]
         th = [keep.tile([P, 4 * M], F32, name="th%d" % b, tag="th%d" % b) for b in range(2)]
         x_bf = [keep.tile([P, 4 * M], BF16, name="x_bf%d" % b, align_bytes=64) for b in range(2)]
         x_w = [keep.tile([P, M], U32, name="x_w%d" % b, align_bytes=64) for b in range(2)]
@@ -154,8 +157,8 @@ def tile_list_dental_unet_skip_kernel(
             nc.vector.tensor_copy(g1[j][:], h[j][:].indirect(pos1_sb[:]))
 
         def pick_skip(j, tag):
-            g2[j] = keep.tile([P, M], F32, name="g2_%d" % j, tag=tag)
-            nc.vector.tensor_copy(g2[j][:], h[j][:].indirect(pos2_sb[:]))
+            enc[j] = keep.tile([P, M], F32, name="enc%d" % j, tag=tag)
+            nc.vector.tensor_tensor(enc[j][:], h[j][:].indirect(pos2_sb[:]), skip_wide[j][:], ALU.mult)
 
         def squash(j):
             b, t = divmod(j, 4)
@@ -169,14 +172,14 @@ def tile_list_dental_unet_skip_kernel(
                 )
                 nc.vector.quantize_mx(out=x_w[b][:].bitcast(FP8X4), scales=x_s[b][:], in_=x_bf[b][:])
 
-        def scale_skip(j):
-            nc.scalar.activation(enc[j][:], g2[j][:], ACT.Copy, scale=col(skip_cols, j))
-
-        def quantize_w2(c):
+        def cast_w2(piece):
+            c, half = divmod(piece, 2)
             b, nb = divmod(c, 2)
-            src = w2_raw[b][:].rearrange("p (r nb m t) -> p nb m t r", r=4, nb=2, t=4)[:, nb]
-            nc.scalar.copy(w2_bf[c][:].rearrange("p (t m r) -> p m t r", t=4, r=4), src)
-            nc.vector.quantize_mx(out=w2_w[c][:].bitcast(FP8X4), scales=w2_s[c][:], in_=w2_bf[c][:])
+            ms = slice(64 * half, 64 * (half + 1))
+            src = w2_raw[b][:].rearrange("p (r nb m t) -> p nb m r t", r=4, nb=2, t=4)[:, nb, ms]
+            nc.scalar.copy(w2_bf[c][:].rearrange("p (t m r) -> p m r t", t=4, r=4)[:, ms], src)
+            if half == 1:
+                nc.vector.quantize_mx(out=w2_w[c][:].bitcast(FP8X4), scales=w2_s[c][:], in_=w2_bf[c][:])
 
         out_rows = out.rearrange("(b p t) m -> b t p m", b=2, t=4)
 
@@ -197,33 +200,18 @@ def tile_list_dental_unet_skip_kernel(
             nc.vector.scalar_tensor_tensor(res[j][:], acc[:], col(b2_cols, j), enc[j][:], ALU.add, ALU.max)
             nc.sync.dma_start(out_rows[nb, t], res[j][:])
 
-        for j in range(3):
+        for j in range(8):
             encode(j)
-            pick_skip(j, "g2_%d" % j)
-        quantize_w2(0)
-        encode(3)
-        pick_skip(3, "g2_3")
-        squash(0)
-        encode(4)
-        pick_skip(4, "g2_4")
-        squash(1)
-        squash(2)
-        encode(5)
-        pick_skip(5, "g2_5")
-        squash(3)
-        quantize_w2(1)
-        encode(6)
-        squash(4)
-        encode(7)
-        squash(5)
+            if j < 6:
+                pick_skip(j, "enc%d" % j)
+            if j >= 2:
+                squash(j - 2)
+                cast_w2(j - 2)
         pick_skip(6, "g1_5")
-        quantize_w2(2)
         squash(6)
+        cast_w2(6)
         squash(7)
         pick_skip(7, "th1")
-        scale_skip(0)
-        quantize_w2(3)
+        cast_w2(7)
         for j in range(8):
-            if j > 0:
-                scale_skip(j)
             decode(j)

@@ -127,14 +127,15 @@ def tile_list_dental_unet_skip_kernel(
         nc.sync.dma_start(w2_raw[1][:], w2_rows[1])
 
         h = [keep.tile([P, S], F32, name="h%d" % j) for j in range(8)]
-        g1 = [keep.tile([P, M], F32, name="g1_%d" % j, tag="g1_%d" % j) for j in range(8)]
+        g1 = [keep.tile([P, M], F32, name="g1_%d" % j, tag="g1_%d" % j, align_bytes=64) for j in range(8)]
         enc = {}
         res = [keep.tile([P, M], F32, name="res%d" % j) for j in range(8)]
-        th = [keep.tile([P, 4 * M], F32, name="th%d" % b, tag="th%d" % b) for b in range(2)]
+        th = [keep.tile([P, M], F32, name="th%d" % j) for j in range(8)]
+        x_rows = [keep.tile([P, 4 * M], BF16, name="x_rows%d" % b, tag="x_rows%d" % b, align_bytes=64) for b in range(2)]
         x_bf = [keep.tile([P, 4 * M], BF16, name="x_bf%d" % b, align_bytes=64) for b in range(2)]
         x_w = [keep.tile([P, M], U32, name="x_w%d" % b, align_bytes=64) for b in range(2)]
         x_s = [keep.tile([P, M], U8, name="x_s%d" % b, align_bytes=64) for b in range(2)]
-        w2_bf = [keep.tile([P, 4 * N], BF16, name="w2_bf%d" % c, align_bytes=64) for c in range(4)]
+        w2_bf = [keep.tile([P, 4 * N], BF16, name="w2_bf%d" % c, tag="w2_bf%d" % c, align_bytes=64) for c in range(4)]
         w2_w = [keep.tile([P, N], U32, name="w2_w%d" % c, align_bytes=64) for c in range(4)]
         w2_s = [keep.tile([P, N], U8, name="w2_s%d" % c, align_bytes=64) for c in range(4)]
 
@@ -157,18 +158,17 @@ def tile_list_dental_unet_skip_kernel(
             nc.vector.tensor_copy(g1[j][:], h[j][:].indirect(pos1_sb[:]))
 
         def pick_skip(j, tag):
-            enc[j] = keep.tile([P, M], F32, name="enc%d" % j, tag=tag)
+            enc[j] = keep.tile([P, M], F32, name="enc%d" % j, tag=tag, align_bytes=64)
             nc.vector.tensor_tensor(enc[j][:], h[j][:].indirect(pos2_sb[:]), skip_wide[j][:], ALU.mult)
 
         def squash(j):
             b, t = divmod(j, 4)
-            nc.scalar.activation(th[b][:, t * M : (t + 1) * M], g1[j][:], ACT.Tanh, bias=zero[:, 0:1])
+            nc.scalar.activation(th[j][:], g1[j][:], ACT.Tanh, bias=zero[:, 0:1])
+            nc.gpsimd.tensor_scalar(x_rows[b][:, t * M : (t + 1) * M], th[j][:], col(gain_cols, j), 0.0, ALU.mult, ALU.add)
             if t == 3:
-                nc.vector.tensor_tensor(
+                nc.vector.tensor_copy(
                     x_bf[b][:].rearrange("p (c i t) -> p c t i", i=4, t=4),
-                    th[b][:].rearrange("p (t c i) -> p c t i", i=4, t=4),
-                    gain_cols[:, b, 0:4].unsqueeze(1).unsqueeze(3).broadcast_to([P, M // 4, 4, 4]),
-                    ALU.mult,
+                    x_rows[b][:].rearrange("p (t c i) -> p c t i", i=4, t=4),
                 )
                 nc.vector.quantize_mx(out=x_w[b][:].bitcast(FP8X4), scales=x_s[b][:], in_=x_bf[b][:])
 
@@ -202,16 +202,21 @@ def tile_list_dental_unet_skip_kernel(
 
         for j in range(8):
             encode(j)
-            if j < 6:
+            if j < 4:
                 pick_skip(j, "enc%d" % j)
             if j >= 2:
                 squash(j - 2)
-                cast_w2(j - 2)
-        pick_skip(6, "g1_5")
+            if 3 <= j < 7:
+                cast_w2(j - 3)
+        pick_skip(4, "g1_5")
         squash(6)
-        cast_w2(6)
+        pick_skip(5, "g1_6")
+        cast_w2(4)
         squash(7)
-        pick_skip(7, "th1")
+        pick_skip(6, "x_rows1")
+        cast_w2(5)
+        pick_skip(7, "w2_bf2")
+        cast_w2(6)
         cast_w2(7)
         for j in range(8):
             decode(j)

@@ -39,13 +39,17 @@ def tile_list_dental_unet_skip_kernel(
         def col(cols, j):
             return cols[:, j // 4, j % 4 : j % 4 + 1]
 
-        tab_s = head.tile([P, T], U8, name="tab_s", align_bytes=64, offset=0)
-        nc.sync.dma_start(tab_s[0:32, :].bitcast(I32), tab_scales.rearrange("a q n -> (a q) n").bitcast(I32))
+        def load_scale_rows(tile, scales):
+            for a in range(2):
+                nc.sync.dma_start(tile[a:32:2, :].bitcast(I32), scales[a].bitcast(I32))
+            nc.vector.memset(tile[32:64, :].bitcast(I32), 0)
+            nc.vector.memset(tile[64:128, :].bitcast(I32), 0)
+
         nc.sync.dma_start(offs_sb[:], offs)
-        nc.sync.dma_start(pos1_sb[:], pos1)
-        nc.sync.dma_start(pos2_sb[:], pos2)
-        b1_cols = keep.tile([P, 2, 8], F32, name="b1_cols")
-        load_channels(nc.scalar, b1_cols, b1)
+        tab_s = keep.tile([P, T], U8, name="tab_s", align_bytes=64)
+        load_scale_rows(tab_s, tab_scales)
+        w1s_raw = keep.tile([P, H], U8, name="w1s_raw", align_bytes=64)
+        load_scale_rows(w1s_raw, w1_scales)
         skip_cols = keep.tile([P, 2, 8], F32, name="skip_cols")
         load_channels(nc.gpsimd, skip_cols, skip)
         w1w_raw = keep.tile([P, 2 * 512], I32, name="w1w_raw", align_bytes=64)
@@ -54,51 +58,36 @@ def tile_list_dental_unet_skip_kernel(
         )
         tab_w0 = keep.tile([P, T], I32, name="tab_w0", tag="stage0", align_bytes=64)
         nc.sync.dma_start(tab_w0[:], tab_words[0].rearrange("p n t -> p (n t)").bitcast(I32))
-
-        nc.vector.memset(tab_s[32:64, :].bitcast(I32), 0)
-        nc.vector.memset(tab_s[64:128, :].bitcast(I32), 0)
+        tab_w1 = head.tile([P, T], I32, name="tab_w1", align_bytes=64, offset=0)
+        nc.sync.dma_start(tab_w1[:], tab_words[1].rearrange("p n t -> p (n t)").bitcast(I32))
+        nc.sync.dma_start(pos1_sb[:], pos1)
+        nc.sync.dma_start(pos2_sb[:], pos2)
+        b1_cols = keep.tile([P, 2, 8], F32, name="b1_cols")
+        load_channels(nc.gpsimd, b1_cols, b1)
 
         zero_in = keep.tile([P, 8], F32, name="zero_in")
         zero = keep.tile([P, 8], F32, name="zero")
         nc.vector.memset(zero_in[:], 0.0)
         nc.scalar.activation(zero[:, 0:1], zero_in[:, 0:1], ACT.Tanh)
 
-        v_s = [keep.tile([P, S], U8, name="v_s%d" % a, align_bytes=64) for a in range(2)]
-        for a in range(2):
-            nc.vector.memset(v_s[a][:].bitcast(I32), 0)
-
-        w1s_raw = keep.tile([P, 2 * 256], I32, name="w1s_raw", align_bytes=64)
-        nc.vector.memset(w1s_raw[:], 0)
-        for q in range(4):
-            nc.scalar.dma_start(
-                w1s_raw[32 * q : 32 * q + 4, :].rearrange("r (a n) -> r a n", a=2),
-                w1_scales[:, 4 * q : 4 * q + 4, :].rearrange("a r n -> r a n").bitcast(I32),
-            )
+        scales = keep.tile([P, 2, S + H], U8, name="scales", align_bytes=64)
+        nc.vector.memset(scales[:].rearrange("p a n -> p (a n)").bitcast(I32), 0)
 
         picked_s = keep.tile([P, S], U8, name="picked_s", align_bytes=64)
         nc.vector.tensor_copy(picked_s[:], tab_s[:].indirect(offs_sb[:]))
-
-        def move_scales(queue, a, q):
-            row = 16 * a + 4 * q
-            queue.dma_start(v_s[a][32 * q : 32 * q + 4, :].bitcast(I32), picked_s[row : row + 4, :].bitcast(I32))
-
-        moves = [(a, q) for a in range(2) for q in range(4)]
-        for a, q in moves[:2]:
-            move_scales(nc.sync, a, q)
-        tab_w1 = head.tile([P, T], I32, name="tab_w1", align_bytes=64, offset=0)
-        nc.sync.dma_start(tab_w1[:], tab_words[1].rearrange("p n t -> p (n t)").bitcast(I32))
-        for a, q in moves[2:]:
-            move_scales(nc.scalar, a, q)
+        rows = keep.tile([P, S + H], U8, name="rows", align_bytes=64)
+        nc.vector.tensor_copy(rows[:, 0:S].bitcast(I32), picked_s[:].bitcast(I32))
+        nc.vector.tensor_copy(
+            rows[:, S : S + H].rearrange("p (c t m) -> p c t m", c=2, t=4),
+            w1s_raw[:].rearrange("p (c m t) -> p c t m", c=2, t=4),
+        )
+        for q in range(4):
+            nc.scalar.dma_start(scales[32 * q : 32 * q + 4, :, :].bitcast(I32), rows[8 * q : 8 * q + 8, :].bitcast(I32))
 
         w1w = keep.tile([P, 2 * 512], I32, name="w1w", align_bytes=64)
         nc.vector.tensor_copy(
             w1w[:].bitcast(U16).rearrange("p (c t m) -> p c t m", c=4, t=4),
             w1w_raw[:].bitcast(U16).rearrange("p (c m t) -> p c t m", c=4, t=4),
-        )
-        w1s = keep.tile([P, 2 * 256], I32, name="w1s", align_bytes=64)
-        nc.vector.tensor_copy(
-            w1s[:].bitcast(U8).rearrange("p (c t m) -> p c t m", c=4, t=4),
-            w1s_raw[:].bitcast(U8).rearrange("p (c m t) -> p c t m", c=4, t=4),
         )
 
         v_w0 = keep.tile([P, S], I32, name="v_w0", align_bytes=64)
@@ -130,14 +119,20 @@ def tile_list_dental_unet_skip_kernel(
         g1 = [keep.tile([P, M], F32, name="g1_%d" % j, tag="g1_%d" % j, align_bytes=64) for j in range(8)]
         enc = {}
         res = [keep.tile([P, M], F32, name="res%d" % j) for j in range(8)]
-        th = [keep.tile([P, M], F32, name="th%d" % j) for j in range(8)]
+        th = [keep.tile([P, 4 * M], F32, name="th%d" % b) for b in range(2)]
         x_rows = [keep.tile([P, 4 * M], BF16, name="x_rows%d" % b, tag="x_rows%d" % b, align_bytes=64) for b in range(2)]
         x_bf = [keep.tile([P, 4 * M], BF16, name="x_bf%d" % b, align_bytes=64) for b in range(2)]
         x_w = [keep.tile([P, M], U32, name="x_w%d" % b, align_bytes=64) for b in range(2)]
         x_s = [keep.tile([P, M], U8, name="x_s%d" % b, align_bytes=64) for b in range(2)]
-        w2_bf = [keep.tile([P, 4 * N], BF16, name="w2_bf%d" % c, tag="w2_bf%d" % c, align_bytes=64) for c in range(4)]
-        w2_w = [keep.tile([P, N], U32, name="w2_w%d" % c, align_bytes=64) for c in range(4)]
-        w2_s = [keep.tile([P, N], U8, name="w2_s%d" % c, align_bytes=64) for c in range(4)]
+        def w2_tiles(name, width, dtype):
+            return [
+                [keep.tile([P, width], dtype, name="%s%d_%d" % (name, pair, b), align_bytes=64) for b in range(2)]
+                for pair in range(4)
+            ]
+
+        w2_bf = w2_tiles("w2_bf", 8 * P, BF16)
+        w2_w = w2_tiles("w2_w", 2 * P, U32)
+        w2_s = w2_tiles("w2_s", 2 * P, U8)
 
         def encode(j):
             for half in range(2):
@@ -148,13 +143,16 @@ def tile_list_dental_unet_skip_kernel(
                     nc.tensor.matmul_mx(
                         out=acc[:],
                         lhsT=w1w[:, 512 * a + 64 * j : 512 * a + 64 * (j + 1)].bitcast(FP4X4),
-                        lhsT_scale=w1s[:, 256 * a + 32 * j : 256 * a + 32 * (j + 1)].bitcast(U8),
+                        lhsT_scale=scales[:, a, S + P * j : S + P * (j + 1)],
                         rhs=words.bitcast(FP8X4),
-                        rhs_scale=v_s[a][:, cols],
+                        rhs_scale=scales[:, a, cols],
                         start=(a == 0),
                         stop=(a == 1),
                     )
-                nc.scalar.activation(h[j][:, cols], acc[:], ACT.Identity, bias=col(b1_cols, j))
+                if (j, half) == (0, 1):
+                    nc.vector.tensor_scalar_add(h[j][:, cols], acc[:], col(b1_cols, j))
+                else:
+                    nc.scalar.activation(h[j][:, cols], acc[:], ACT.Identity, bias=col(b1_cols, j))
             nc.vector.tensor_copy(g1[j][:], h[j][:].indirect(pos1_sb[:]))
 
         def pick_skip(j, tag):
@@ -163,8 +161,12 @@ def tile_list_dental_unet_skip_kernel(
 
         def squash(j):
             b, t = divmod(j, 4)
-            nc.scalar.activation(th[j][:], g1[j][:], ACT.Tanh, bias=zero[:, 0:1])
-            nc.gpsimd.tensor_scalar(x_rows[b][:, t * M : (t + 1) * M], th[j][:], col(gain_cols, j), 0.0, ALU.mult, ALU.add)
+            nc.scalar.activation(th[b][:, t * M : (t + 1) * M], g1[j][:], ACT.Tanh, bias=zero[:, 0:1])
+
+        def scale_row(j):
+            b, t = divmod(j, 4)
+            cols = slice(t * M, (t + 1) * M)
+            nc.scalar.activation(x_rows[b][:, cols], th[b][:, cols], ACT.Copy, scale=col(gain_cols, j))
             if t == 3:
                 nc.vector.tensor_copy(
                     x_bf[b][:].rearrange("p (c i t) -> p c t i", i=4, t=4),
@@ -172,26 +174,23 @@ def tile_list_dental_unet_skip_kernel(
                 )
                 nc.vector.quantize_mx(out=x_w[b][:].bitcast(FP8X4), scales=x_s[b][:], in_=x_bf[b][:])
 
-        def cast_w2(piece):
-            c, half = divmod(piece, 2)
-            b, nb = divmod(c, 2)
-            ms = slice(64 * half, 64 * (half + 1))
-            src = w2_raw[b][:].rearrange("p (r nb m t) -> p nb m r t", r=4, nb=2, t=4)[:, nb, ms]
-            nc.scalar.copy(w2_bf[c][:].rearrange("p (t m r) -> p m r t", t=4, r=4)[:, ms], src)
-            if half == 1:
-                nc.vector.quantize_mx(out=w2_w[c][:].bitcast(FP8X4), scales=w2_s[c][:], in_=w2_bf[c][:])
+        def cast_w2(pair, b):
+            nb, u = divmod(pair, 2)
+            src = w2_raw[b][:].rearrange("p (r nb m u e) -> p nb u m r e", r=4, nb=2, u=2, e=2)[:, nb, u]
+            nc.scalar.copy(w2_bf[pair][b][:].rearrange("p (e m r) -> p m r e", e=2, r=4), src)
+            nc.vector.quantize_mx(out=w2_w[pair][b][:].bitcast(FP8X4), scales=w2_s[pair][b][:], in_=w2_bf[pair][b][:])
 
         out_rows = out.rearrange("(b p t) m -> b t p m", b=2, t=4)
 
         def decode(j):
             nb, t = divmod(j, 4)
+            pair, e = divmod(j, 2)
             acc = psum.tile([P, N], F32, name="acc", tag="dec_bank" if j < 4 else "enc_bank")
             for b in range(2):
-                c = 2 * b + nb
                 nc.tensor.matmul_mx(
                     out=acc[:],
-                    lhsT=w2_w[c][:, t * P : (t + 1) * P].bitcast(FP8X4),
-                    lhsT_scale=w2_s[c][:, t * P : (t + 1) * P],
+                    lhsT=w2_w[pair][b][:, e * P : (e + 1) * P].bitcast(FP8X4),
+                    lhsT_scale=w2_s[pair][b][:, e * P : (e + 1) * P],
                     rhs=x_w[b][:].bitcast(FP8X4),
                     rhs_scale=x_s[b][:],
                     start=(b == 0),
@@ -202,21 +201,25 @@ def tile_list_dental_unet_skip_kernel(
 
         for j in range(8):
             encode(j)
-            if j < 4:
+            if j < 6:
                 pick_skip(j, "enc%d" % j)
             if j >= 2:
                 squash(j - 2)
-            if 3 <= j < 7:
-                cast_w2(j - 3)
-        pick_skip(4, "g1_5")
+            if j >= 3:
+                scale_row(j - 3)
+        pick_skip(6, "g1_5")
+        cast_w2(0, 0)
         squash(6)
-        pick_skip(5, "g1_6")
-        cast_w2(4)
+        scale_row(5)
+        scale_row(6)
+        cast_w2(0, 1)
         squash(7)
-        pick_skip(6, "x_rows1")
-        cast_w2(5)
-        pick_skip(7, "w2_bf2")
-        cast_w2(6)
-        cast_w2(7)
+        cast_w2(1, 0)
+        scale_row(7)
+        pick_skip(7, "x_rows1")
+        cast_w2(1, 1)
+        for pair in range(2, 4):
+            for b in range(2):
+                cast_w2(pair, b)
         for j in range(8):
             decode(j)

@@ -45,25 +45,38 @@ def tile_list_dental_unet_skip_kernel(
             nc.vector.memset(tile[32:64, :].bitcast(I32), 0)
             nc.vector.memset(tile[64:128, :].bitcast(I32), 0)
 
+        w1w_raw = [keep.tile([P, 2, 256], I32, name="w1w_raw%d" % b, align_bytes=64) for b in range(2)]
+        w1w = {}
+
+        def load_w1_words(b):
+            words = w1_words.rearrange("a p n -> p a n").bitcast(I32)
+            nc.sync.dma_start(w1w_raw[b][:], words[:, :, 256 * b : 256 * (b + 1)])
+
+        def order_w1_words(tile, b, t0, t1):
+            nc.vector.tensor_copy(
+                tile[:].bitcast(U16).rearrange("p a (t m) -> p a t m", m=P),
+                w1w_raw[b][:].bitcast(U16).rearrange("p a (m t) -> p a t m", t=4)[:, :, t0:t1],
+            )
+            for t in range(t0, t1):
+                w1w[4 * b + t] = [tile[:, a, 64 * (t - t0) : 64 * (t - t0 + 1)] for a in range(2)]
+
+        load_w1_words(0)
         nc.sync.dma_start(offs_sb[:], offs)
         tab_s = keep.tile([P, T], U8, name="tab_s", align_bytes=64)
         load_scale_rows(tab_s, tab_scales)
         w1s_raw = keep.tile([P, H], U8, name="w1s_raw", align_bytes=64)
         load_scale_rows(w1s_raw, w1_scales)
-        skip_cols = keep.tile([P, 2, 8], F32, name="skip_cols")
-        load_channels(nc.gpsimd, skip_cols, skip)
-        w1w_raw = keep.tile([P, 2 * 512], I32, name="w1w_raw", align_bytes=64)
-        nc.sync.dma_start(
-            w1w_raw[:].rearrange("p (a n) -> p a n", a=2), w1_words.rearrange("a p n -> p a n").bitcast(I32)
-        )
         tab_w0 = keep.tile([P, T], I32, name="tab_w0", tag="stage0", align_bytes=64)
         nc.sync.dma_start(tab_w0[:], tab_words[0].rearrange("p n t -> p (n t)").bitcast(I32))
+        skip_cols = keep.tile([P, 2, 8], F32, name="skip_cols")
+        load_channels(nc.sync, skip_cols, skip)
+        b1_cols = keep.tile([P, 2, 8], F32, name="b1_cols")
+        load_channels(nc.sync, b1_cols, b1)
         tab_w1 = head.tile([P, T], I32, name="tab_w1", align_bytes=64, offset=0)
         nc.sync.dma_start(tab_w1[:], tab_words[1].rearrange("p n t -> p (n t)").bitcast(I32))
+        load_w1_words(1)
         nc.sync.dma_start(pos1_sb[:], pos1)
         nc.sync.dma_start(pos2_sb[:], pos2)
-        b1_cols = keep.tile([P, 2, 8], F32, name="b1_cols")
-        load_channels(nc.gpsimd, b1_cols, b1)
 
         zero_in = keep.tile([P, 8], F32, name="zero_in")
         zero = keep.tile([P, 8], F32, name="zero")
@@ -84,11 +97,7 @@ def tile_list_dental_unet_skip_kernel(
         for q in range(4):
             nc.scalar.dma_start(scales[32 * q : 32 * q + 4, :, :].bitcast(I32), rows[8 * q : 8 * q + 8, :].bitcast(I32))
 
-        w1w = keep.tile([P, 2 * 512], I32, name="w1w", align_bytes=64)
-        nc.vector.tensor_copy(
-            w1w[:].bitcast(U16).rearrange("p (c t m) -> p c t m", c=4, t=4),
-            w1w_raw[:].bitcast(U16).rearrange("p (c m t) -> p c t m", c=4, t=4),
-        )
+        order_w1_words(keep.tile([P, 2, 64], I32, name="w1w_first", align_bytes=64), 0, 0, 1)
 
         v_w0 = keep.tile([P, S], I32, name="v_w0", align_bytes=64)
         nc.vector.tensor_copy(v_w0[:].bitcast(U32), tab_w0[:].bitcast(U32).indirect(offs_sb[:]))
@@ -99,13 +108,16 @@ def tile_list_dental_unet_skip_kernel(
                 tab_w1[:].bitcast(U32).indirect(offs_sb[:, 32 * half : 32 * half + 32]),
             )
 
+        order_w1_words(head.tile([P, 2, 192], I32, name="w1w_next", align_bytes=64, offset=256), 0, 1, 4)
+        order_w1_words(keep.tile([P, 2, 256], I32, name="w1w_last", align_bytes=64), 1, 0, 4)
+
         skip_wide = [keep.tile([P, M], F32, name="skip_wide%d" % j) for j in range(8)]
         for j in range(8):
             nc.scalar.activation(skip_wide[j][:], col(skip_cols, j).to_broadcast([P, M]), ACT.Copy)
 
         w2_raw = [
             keep.tile([P, 4 * H], F32, name="w2_raw0", tag="stage0", align_bytes=64),
-            head.tile([P, 4 * H], F32, name="w2_raw1", align_bytes=64, offset=256),
+            head.tile([P, 4 * H], F32, name="w2_raw1", align_bytes=64, offset=1792),
         ]
         w2_rows = w2.rearrange("(b p r) n -> b p (r n)", b=2, r=4)
         nc.sync.dma_start(w2_raw[0][:], w2_rows[0])
@@ -142,17 +154,14 @@ def tile_list_dental_unet_skip_kernel(
                     words = v_w0[:, cols] if a == 0 else v_w1[half][:]
                     nc.tensor.matmul_mx(
                         out=acc[:],
-                        lhsT=w1w[:, 512 * a + 64 * j : 512 * a + 64 * (j + 1)].bitcast(FP4X4),
+                        lhsT=w1w[j][a].bitcast(FP4X4),
                         lhsT_scale=scales[:, a, S + P * j : S + P * (j + 1)],
                         rhs=words.bitcast(FP8X4),
                         rhs_scale=scales[:, a, cols],
                         start=(a == 0),
                         stop=(a == 1),
                     )
-                if (j, half) == (0, 1):
-                    nc.vector.tensor_scalar_add(h[j][:, cols], acc[:], col(b1_cols, j))
-                else:
-                    nc.scalar.activation(h[j][:, cols], acc[:], ACT.Identity, bias=col(b1_cols, j))
+                nc.scalar.activation(h[j][:, cols], acc[:], ACT.Identity, bias=col(b1_cols, j))
             nc.vector.tensor_copy(g1[j][:], h[j][:].indirect(pos1_sb[:]))
 
         def pick_skip(j, tag):
@@ -196,8 +205,11 @@ def tile_list_dental_unet_skip_kernel(
                     start=(b == 0),
                     stop=(b == 1),
                 )
-            nc.vector.scalar_tensor_tensor(res[j][:], acc[:], col(b2_cols, j), enc[j][:], ALU.add, ALU.max)
-            nc.sync.dma_start(out_rows[nb, t], res[j][:])
+            width = M // 2 if j == 7 else M
+            for m0 in range(0, M, width):
+                ms = slice(m0, m0 + width)
+                nc.vector.scalar_tensor_tensor(res[j][:, ms], acc[:, ms], col(b2_cols, j), enc[j][:, ms], ALU.add, ALU.max)
+                nc.sync.dma_start(out_rows[nb, t][:, ms], res[j][:, ms])
 
         for j in range(8):
             encode(j)

@@ -40,15 +40,15 @@ def tile_list_dental_unet_skip_kernel(
             return cols[:, j // 4, j % 4 : j % 4 + 1]
 
         def load_scale_rows(tile, scales):
-            for a in range(2):
-                nc.sync.dma_start(tile[a:32:2, :].bitcast(I32), scales[a].bitcast(I32))
+            nc.sync.dma_start(tile[0:32, :].bitcast(I32), scales.rearrange("a q n -> q a n").bitcast(I32))
             nc.vector.memset(tile[32:64, :].bitcast(I32), 0)
             nc.vector.memset(tile[64:128, :].bitcast(I32), 0)
 
-        w1w_raw = [keep.tile([P, 2, 256], I32, name="w1w_raw%d" % b, align_bytes=64) for b in range(2)]
+        w1w_raw = {}
         w1w = {}
 
-        def load_w1_words(b):
+        def load_w1_words(b, tag):
+            w1w_raw[b] = keep.tile([P, 2, 256], I32, name="w1w_raw%d" % b, tag=tag, align_bytes=64)
             words = w1_words.rearrange("a p n -> p a n").bitcast(I32)
             nc.sync.dma_start(w1w_raw[b][:], words[:, :, 256 * b : 256 * (b + 1)])
 
@@ -60,22 +60,21 @@ def tile_list_dental_unet_skip_kernel(
             for t in range(t0, t1):
                 w1w[4 * b + t] = [tile[:, a, 64 * (t - t0) : 64 * (t - t0 + 1)] for a in range(2)]
 
-        load_w1_words(0)
+        load_w1_words(0, "w1w_raw0")
         nc.sync.dma_start(offs_sb[:], offs)
         tab_s = keep.tile([P, T], U8, name="tab_s", align_bytes=64)
         load_scale_rows(tab_s, tab_scales)
-        w1s_raw = keep.tile([P, H], U8, name="w1s_raw", align_bytes=64)
+        w1s_raw = keep.tile([P, H], U8, name="w1s_raw", tag="w1s_raw", align_bytes=64)
         load_scale_rows(w1s_raw, w1_scales)
         tab_w0 = keep.tile([P, T], I32, name="tab_w0", tag="stage0", align_bytes=64)
         nc.sync.dma_start(tab_w0[:], tab_words[0].rearrange("p n t -> p (n t)").bitcast(I32))
         skip_cols = keep.tile([P, 2, 8], F32, name="skip_cols")
         load_channels(nc.sync, skip_cols, skip)
-        b1_cols = keep.tile([P, 2, 8], F32, name="b1_cols")
-        load_channels(nc.sync, b1_cols, b1)
+        nc.sync.dma_start(pos1_sb[:], pos1)
         tab_w1 = head.tile([P, T], I32, name="tab_w1", align_bytes=64, offset=0)
         nc.sync.dma_start(tab_w1[:], tab_words[1].rearrange("p n t -> p (n t)").bitcast(I32))
-        load_w1_words(1)
-        nc.sync.dma_start(pos1_sb[:], pos1)
+        b1_cols = keep.tile([P, 2, 8], F32, name="b1_cols")
+        load_channels(nc.sync, b1_cols, b1)
         nc.sync.dma_start(pos2_sb[:], pos2)
 
         zero_in = keep.tile([P, 8], F32, name="zero_in")
@@ -83,8 +82,10 @@ def tile_list_dental_unet_skip_kernel(
         nc.vector.memset(zero_in[:], 0.0)
         nc.scalar.activation(zero[:, 0:1], zero_in[:, 0:1], ACT.Tanh)
 
-        scales = keep.tile([P, 2, S + H], U8, name="scales", align_bytes=64)
-        nc.vector.memset(scales[:].rearrange("p a n -> p (a n)").bitcast(I32), 0)
+        scales = keep.tile([P, 2, S + N], U8, name="scales", align_bytes=64)
+        scales_late = keep.tile([P, 2, N], U8, name="scales_late", align_bytes=64)
+        for tile in (scales, scales_late):
+            nc.vector.memset(tile[:].rearrange("p a n -> p (a n)").bitcast(I32), 0)
 
         picked_s = keep.tile([P, S], U8, name="picked_s", align_bytes=64)
         nc.vector.tensor_copy(picked_s[:], tab_s[:].indirect(offs_sb[:]))
@@ -94,8 +95,14 @@ def tile_list_dental_unet_skip_kernel(
             rows[:, S : S + H].rearrange("p (c t m) -> p c t m", c=2, t=4),
             w1s_raw[:].rearrange("p (c m t) -> p c t m", c=2, t=4),
         )
-        for q in range(4):
-            nc.scalar.dma_start(scales[32 * q : 32 * q + 4, :, :].bitcast(I32), rows[8 * q : 8 * q + 8, :].bitcast(I32))
+
+        def move_rows(tile, cols):
+            for q in (0, 2, 1, 3):
+                nc.sync.dma_start(tile[32 * q : 32 * q + 4, :, :].bitcast(I32), rows[8 * q : 8 * q + 8, cols].bitcast(I32))
+
+        move_rows(scales, slice(0, S + N))
+        load_w1_words(1, "w1s_raw")
+        move_rows(scales_late, slice(S + N, S + H))
 
         order_w1_words(keep.tile([P, 2, 64], I32, name="w1w_first", align_bytes=64), 0, 0, 1)
 
@@ -155,7 +162,7 @@ def tile_list_dental_unet_skip_kernel(
                     nc.tensor.matmul_mx(
                         out=acc[:],
                         lhsT=w1w[j][a].bitcast(FP4X4),
-                        lhsT_scale=scales[:, a, S + P * j : S + P * (j + 1)],
+                        lhsT_scale=scales[:, a, S + P * j : S + P * (j + 1)] if j < 4 else scales_late[:, a, P * (j - 4) : P * (j - 3)],
                         rhs=words.bitcast(FP8X4),
                         rhs_scale=scales[:, a, cols],
                         start=(a == 0),

@@ -104,7 +104,8 @@ def tile_list_dental_unet_skip_kernel(
         load_w1_words(1, "w1s_raw")
         move_rows(scales_late, slice(S + N, S + H))
 
-        order_w1_words(keep.tile([P, 2, 64], I32, name="w1w_first", align_bytes=64), 0, 0, 1)
+        order_w1_words(keep.tile([P, 2, 64], I32, name="w1w_tile0", align_bytes=64), 0, 0, 1)
+        order_w1_words(keep.tile([P, 2, 128], I32, name="w1w_tiles23", align_bytes=64), 0, 2, 4)
 
         v_w0 = keep.tile([P, S], I32, name="v_w0", align_bytes=64)
         nc.vector.tensor_copy(v_w0[:].bitcast(U32), tab_w0[:].bitcast(U32).indirect(offs_sb[:]))
@@ -115,7 +116,7 @@ def tile_list_dental_unet_skip_kernel(
                 tab_w1[:].bitcast(U32).indirect(offs_sb[:, 32 * half : 32 * half + 32]),
             )
 
-        order_w1_words(head.tile([P, 2, 192], I32, name="w1w_next", align_bytes=64, offset=256), 0, 1, 4)
+        order_w1_words(head.tile([P, 2, 64], I32, name="w1w_tile1", align_bytes=64, offset=256), 0, 1, 2)
         order_w1_words(keep.tile([P, 2, 256], I32, name="w1w_last", align_bytes=64), 1, 0, 4)
 
         skip_wide = [keep.tile([P, M], F32, name="skip_wide%d" % j) for j in range(8)]
@@ -124,7 +125,7 @@ def tile_list_dental_unet_skip_kernel(
 
         w2_raw = [
             keep.tile([P, 4 * H], F32, name="w2_raw0", tag="stage0", align_bytes=64),
-            head.tile([P, 4 * H], F32, name="w2_raw1", align_bytes=64, offset=1792),
+            head.tile([P, 4 * H], F32, name="w2_raw1", align_bytes=64, offset=768),
         ]
         w2_rows = w2.rearrange("(b p r) n -> b p (r n)", b=2, r=4)
         nc.sync.dma_start(w2_raw[0][:], w2_rows[0])
@@ -150,7 +151,7 @@ def tile_list_dental_unet_skip_kernel(
             ]
 
         w2_bf = w2_tiles("w2_bf", 8 * P, BF16)
-        w2_w = w2_tiles("w2_w", 2 * P, U32)
+        w2_w = {}
         w2_s = w2_tiles("w2_s", 2 * P, U8)
 
         def encode(j):
@@ -194,7 +195,14 @@ def tile_list_dental_unet_skip_kernel(
             nb, u = divmod(pair, 2)
             src = w2_raw[b][:].rearrange("p (r nb m u e) -> p nb u m r e", r=4, nb=2, u=2, e=2)[:, nb, u]
             nc.scalar.copy(w2_bf[pair][b][:].rearrange("p (e m r) -> p m r e", e=2, r=4), src)
-            nc.vector.quantize_mx(out=w2_w[pair][b][:].bitcast(FP8X4), scales=w2_s[pair][b][:], in_=w2_bf[pair][b][:])
+
+        def quantize_w2(pair, b, tag):
+            w2_w[pair, b] = keep.tile([P, 2 * P], U32, name="w2_w%d_%d" % (pair, b), tag=tag, align_bytes=64)
+            nc.vector.quantize_mx(out=w2_w[pair, b][:].bitcast(FP8X4), scales=w2_s[pair][b][:], in_=w2_bf[pair][b][:])
+
+        def make_w2(pair, b):
+            cast_w2(pair, b)
+            quantize_w2(pair, b, "w2_w%d_%d" % (pair, b))
 
         out_rows = out.rearrange("(b p t) m -> b t p m", b=2, t=4)
 
@@ -205,7 +213,7 @@ def tile_list_dental_unet_skip_kernel(
             for b in range(2):
                 nc.tensor.matmul_mx(
                     out=acc[:],
-                    lhsT=w2_w[pair][b][:, e * P : (e + 1) * P].bitcast(FP8X4),
+                    lhsT=w2_w[pair, b][:, e * P : (e + 1) * P].bitcast(FP8X4),
                     lhsT_scale=w2_s[pair][b][:, e * P : (e + 1) * P],
                     rhs=x_w[b][:].bitcast(FP8X4),
                     rhs_scale=x_s[b][:],
@@ -227,18 +235,19 @@ def tile_list_dental_unet_skip_kernel(
             if j >= 3:
                 scale_row(j - 3)
         pick_skip(6, "g1_5")
-        cast_w2(0, 0)
+        make_w2(0, 0)
         squash(6)
         scale_row(5)
-        scale_row(6)
-        cast_w2(0, 1)
+        make_w2(0, 1)
         squash(7)
-        cast_w2(1, 0)
+        scale_row(6)
         scale_row(7)
         pick_skip(7, "x_rows1")
-        cast_w2(1, 1)
-        for pair in range(2, 4):
-            for b in range(2):
-                cast_w2(pair, b)
+        make_w2(1, 0)
+        make_w2(1, 1)
+        make_w2(2, 0)
+        make_w2(2, 1)
+        make_w2(3, 0)
+        make_w2(3, 1)
         for j in range(8):
             decode(j)

@@ -27,6 +27,7 @@ def tile_list_dental_unet_skip_kernel(
     with ExitStack() as ctx:
         keep = ctx.enter_context(tc.tile_pool(name="keep", bufs=1))
         head = ctx.enter_context(tc.tile_pool(name="head", bufs=1))
+        late = ctx.enter_context(tc.tile_pool(name="late", bufs=1))
         psum = ctx.enter_context(tc.psum_pool(name="psum", bufs=4))
 
         offs_sb = keep.tile([P, S // 16], U16, name="offs_sb")
@@ -68,8 +69,6 @@ def tile_list_dental_unet_skip_kernel(
         load_scale_rows(w1s_raw, w1_scales)
         tab_w0 = keep.tile([P, T], I32, name="tab_w0", tag="stage0", align_bytes=64)
         nc.sync.dma_start(tab_w0[:], tab_words[0].rearrange("p n t -> p (n t)").bitcast(I32))
-        skip_cols = keep.tile([P, 2, 8], F32, name="skip_cols")
-        load_channels(nc.sync, skip_cols, skip)
         nc.sync.dma_start(pos1_sb[:], pos1)
         tab_w1 = head.tile([P, T], I32, name="tab_w1", align_bytes=64, offset=0)
         nc.sync.dma_start(tab_w1[:], tab_words[1].rearrange("p n t -> p (n t)").bitcast(I32))
@@ -119,10 +118,6 @@ def tile_list_dental_unet_skip_kernel(
         order_w1_words(head.tile([P, 2, 64], I32, name="w1w_tile1", align_bytes=64, offset=256), 0, 1, 2)
         order_w1_words(keep.tile([P, 2, 256], I32, name="w1w_last", align_bytes=64), 1, 0, 4)
 
-        skip_wide = [keep.tile([P, M], F32, name="skip_wide%d" % j) for j in range(8)]
-        for j in range(8):
-            nc.scalar.activation(skip_wide[j][:], col(skip_cols, j).to_broadcast([P, M]), ACT.Copy)
-
         w2_raw = [
             keep.tile([P, 4 * H], F32, name="w2_raw0", tag="stage0", align_bytes=64),
             head.tile([P, 4 * H], F32, name="w2_raw1", align_bytes=64, offset=768),
@@ -132,6 +127,8 @@ def tile_list_dental_unet_skip_kernel(
         gain_cols = head.tile([P, 2, 8], F32, name="gain_cols", align_bytes=64, offset=0)
         b2_cols = head.tile([P, 2, 8], F32, name="b2_cols", align_bytes=64, offset=128)
         load_channels(nc.sync, gain_cols, gain)
+        skip_cols = head.tile([P, 2, 8], F32, name="skip_cols", align_bytes=64, offset=64)
+        load_channels(nc.sync, skip_cols, skip)
         load_channels(nc.sync, b2_cols, b2)
         nc.sync.dma_start(w2_raw[1][:], w2_rows[1])
 
@@ -139,8 +136,9 @@ def tile_list_dental_unet_skip_kernel(
         g1 = [keep.tile([P, M], F32, name="g1_%d" % j, tag="g1_%d" % j, align_bytes=64) for j in range(8)]
         enc = {}
         res = [keep.tile([P, M], F32, name="res%d" % j) for j in range(8)]
-        th = [keep.tile([P, 4 * M], F32, name="th%d" % b) for b in range(2)]
+        th = [keep.tile([P, 4 * M], F32, name="th0"), late.tile([P, 4 * M], F32, name="th1", align_bytes=64, offset=0)]
         x_rows = [keep.tile([P, 4 * M], BF16, name="x_rows%d" % b, tag="x_rows%d" % b, align_bytes=64) for b in range(2)]
+        g2 = {}
         x_bf = [keep.tile([P, 4 * M], BF16, name="x_bf%d" % b, align_bytes=64) for b in range(2)]
         x_w = [keep.tile([P, M], U32, name="x_w%d" % b, align_bytes=64) for b in range(2)]
         x_s = [keep.tile([P, M], U8, name="x_s%d" % b, align_bytes=64) for b in range(2)]
@@ -173,8 +171,15 @@ def tile_list_dental_unet_skip_kernel(
             nc.vector.tensor_copy(g1[j][:], h[j][:].indirect(pos1_sb[:]))
 
         def pick_skip(j, tag):
-            enc[j] = keep.tile([P, M], F32, name="enc%d" % j, tag=tag, align_bytes=64)
-            nc.vector.tensor_tensor(enc[j][:], h[j][:].indirect(pos2_sb[:]), skip_wide[j][:], ALU.mult)
+            g2[j] = keep.tile([P, M], F32, name="g2_%d" % j, tag=tag, align_bytes=64)
+            nc.vector.tensor_copy(g2[j][:], h[j][:].indirect(pos2_sb[:]))
+
+        def scale_skip(j):
+            if j < 4:
+                enc[j] = keep.tile([P, M], F32, name="enc%d" % j, align_bytes=64)
+            else:
+                enc[j] = late.tile([P, M], F32, name="enc%d" % j, align_bytes=64, offset=4 * M * (j - 4))
+            nc.gpsimd.tensor_scalar(enc[j][:], g2[j][:], col(skip_cols, j), 0.0, ALU.mult, ALU.add)
 
         def squash(j):
             b, t = divmod(j, 4)
@@ -183,11 +188,15 @@ def tile_list_dental_unet_skip_kernel(
         def scale_row(j):
             b, t = divmod(j, 4)
             cols = slice(t * M, (t + 1) * M)
-            nc.scalar.activation(x_rows[b][:, cols], th[b][:, cols], ACT.Copy, scale=col(gain_cols, j))
+            nc.gpsimd.tensor_scalar(x_rows[b][:, cols], th[b][:, cols], col(gain_cols, j), 0.0, ALU.mult, ALU.add)
             if t == 3:
-                nc.vector.tensor_copy(
-                    x_bf[b][:].rearrange("p (c i t) -> p c t i", i=4, t=4),
-                    x_rows[b][:].rearrange("p (t c i) -> p c t i", i=4, t=4),
+                nc.gpsimd.tensor_scalar(
+                    x_bf[b][:].rearrange("p (m t) -> p m t", t=4),
+                    x_rows[b][:].rearrange("p (t m) -> p m t", t=4),
+                    1.0,
+                    0.0,
+                    ALU.mult,
+                    ALU.add,
                 )
                 nc.vector.quantize_mx(out=x_w[b][:].bitcast(FP8X4), scales=x_s[b][:], in_=x_bf[b][:])
 
@@ -228,26 +237,23 @@ def tile_list_dental_unet_skip_kernel(
 
         for j in range(8):
             encode(j)
-            if j < 6:
-                pick_skip(j, "enc%d" % j)
-            if j >= 2:
+            if j % 2 == 0:
+                pick_skip(j // 2, "g2_%d" % (j // 2))
+            if 2 <= j < 7:
                 squash(j - 2)
-            if j >= 3:
-                scale_row(j - 3)
-        pick_skip(6, "g1_5")
-        make_w2(0, 0)
-        squash(6)
-        scale_row(5)
-        make_w2(0, 1)
-        squash(7)
-        scale_row(6)
-        scale_row(7)
-        pick_skip(7, "x_rows1")
-        make_w2(1, 0)
-        make_w2(1, 1)
-        make_w2(2, 0)
-        make_w2(2, 1)
-        make_w2(3, 0)
-        make_w2(3, 1)
+                scale_row(j - 2)
+            if j % 2 == 1:
+                scale_skip(j // 2)
+        for j in range(5, 8):
+            squash(j)
+            scale_row(j)
+        pick_skip(7, "g2_7")
+        for j in range(4, 7):
+            pick_skip(j, "g1_%d" % (j + 1))
+        for j in range(4, 8):
+            scale_skip(j)
+        for pair in range(4):
+            for b in range(2):
+                make_w2(pair, b)
         for j in range(8):
             decode(j)

@@ -28,6 +28,7 @@ def tile_list_dental_unet_skip_kernel(
         keep = ctx.enter_context(tc.tile_pool(name="keep", bufs=1))
         head = ctx.enter_context(tc.tile_pool(name="head", bufs=1))
         late = ctx.enter_context(tc.tile_pool(name="late", bufs=1))
+        held = ctx.enter_context(tc.tile_pool(name="held", bufs=1))
         psum = ctx.enter_context(tc.psum_pool(name="psum", bufs=4))
 
         offs_sb = keep.tile([P, S // 16], U16, name="offs_sb")
@@ -133,15 +134,16 @@ def tile_list_dental_unet_skip_kernel(
         nc.sync.dma_start(w2_raw[1][:], w2_rows[1])
 
         h = [keep.tile([P, S], F32, name="h%d" % j) for j in range(8)]
-        g1 = [keep.tile([P, M], F32, name="g1_%d" % j, tag="g1_%d" % j, align_bytes=64) for j in range(8)]
+        g1 = [keep.tile([P, M], F32, name="g1_%d" % j, align_bytes=64) for j in range(5)]
+        g1 = g1 + [held.tile([P, M], F32, name="g1_%d" % j, align_bytes=64, offset=2 * M + 8 * M * (j - 5)) for j in range(5, 8)]
         enc = {}
         res = [keep.tile([P, M], F32, name="res%d" % j) for j in range(8)]
-        th = [keep.tile([P, 4 * M], F32, name="th0"), late.tile([P, 4 * M], F32, name="th1", align_bytes=64, offset=0)]
-        x_rows = [keep.tile([P, 4 * M], BF16, name="x_rows%d" % b, tag="x_rows%d" % b, align_bytes=64) for b in range(2)]
+        th = [keep.tile([P, 4 * M], F32, name="th%d" % b) for b in range(2)]
+        x_rows = [keep.tile([P, 4 * M], BF16, name="x_rows0"), late.tile([P, 4 * M], BF16, name="x_rows1", align_bytes=64, offset=0)]
         g2 = {}
         x_bf = [keep.tile([P, 4 * M], BF16, name="x_bf%d" % b, align_bytes=64) for b in range(2)]
         x_w = [keep.tile([P, M], U32, name="x_w%d" % b, align_bytes=64) for b in range(2)]
-        x_s = [keep.tile([P, M], U8, name="x_s%d" % b, align_bytes=64) for b in range(2)]
+        x_s = {}
         def w2_tiles(name, width, dtype):
             return [
                 [keep.tile([P, width], dtype, name="%s%d_%d" % (name, pair, b), align_bytes=64) for b in range(2)]
@@ -150,7 +152,7 @@ def tile_list_dental_unet_skip_kernel(
 
         w2_bf = w2_tiles("w2_bf", 8 * P, BF16)
         w2_w = {}
-        w2_s = w2_tiles("w2_s", 2 * P, U8)
+        w2_s = {}
 
         def encode(j):
             for half in range(2):
@@ -170,16 +172,19 @@ def tile_list_dental_unet_skip_kernel(
                 nc.scalar.activation(h[j][:, cols], acc[:], ACT.Identity, bias=col(b1_cols, j))
             nc.vector.tensor_copy(g1[j][:], h[j][:].indirect(pos1_sb[:]))
 
-        def pick_skip(j, tag):
-            g2[j] = keep.tile([P, M], F32, name="g2_%d" % j, tag=tag, align_bytes=64)
+        def pick_skip(j):
+            if 2 <= j < 7:
+                g2[j] = held.tile([P, M], F32, name="g2_%d" % j, align_bytes=64, offset=4 * M * (j - 2))
+            else:
+                g2[j] = keep.tile([P, M], F32, name="g2_%d" % j, align_bytes=64)
             nc.vector.tensor_copy(g2[j][:], h[j][:].indirect(pos2_sb[:]))
 
         def scale_skip(j):
-            if j < 4:
-                enc[j] = keep.tile([P, M], F32, name="enc%d" % j, align_bytes=64)
+            enc[j] = keep.tile([P, M], F32, name="enc%d" % j, align_bytes=64)
+            if j < 2:
+                nc.gpsimd.tensor_scalar(enc[j][:], g2[j][:], col(skip_cols, j), 0.0, ALU.mult, ALU.add)
             else:
-                enc[j] = late.tile([P, M], F32, name="enc%d" % j, align_bytes=64, offset=4 * M * (j - 4))
-            nc.gpsimd.tensor_scalar(enc[j][:], g2[j][:], col(skip_cols, j), 0.0, ALU.mult, ALU.add)
+                nc.scalar.activation(enc[j][:], g2[j][:], ACT.Copy, scale=col(skip_cols, j))
 
         def squash(j):
             b, t = divmod(j, 4)
@@ -198,7 +203,10 @@ def tile_list_dental_unet_skip_kernel(
                     ALU.mult,
                     ALU.add,
                 )
-                nc.vector.quantize_mx(out=x_w[b][:].bitcast(FP8X4), scales=x_s[b][:], in_=x_bf[b][:])
+
+        def quantize_x(b):
+            x_s[b] = late.tile([P, M], U8, name="x_s%d" % b, align_bytes=64, offset=M * b)
+            nc.vector.quantize_mx(out=x_w[b][:].bitcast(FP8X4), scales=x_s[b][:], in_=x_bf[b][:])
 
         def cast_w2(pair, b):
             nb, u = divmod(pair, 2)
@@ -207,7 +215,8 @@ def tile_list_dental_unet_skip_kernel(
 
         def quantize_w2(pair, b, tag):
             w2_w[pair, b] = keep.tile([P, 2 * P], U32, name="w2_w%d_%d" % (pair, b), tag=tag, align_bytes=64)
-            nc.vector.quantize_mx(out=w2_w[pair, b][:].bitcast(FP8X4), scales=w2_s[pair][b][:], in_=w2_bf[pair][b][:])
+            w2_s[pair, b] = late.tile([P, 2 * P], U8, name="w2_s%d_%d" % (pair, b), align_bytes=64, offset=2 * M + 2 * P * (2 * pair + b))
+            nc.vector.quantize_mx(out=w2_w[pair, b][:].bitcast(FP8X4), scales=w2_s[pair, b][:], in_=w2_bf[pair][b][:])
 
         def make_w2(pair, b):
             cast_w2(pair, b)
@@ -223,7 +232,7 @@ def tile_list_dental_unet_skip_kernel(
                 nc.tensor.matmul_mx(
                     out=acc[:],
                     lhsT=w2_w[pair, b][:, e * P : (e + 1) * P].bitcast(FP8X4),
-                    lhsT_scale=w2_s[pair][b][:, e * P : (e + 1) * P],
+                    lhsT_scale=w2_s[pair, b][:, e * P : (e + 1) * P],
                     rhs=x_w[b][:].bitcast(FP8X4),
                     rhs_scale=x_s[b][:],
                     start=(b == 0),
@@ -237,23 +246,26 @@ def tile_list_dental_unet_skip_kernel(
 
         for j in range(8):
             encode(j)
-            if j % 2 == 0:
-                pick_skip(j // 2, "g2_%d" % (j // 2))
+            if j < 2:
+                pick_skip(j)
             if 2 <= j < 7:
                 squash(j - 2)
                 scale_row(j - 2)
-            if j % 2 == 1:
-                scale_skip(j // 2)
+            if j in (2, 3):
+                scale_skip(j - 2)
         for j in range(5, 8):
             squash(j)
             scale_row(j)
-        pick_skip(7, "g2_7")
-        for j in range(4, 7):
-            pick_skip(j, "g1_%d" % (j + 1))
-        for j in range(4, 8):
-            scale_skip(j)
+        pick_skip(7)
+        for j in range(2, 7):
+            pick_skip(j)
         for pair in range(4):
             for b in range(2):
                 make_w2(pair, b)
+                if pair == 0:
+                    quantize_x(b)
+            if pair > 0:
+                scale_skip(2 * pair)
+                scale_skip(2 * pair + 1)
         for j in range(8):
             decode(j)

@@ -29,7 +29,9 @@ def tile_list_dental_unet_skip_kernel(
         head = ctx.enter_context(tc.tile_pool(name="head", bufs=1))
         late = ctx.enter_context(tc.tile_pool(name="late", bufs=1))
         held = ctx.enter_context(tc.tile_pool(name="held", bufs=1))
-        psum = ctx.enter_context(tc.psum_pool(name="psum", bufs=4))
+        last = ctx.enter_context(tc.tile_pool(name="last", bufs=1))
+        after = ctx.enter_context(tc.tile_pool(name="after", bufs=1))
+        psum = ctx.enter_context(tc.psum_pool(name="psum", bufs=8))
 
         offs_sb = keep.tile([P, S // 16], U16, name="offs_sb")
         pos1_sb = keep.tile([P, M // 16], U16, name="pos1_sb")
@@ -49,33 +51,31 @@ def tile_list_dental_unet_skip_kernel(
         w1w_raw = {}
         w1w = {}
 
-        def load_w1_words(b, tag):
-            w1w_raw[b] = keep.tile([P, 2, 256], I32, name="w1w_raw%d" % b, tag=tag, align_bytes=64)
+        def load_w1_words(b, tile):
+            w1w_raw[b] = tile
             words = w1_words.rearrange("a p n -> p a n").bitcast(I32)
             nc.sync.dma_start(w1w_raw[b][:], words[:, :, 256 * b : 256 * (b + 1)])
 
-        def order_w1_words(tile, b, t0, t1):
-            nc.vector.tensor_copy(
+        def order_w1_words(copy, tile, b, t0, t1):
+            copy(
                 tile[:].bitcast(U16).rearrange("p a (t m) -> p a t m", m=P),
                 w1w_raw[b][:].bitcast(U16).rearrange("p a (m t) -> p a t m", t=4)[:, :, t0:t1],
             )
             for t in range(t0, t1):
                 w1w[4 * b + t] = [tile[:, a, 64 * (t - t0) : 64 * (t - t0 + 1)] for a in range(2)]
 
-        load_w1_words(0, "w1w_raw0")
         nc.sync.dma_start(offs_sb[:], offs)
         tab_s = keep.tile([P, T], U8, name="tab_s", align_bytes=64)
         load_scale_rows(tab_s, tab_scales)
-        w1s_raw = keep.tile([P, H], U8, name="w1s_raw", tag="w1s_raw", align_bytes=64)
+        w1s_raw = after.tile([P, H], U8, name="w1s_raw", align_bytes=64, offset=0)
         load_scale_rows(w1s_raw, w1_scales)
         tab_w0 = keep.tile([P, T], I32, name="tab_w0", tag="stage0", align_bytes=64)
         nc.sync.dma_start(tab_w0[:], tab_words[0].rearrange("p n t -> p (n t)").bitcast(I32))
         nc.sync.dma_start(pos1_sb[:], pos1)
+        nc.sync.dma_start(pos2_sb[:], pos2)
         tab_w1 = head.tile([P, T], I32, name="tab_w1", align_bytes=64, offset=0)
         nc.sync.dma_start(tab_w1[:], tab_words[1].rearrange("p n t -> p (n t)").bitcast(I32))
-        b1_cols = keep.tile([P, 2, 8], F32, name="b1_cols")
-        load_channels(nc.sync, b1_cols, b1)
-        nc.sync.dma_start(pos2_sb[:], pos2)
+        load_w1_words(0, keep.tile([P, 2, 256], I32, name="w1w_raw0", align_bytes=64))
 
         zero_in = keep.tile([P, 8], F32, name="zero_in")
         zero = keep.tile([P, 8], F32, name="zero")
@@ -101,23 +101,25 @@ def tile_list_dental_unet_skip_kernel(
                 nc.sync.dma_start(tile[32 * q : 32 * q + 4, :, :].bitcast(I32), rows[8 * q : 8 * q + 8, cols].bitcast(I32))
 
         move_rows(scales, slice(0, S + N))
-        load_w1_words(1, "w1s_raw")
+        b1_cols = after.tile([P, 2, 8], F32, name="b1_cols", align_bytes=64, offset=0)
+        load_channels(nc.sync, b1_cols, b1)
+        load_w1_words(1, after.tile([P, 2, 256], I32, name="w1w_raw1", align_bytes=64, offset=64))
         move_rows(scales_late, slice(S + N, S + H))
 
-        order_w1_words(keep.tile([P, 2, 64], I32, name="w1w_tile0", align_bytes=64), 0, 0, 1)
-        order_w1_words(keep.tile([P, 2, 128], I32, name="w1w_tiles23", align_bytes=64), 0, 2, 4)
+        order_w1_words(nc.scalar.copy, keep.tile([P, 2, 64], I32, name="w1w_tile0", align_bytes=64), 0, 0, 1)
+        order_w1_words(nc.scalar.copy, keep.tile([P, 2, 192], I32, name="w1w_tiles123", align_bytes=64), 0, 1, 4)
 
         v_w0 = keep.tile([P, S], I32, name="v_w0", align_bytes=64)
         nc.vector.tensor_copy(v_w0[:].bitcast(U32), tab_w0[:].bitcast(U32).indirect(offs_sb[:]))
         v_w1 = [keep.tile([P, N], I32, name="v_w1_%d" % half, align_bytes=64) for half in range(2)]
-        for half in range(2):
+        pieces = ((0, 512), (512, 768), (768, 1024))
+        for c0, c1 in pieces:
             nc.vector.tensor_copy(
-                v_w1[half][:].bitcast(U32),
-                tab_w1[:].bitcast(U32).indirect(offs_sb[:, 32 * half : 32 * half + 32]),
+                v_w1[c0 // N][:, c0 % N : c0 % N + c1 - c0].bitcast(U32),
+                tab_w1[:].bitcast(U32).indirect(offs_sb[:, c0 // 16 : c1 // 16]),
             )
 
-        order_w1_words(head.tile([P, 2, 64], I32, name="w1w_tile1", align_bytes=64, offset=256), 0, 1, 2)
-        order_w1_words(keep.tile([P, 2, 256], I32, name="w1w_last", align_bytes=64), 1, 0, 4)
+        order_w1_words(nc.vector.tensor_copy, keep.tile([P, 2, 256], I32, name="w1w_last", align_bytes=64), 1, 0, 4)
 
         w2_raw = [
             keep.tile([P, 4 * H], F32, name="w2_raw0", tag="stage0", align_bytes=64),
@@ -134,34 +136,30 @@ def tile_list_dental_unet_skip_kernel(
         nc.sync.dma_start(w2_raw[1][:], w2_rows[1])
 
         h = [keep.tile([P, S], F32, name="h%d" % j) for j in range(8)]
-        g1 = [keep.tile([P, M], F32, name="g1_%d" % j, align_bytes=64) for j in range(5)]
+        g1 = [keep.tile([P, M], F32, name="g1_%d" % j, tag="g1_%d" % j, align_bytes=64) for j in range(5)]
         g1 = g1 + [held.tile([P, M], F32, name="g1_%d" % j, align_bytes=64, offset=2 * M + 8 * M * (j - 5)) for j in range(5, 8)]
         enc = {}
         res = [keep.tile([P, M], F32, name="res%d" % j) for j in range(8)]
         th = [keep.tile([P, 4 * M], F32, name="th%d" % b) for b in range(2)]
-        x_rows = [keep.tile([P, 4 * M], BF16, name="x_rows0"), late.tile([P, 4 * M], BF16, name="x_rows1", align_bytes=64, offset=0)]
+        x_rows = [keep.tile([P, 4 * M], BF16, name="x_rows0"), late.tile([P, 4 * M], BF16, name="x_rows1", align_bytes=64, offset=3 * M)]
         g2 = {}
         x_bf = [keep.tile([P, 4 * M], BF16, name="x_bf%d" % b, align_bytes=64) for b in range(2)]
         x_w = [keep.tile([P, M], U32, name="x_w%d" % b, align_bytes=64) for b in range(2)]
         x_s = {}
-        def w2_tiles(name, width, dtype):
-            return [
-                [keep.tile([P, width], dtype, name="%s%d_%d" % (name, pair, b), align_bytes=64) for b in range(2)]
-                for pair in range(4)
-            ]
-
-        w2_bf = w2_tiles("w2_bf", 8 * P, BF16)
-        w2_w = {}
+        w2_bf = [keep.tile([P, 16 * P], BF16, name="w2_bf%d" % pair, tag="w2_bf%d" % pair, align_bytes=64) for pair in range(3)]
+        w2_bf.append(last.tile([P, 16 * P], BF16, name="w2_bf3", align_bytes=64, offset=0))
+        w2_w = [keep.tile([P, 4 * P], U32, name="w2_w%d" % pair, align_bytes=64) for pair in range(4)]
         w2_s = {}
 
         def encode(j):
-            for half in range(2):
-                acc = psum.tile([P, N], F32, name="acc", tag="enc_bank")
-                cols = slice(half * N, (half + 1) * N)
+            for c0, c1 in pieces if j == 0 else ((0, N), (N, S)):
+                bank = psum.tile([P, N], F32, name="acc", tag="bank")
+                acc = bank[:, 0 : c1 - c0]
+                cols = slice(c0, c1)
                 for a in range(2):
-                    words = v_w0[:, cols] if a == 0 else v_w1[half][:]
+                    words = v_w0[:, cols] if a == 0 else v_w1[c0 // N][:, c0 % N : c0 % N + c1 - c0]
                     nc.tensor.matmul_mx(
-                        out=acc[:],
+                        out=acc,
                         lhsT=w1w[j][a].bitcast(FP4X4),
                         lhsT_scale=scales[:, a, S + P * j : S + P * (j + 1)] if j < 4 else scales_late[:, a, P * (j - 4) : P * (j - 3)],
                         rhs=words.bitcast(FP8X4),
@@ -169,22 +167,29 @@ def tile_list_dental_unet_skip_kernel(
                         start=(a == 0),
                         stop=(a == 1),
                     )
-                nc.scalar.activation(h[j][:, cols], acc[:], ACT.Identity, bias=col(b1_cols, j))
+                nc.scalar.activation(h[j][:, cols], acc, ACT.Identity, bias=col(b1_cols, j))
             nc.vector.tensor_copy(g1[j][:], h[j][:].indirect(pos1_sb[:]))
 
         def pick_skip(j):
-            if 2 <= j < 7:
+            if j == 6:
+                g2[j] = keep.tile([P, M], F32, name="g2_6", tag="w2_bf1", align_bytes=64)
+            elif 2 <= j < 6:
                 g2[j] = held.tile([P, M], F32, name="g2_%d" % j, align_bytes=64, offset=4 * M * (j - 2))
             else:
-                g2[j] = keep.tile([P, M], F32, name="g2_%d" % j, align_bytes=64)
+                g2[j] = keep.tile([P, M], F32, name="g2_%d" % j, tag="g1_%d" % j if j < 2 else "g2_7", align_bytes=64)
             nc.vector.tensor_copy(g2[j][:], h[j][:].indirect(pos2_sb[:]))
 
         def scale_skip(j):
-            enc[j] = keep.tile([P, M], F32, name="enc%d" % j, align_bytes=64)
             if j < 2:
-                nc.gpsimd.tensor_scalar(enc[j][:], g2[j][:], col(skip_cols, j), 0.0, ALU.mult, ALU.add)
+                enc[j] = keep.tile([P, M], F32, name="enc%d" % j, align_bytes=64)
+            elif j < 6:
+                enc[j] = head.tile([P, M], F32, name="enc%d" % j, align_bytes=64, offset=768 + 4 * M * (j - 2))
             else:
+                enc[j] = last.tile([P, M], F32, name="enc%d" % j, align_bytes=64, offset=4 * M * (j - 6))
+            if 2 <= j < 6:
                 nc.scalar.activation(enc[j][:], g2[j][:], ACT.Copy, scale=col(skip_cols, j))
+            else:
+                nc.gpsimd.tensor_scalar(enc[j][:], g2[j][:], col(skip_cols, j), 0.0, ALU.mult, ALU.add)
 
         def squash(j):
             b, t = divmod(j, 4)
@@ -205,67 +210,68 @@ def tile_list_dental_unet_skip_kernel(
                 )
 
         def quantize_x(b):
-            x_s[b] = late.tile([P, M], U8, name="x_s%d" % b, align_bytes=64, offset=M * b)
+            x_s[b] = late.tile([P, M], U8, name="x_s%d" % b, align_bytes=64, offset=4 * M + M * b)
             nc.vector.quantize_mx(out=x_w[b][:].bitcast(FP8X4), scales=x_s[b][:], in_=x_bf[b][:])
 
         def cast_w2(pair, b):
             nb, u = divmod(pair, 2)
             src = w2_raw[b][:].rearrange("p (r nb m u e) -> p nb u m r e", r=4, nb=2, u=2, e=2)[:, nb, u]
-            nc.scalar.copy(w2_bf[pair][b][:].rearrange("p (e m r) -> p m r e", e=2, r=4), src)
+            nc.scalar.copy(w2_bf[pair][:, 8 * P * b : 8 * P * (b + 1)].rearrange("p (e m r) -> p m r e", e=2, r=4), src)
 
-        def quantize_w2(pair, b, tag):
-            w2_w[pair, b] = keep.tile([P, 2 * P], U32, name="w2_w%d_%d" % (pair, b), tag=tag, align_bytes=64)
-            w2_s[pair, b] = late.tile([P, 2 * P], U8, name="w2_s%d_%d" % (pair, b), align_bytes=64, offset=2 * M + 2 * P * (2 * pair + b))
-            nc.vector.quantize_mx(out=w2_w[pair, b][:].bitcast(FP8X4), scales=w2_s[pair, b][:], in_=w2_bf[pair][b][:])
-
-        def make_w2(pair, b):
-            cast_w2(pair, b)
-            quantize_w2(pair, b, "w2_w%d_%d" % (pair, b))
+        def quantize_w2(pair, b0, b1):
+            if b0 == 0:
+                w2_s[pair] = late.tile([P, 4 * P], U8, name="w2_s%d" % pair, align_bytes=64, offset=6 * M + 4 * P * pair)
+            cols = slice(2 * P * b0, 2 * P * b1)
+            nc.vector.quantize_mx(
+                out=w2_w[pair][:, cols].bitcast(FP8X4), scales=w2_s[pair][:, cols], in_=w2_bf[pair][:, 8 * P * b0 : 8 * P * b1]
+            )
 
         out_rows = out.rearrange("(b p t) m -> b t p m", b=2, t=4)
 
         def decode(j):
             nb, t = divmod(j, 4)
             pair, e = divmod(j, 2)
-            acc = psum.tile([P, N], F32, name="acc", tag="dec_bank" if j < 4 else "enc_bank")
+            acc = psum.tile([P, N], F32, name="acc", tag="bank")
             for b in range(2):
                 nc.tensor.matmul_mx(
                     out=acc[:],
-                    lhsT=w2_w[pair, b][:, e * P : (e + 1) * P].bitcast(FP8X4),
-                    lhsT_scale=w2_s[pair, b][:, e * P : (e + 1) * P],
+                    lhsT=w2_w[pair][:, (2 * b + e) * P : (2 * b + e + 1) * P].bitcast(FP8X4),
+                    lhsT_scale=w2_s[pair][:, (2 * b + e) * P : (2 * b + e + 1) * P],
                     rhs=x_w[b][:].bitcast(FP8X4),
                     rhs_scale=x_s[b][:],
                     start=(b == 0),
                     stop=(b == 1),
                 )
-            width = M // 2 if j == 7 else M
-            for m0 in range(0, M, width):
-                ms = slice(m0, m0 + width)
+            for m0, m1 in ((0, 384), (384, M)) if j == 7 else ((0, M),):
+                ms = slice(m0, m1)
                 nc.vector.scalar_tensor_tensor(res[j][:, ms], acc[:, ms], col(b2_cols, j), enc[j][:, ms], ALU.add, ALU.max)
                 nc.sync.dma_start(out_rows[nb, t][:, ms], res[j][:, ms])
 
-        for j in range(8):
-            encode(j)
-            if j < 2:
-                pick_skip(j)
-            if 2 <= j < 7:
-                squash(j - 2)
-                scale_row(j - 2)
-            if j in (2, 3):
-                scale_skip(j - 2)
-        for j in range(5, 8):
-            squash(j)
-            scale_row(j)
+        for b in range(2):
+            for j in range(4 * b, 4 * b + 4):
+                encode(j)
+            for j in range(4 * b, 4 * b + 4):
+                squash(j)
+                scale_row(j)
+            if b == 0:
+                for j in range(2):
+                    pick_skip(j)
+                    scale_skip(j)
         pick_skip(7)
-        for j in range(2, 7):
+        for j in range(2, 6):
             pick_skip(j)
-        for pair in range(4):
-            for b in range(2):
-                make_w2(pair, b)
-                if pair == 0:
-                    quantize_x(b)
-            if pair > 0:
-                scale_skip(2 * pair)
-                scale_skip(2 * pair + 1)
+        for pair in range(3):
+            if pair < 2:
+                quantize_x(pair)
+            else:
+                pick_skip(6)
+            cast_w2(pair, 0)
+            cast_w2(pair, 1)
+            quantize_w2(pair, 0, 2)
+        for b in range(2):
+            cast_w2(3, b)
+            quantize_w2(3, b, b + 1)
+        for j in range(2, 8):
+            scale_skip(j)
         for j in range(8):
             decode(j)

@@ -31,6 +31,7 @@ def tile_list_dental_unet_skip_kernel(
         held = ctx.enter_context(tc.tile_pool(name="held", bufs=1))
         last = ctx.enter_context(tc.tile_pool(name="last", bufs=1))
         after = ctx.enter_context(tc.tile_pool(name="after", bufs=1))
+        stage = ctx.enter_context(tc.tile_pool(name="stage", bufs=1))
         psum = ctx.enter_context(tc.psum_pool(name="psum", bufs=8))
 
         offs_sb = keep.tile([P, S // 16], U16, name="offs_sb")
@@ -69,7 +70,7 @@ def tile_list_dental_unet_skip_kernel(
         load_scale_rows(tab_s, tab_scales)
         w1s_raw = after.tile([P, H], U8, name="w1s_raw", align_bytes=64, offset=0)
         load_scale_rows(w1s_raw, w1_scales)
-        tab_w0 = keep.tile([P, T], I32, name="tab_w0", tag="stage0", align_bytes=64)
+        tab_w0 = stage.tile([P, T], I32, name="tab_w0", align_bytes=64, offset=0)
         nc.sync.dma_start(tab_w0[:], tab_words[0].rearrange("p n t -> p (n t)").bitcast(I32))
         nc.sync.dma_start(pos1_sb[:], pos1)
         nc.sync.dma_start(pos2_sb[:], pos2)
@@ -111,6 +112,24 @@ def tile_list_dental_unet_skip_kernel(
 
         v_w0 = keep.tile([P, S], I32, name="v_w0", align_bytes=64)
         nc.vector.tensor_copy(v_w0[:].bitcast(U32), tab_w0[:].bitcast(U32).indirect(offs_sb[:]))
+
+        warm = keep.tile([P, N + N // 4 + P // 2], U32, name="warm", align_bytes=64)
+        nc.gpsimd.memset(warm[:], 0)
+        warm_s = warm[:, N : N + N // 4].bitcast(U8)
+        nc.vector.quantize_mx(out=warm[:, 0 : P // 4].bitcast(FP8X4), scales=warm_s[:, 0 : P // 4], in_=warm[:, N + N // 4 :].bitcast(BF16))
+        warm_lhs = stage.tile([P, P], U32, name="warm_lhs", align_bytes=64, offset=0)
+        nc.scalar.copy(warm_lhs[:], warm[:, 0:P])
+        warm_acc = psum.tile([P, N], F32, name="acc", tag="bank")
+        for step in range(4):
+            nc.tensor.matmul_mx(
+                out=warm_acc[:],
+                lhsT=warm_lhs[:].bitcast(FP8X4),
+                lhsT_scale=warm_s[:, 0:P],
+                rhs=warm[:, 0:N].bitcast(FP8X4),
+                rhs_scale=warm_s[:],
+                start=True,
+                stop=True,
+            )
         v_w1 = [keep.tile([P, N], I32, name="v_w1_%d" % half, align_bytes=64) for half in range(2)]
         pieces = ((0, 512), (512, 768), (768, 1024))
         for c0, c1 in pieces:
@@ -122,7 +141,7 @@ def tile_list_dental_unet_skip_kernel(
         order_w1_words(nc.vector.tensor_copy, keep.tile([P, 2, 256], I32, name="w1w_last", align_bytes=64), 1, 0, 4)
 
         w2_raw = [
-            keep.tile([P, 4 * H], F32, name="w2_raw0", tag="stage0", align_bytes=64),
+            stage.tile([P, 4 * H], F32, name="w2_raw0", align_bytes=64, offset=5 * N),
             head.tile([P, 4 * H], F32, name="w2_raw1", align_bytes=64, offset=768),
         ]
         w2_rows = w2.rearrange("(b p r) n -> b p (r n)", b=2, r=4)

@@ -18,6 +18,9 @@ ACT = mybir.ActivationFunctionType
 
 P = 128
 N = 512
+KB = 1024
+SPLIT = 256
+SHARED = 1
 
 
 def tile_list_dental_unet_skip_kernel(
@@ -26,20 +29,19 @@ def tile_list_dental_unet_skip_kernel(
     nc = tc.nc
     with ExitStack() as ctx:
         keep = ctx.enter_context(tc.tile_pool(name="keep", bufs=1))
-        head = ctx.enter_context(tc.tile_pool(name="head", bufs=1))
-        late = ctx.enter_context(tc.tile_pool(name="late", bufs=1))
-        held = ctx.enter_context(tc.tile_pool(name="held", bufs=1))
-        last = ctx.enter_context(tc.tile_pool(name="last", bufs=1))
+        stage0 = ctx.enter_context(tc.tile_pool(name="stage0", bufs=1))
+        stage1 = ctx.enter_context(tc.tile_pool(name="stage1", bufs=1))
         after = ctx.enter_context(tc.tile_pool(name="after", bufs=1))
-        stage = ctx.enter_context(tc.tile_pool(name="stage", bufs=1))
+        picks = ctx.enter_context(tc.tile_pool(name="picks", bufs=1))
+        late = ctx.enter_context(tc.tile_pool(name="late", bufs=1))
         psum = ctx.enter_context(tc.psum_pool(name="psum", bufs=8))
 
         offs_sb = keep.tile([P, S // 16], U16, name="offs_sb")
         pos1_sb = keep.tile([P, M // 16], U16, name="pos1_sb")
         pos2_sb = keep.tile([P, M // 16], U16, name="pos2_sb")
 
-        def load_channels(queue, tile, vec):
-            queue.dma_start(tile[:, :, 0:4], vec.rearrange("(b p t) -> p b t", b=2, t=4))
+        def load_channels(tile, vec):
+            nc.sync.dma_start(tile[:, :, 0:4], vec.rearrange("(b p t) -> p b t", b=2, t=4))
 
         def col(cols, j):
             return cols[:, j // 4, j % 4 : j % 4 + 1]
@@ -68,13 +70,13 @@ def tile_list_dental_unet_skip_kernel(
         nc.sync.dma_start(offs_sb[:], offs)
         tab_s = keep.tile([P, T], U8, name="tab_s", align_bytes=64)
         load_scale_rows(tab_s, tab_scales)
-        w1s_raw = after.tile([P, H], U8, name="w1s_raw", align_bytes=64, offset=0)
+        w1s_raw = late.tile([P, H], U8, name="w1s_raw", align_bytes=64, offset=7 * KB)
         load_scale_rows(w1s_raw, w1_scales)
-        tab_w0 = stage.tile([P, T], I32, name="tab_w0", align_bytes=64, offset=0)
+        tab_w0 = stage0.tile([P, T], I32, name="tab_w0", align_bytes=64, offset=4 * KB)
         nc.sync.dma_start(tab_w0[:], tab_words[0].rearrange("p n t -> p (n t)").bitcast(I32))
         nc.sync.dma_start(pos1_sb[:], pos1)
         nc.sync.dma_start(pos2_sb[:], pos2)
-        tab_w1 = head.tile([P, T], I32, name="tab_w1", align_bytes=64, offset=0)
+        tab_w1 = stage1.tile([P, T], I32, name="tab_w1", align_bytes=64, offset=4 * KB)
         nc.sync.dma_start(tab_w1[:], tab_words[1].rearrange("p n t -> p (n t)").bitcast(I32))
         load_w1_words(0, keep.tile([P, 2, 256], I32, name="w1w_raw0", align_bytes=64))
 
@@ -84,9 +86,7 @@ def tile_list_dental_unet_skip_kernel(
         nc.scalar.activation(zero[:, 0:1], zero_in[:, 0:1], ACT.Tanh)
 
         scales = keep.tile([P, 2, S + N], U8, name="scales", align_bytes=64)
-        scales_late = keep.tile([P, 2, N], U8, name="scales_late", align_bytes=64)
-        for tile in (scales, scales_late):
-            nc.vector.memset(tile[:].rearrange("p a n -> p (a n)").bitcast(I32), 0)
+        nc.vector.memset(scales[:].rearrange("p a n -> p (a n)").bitcast(I32), 0)
 
         picked_s = keep.tile([P, S], U8, name="picked_s", align_bytes=64)
         nc.vector.tensor_copy(picked_s[:], tab_s[:].indirect(offs_sb[:]))
@@ -102,13 +102,12 @@ def tile_list_dental_unet_skip_kernel(
                 nc.sync.dma_start(tile[32 * q : 32 * q + 4, :, :].bitcast(I32), rows[8 * q : 8 * q + 8, cols].bitcast(I32))
 
         move_rows(scales, slice(0, S + N))
-        b1_cols = after.tile([P, 2, 8], F32, name="b1_cols", align_bytes=64, offset=0)
-        load_channels(nc.sync, b1_cols, b1)
-        load_w1_words(1, after.tile([P, 2, 256], I32, name="w1w_raw1", align_bytes=64, offset=64))
-        move_rows(scales_late, slice(S + N, S + H))
+        b1_cols = late.tile([P, 2, 8], F32, name="b1_cols", align_bytes=64, offset=7 * KB)
+        load_channels(b1_cols, b1)
+        load_w1_words(1, late.tile([P, 2, 256], I32, name="w1w_raw1", align_bytes=64, offset=7 * KB + 64))
 
         order_w1_words(nc.scalar.copy, keep.tile([P, 2, 64], I32, name="w1w_tile0", align_bytes=64), 0, 0, 1)
-        order_w1_words(nc.scalar.copy, keep.tile([P, 2, 192], I32, name="w1w_tiles123", align_bytes=64), 0, 1, 4)
+        order_w1_words(nc.scalar.copy, after.tile([P, 2, 192], I32, name="w1w_tiles123", align_bytes=64, offset=0), 0, 1, 4)
 
         v_w0 = keep.tile([P, S], I32, name="v_w0", align_bytes=64)
         nc.vector.tensor_copy(v_w0[:].bitcast(U32), tab_w0[:].bitcast(U32).indirect(offs_sb[:]))
@@ -117,7 +116,7 @@ def tile_list_dental_unet_skip_kernel(
         nc.gpsimd.memset(warm[:], 0)
         warm_s = warm[:, N : N + N // 4].bitcast(U8)
         nc.vector.quantize_mx(out=warm[:, 0 : P // 4].bitcast(FP8X4), scales=warm_s[:, 0 : P // 4], in_=warm[:, N + N // 4 :].bitcast(BF16))
-        warm_lhs = stage.tile([P, P], U32, name="warm_lhs", align_bytes=64, offset=0)
+        warm_lhs = stage0.tile([P, P], U32, name="warm_lhs", align_bytes=64, offset=8 * KB)
         nc.scalar.copy(warm_lhs[:], warm[:, 0:P])
         warm_acc = psum.tile([P, N], F32, name="acc", tag="bank")
         for step in range(4):
@@ -130,6 +129,20 @@ def tile_list_dental_unet_skip_kernel(
                 start=True,
                 stop=True,
             )
+
+        w2_rows = w2.rearrange("(b p r) (nb n) -> nb b p r n", b=2, r=4, nb=2)
+        w2_raw = {}
+
+        def load_w2(nb, b, pool, offset):
+            w2_raw[nb, b] = pool.tile([P, 4, N], F32, name="w2_raw%d%d" % (nb, b), align_bytes=64, offset=offset)
+            nc.sync.dma_start(w2_raw[nb, b][:], w2_rows[nb, b])
+
+        load_w2(0, 0, stage0, 0)
+        load_w2(0, 1, stage0, 12 * KB)
+        scales_late = stage0.tile([P, 2, N], U8, name="scales_late", align_bytes=64, offset=9 * KB)
+        nc.vector.memset(scales_late[:].rearrange("p a n -> p (a n)").bitcast(I32), 0)
+        move_rows(scales_late, slice(S + N, S + H))
+
         v_w1 = [keep.tile([P, N], I32, name="v_w1_%d" % half, align_bytes=64) for half in range(2)]
         pieces = ((0, 512), (512, 768), (768, 1024))
         for c0, c1 in pieces:
@@ -140,35 +153,32 @@ def tile_list_dental_unet_skip_kernel(
 
         order_w1_words(nc.vector.tensor_copy, keep.tile([P, 2, 256], I32, name="w1w_last", align_bytes=64), 1, 0, 4)
 
-        w2_raw = [
-            stage.tile([P, 4 * H], F32, name="w2_raw0", align_bytes=64, offset=5 * N),
-            head.tile([P, 4 * H], F32, name="w2_raw1", align_bytes=64, offset=768),
-        ]
-        w2_rows = w2.rearrange("(b p r) n -> b p (r n)", b=2, r=4)
-        nc.sync.dma_start(w2_raw[0][:], w2_rows[0])
-        gain_cols = head.tile([P, 2, 8], F32, name="gain_cols", align_bytes=64, offset=0)
-        b2_cols = head.tile([P, 2, 8], F32, name="b2_cols", align_bytes=64, offset=128)
-        load_channels(nc.sync, gain_cols, gain)
-        skip_cols = head.tile([P, 2, 8], F32, name="skip_cols", align_bytes=64, offset=64)
-        load_channels(nc.sync, skip_cols, skip)
-        load_channels(nc.sync, b2_cols, b2)
-        nc.sync.dma_start(w2_raw[1][:], w2_rows[1])
-
+        gain_cols = stage1.tile([P, 2, 8], F32, name="gain_cols", align_bytes=64, offset=8 * KB)
+        skip_cols = stage1.tile([P, 2, 8], F32, name="skip_cols", align_bytes=64, offset=8 * KB + 64)
+        b2_cols = stage1.tile([P, 2, 8], F32, name="b2_cols", align_bytes=64, offset=8 * KB + 128)
+        load_channels(gain_cols, gain)
+        load_w2(1, 0, stage1, 9 * KB)
+        load_channels(skip_cols, skip)
+        load_channels(b2_cols, b2)
+        load_w2(1, 1, stage1, 17 * KB)
         h = [keep.tile([P, S], F32, name="h%d" % j) for j in range(8)]
-        g1 = [keep.tile([P, M], F32, name="g1_%d" % j, tag="g1_%d" % j, align_bytes=64) for j in range(5)]
-        g1 = g1 + [held.tile([P, M], F32, name="g1_%d" % j, align_bytes=64, offset=2 * M + 8 * M * (j - 5)) for j in range(5, 8)]
-        enc = {}
-        res = [keep.tile([P, M], F32, name="res%d" % j) for j in range(8)]
-        th = [keep.tile([P, 4 * M], F32, name="th%d" % b) for b in range(2)]
-        x_rows = [keep.tile([P, 4 * M], BF16, name="x_rows0"), late.tile([P, 4 * M], BF16, name="x_rows1", align_bytes=64, offset=3 * M)]
-        g2 = {}
-        x_bf = [keep.tile([P, 4 * M], BF16, name="x_bf%d" % b, align_bytes=64) for b in range(2)]
+        g1 = [picks.tile([P, M], F32, name="g1_%d" % j, align_bytes=64, offset=2 * KB * j) for j in range(8)]
+        th = [after.tile([P, 4, M], F32, name="th0", align_bytes=64, offset=0), late.tile([P, 4, M], F32, name="th1", align_bytes=64, offset=0)]
+        x_rows = picks.tile([P, 4, M - SPLIT], BF16, name="x_rows", align_bytes=64, offset=14 * KB)
+        x_bf0 = stage1.tile([P, 4 * M], BF16, name="x_bf0", align_bytes=64, offset=9 * KB)
+        x_bf1 = late.tile([P, 4 * M], BF16, name="x_bf1", align_bytes=64, offset=8 * KB)
+        x_bf = [x_bf0, x_bf1]
         x_w = [keep.tile([P, M], U32, name="x_w%d" % b, align_bytes=64) for b in range(2)]
+        w2_bf = [keep.tile([P, 4, 2, N], BF16, name="w2_bf%d" % nb, align_bytes=64) for nb in range(2)]
+        w2_w = [keep.tile([P, 2 * N], U32, name="w2_w%d" % nb, align_bytes=64) for nb in range(2)]
+        g2 = {}
+        enc = {}
         x_s = {}
-        w2_bf = [keep.tile([P, 16 * P], BF16, name="w2_bf%d" % pair, tag="w2_bf%d" % pair, align_bytes=64) for pair in range(3)]
-        w2_bf.append(last.tile([P, 16 * P], BF16, name="w2_bf3", align_bytes=64, offset=0))
-        w2_w = [keep.tile([P, 4 * P], U32, name="w2_w%d" % pair, align_bytes=64) for pair in range(4)]
         w2_s = {}
+        banks = {}
+        y = {}
+        diff = {}
+        gap = {}
 
         def encode(j):
             for c0, c1 in pieces if j == 0 else ((0, N), (N, S)):
@@ -189,108 +199,140 @@ def tile_list_dental_unet_skip_kernel(
                 nc.scalar.activation(h[j][:, cols], acc, ACT.Identity, bias=col(b1_cols, j))
             nc.vector.tensor_copy(g1[j][:], h[j][:].indirect(pos1_sb[:]))
 
-        def pick_skip(j):
-            if j == 6:
-                g2[j] = keep.tile([P, M], F32, name="g2_6", tag="w2_bf1", align_bytes=64)
-            elif 2 <= j < 6:
-                g2[j] = held.tile([P, M], F32, name="g2_%d" % j, align_bytes=64, offset=4 * M * (j - 2))
-            else:
-                g2[j] = keep.tile([P, M], F32, name="g2_%d" % j, tag="g1_%d" % j if j < 2 else "g2_7", align_bytes=64)
-            nc.vector.tensor_copy(g2[j][:], h[j][:].indirect(pos2_sb[:]))
-
-        def scale_skip(j):
-            if j < 2:
-                enc[j] = keep.tile([P, M], F32, name="enc%d" % j, align_bytes=64)
-            elif j < 6:
-                enc[j] = head.tile([P, M], F32, name="enc%d" % j, align_bytes=64, offset=768 + 4 * M * (j - 2))
-            else:
-                enc[j] = last.tile([P, M], F32, name="enc%d" % j, align_bytes=64, offset=4 * M * (j - 6))
-            if 2 <= j < 6:
-                nc.scalar.activation(enc[j][:], g2[j][:], ACT.Copy, scale=col(skip_cols, j))
-            else:
-                nc.gpsimd.tensor_scalar(enc[j][:], g2[j][:], col(skip_cols, j), 0.0, ALU.mult, ALU.add)
-
         def squash(j):
-            b, t = divmod(j, 4)
-            nc.scalar.activation(th[b][:, t * M : (t + 1) * M], g1[j][:], ACT.Tanh, bias=zero[:, 0:1])
+            nc.scalar.activation(th[j // 4][:, j % 4, :], g1[j][:], ACT.Tanh, bias=zero[:, 0:1])
 
-        def scale_row(j):
-            b, t = divmod(j, 4)
-            cols = slice(t * M, (t + 1) * M)
-            nc.gpsimd.tensor_scalar(x_rows[b][:, cols], th[b][:, cols], col(gain_cols, j), 0.0, ALU.mult, ALU.add)
-            if t == 3:
-                nc.gpsimd.tensor_scalar(
-                    x_bf[b][:].rearrange("p (m t) -> p m t", t=4),
-                    x_rows[b][:].rearrange("p (t m) -> p m t", t=4),
-                    1.0,
-                    0.0,
-                    ALU.mult,
-                    ALU.add,
-                )
-
-        def quantize_x(b):
-            x_s[b] = late.tile([P, M], U8, name="x_s%d" % b, align_bytes=64, offset=4 * M + M * b)
-            nc.vector.quantize_mx(out=x_w[b][:].bitcast(FP8X4), scales=x_s[b][:], in_=x_bf[b][:])
-
-        def cast_w2(pair, b):
-            nb, u = divmod(pair, 2)
-            src = w2_raw[b][:].rearrange("p (r nb m u e) -> p nb u m r e", r=4, nb=2, u=2, e=2)[:, nb, u]
-            nc.scalar.copy(w2_bf[pair][:, 8 * P * b : 8 * P * (b + 1)].rearrange("p (e m r) -> p m r e", e=2, r=4), src)
-
-        def quantize_w2(pair, b0, b1):
-            if b0 == 0:
-                w2_s[pair] = late.tile([P, 4 * P], U8, name="w2_s%d" % pair, align_bytes=64, offset=6 * M + 4 * P * pair)
-            cols = slice(2 * P * b0, 2 * P * b1)
-            nc.vector.quantize_mx(
-                out=w2_w[pair][:, cols].bitcast(FP8X4), scales=w2_s[pair][:, cols], in_=w2_bf[pair][:, 8 * P * b0 : 8 * P * b1]
+        def make_x(b, m0, m1):
+            nc.gpsimd.tensor_tensor(
+                x_bf[b][:, 4 * m0 : 4 * m1].rearrange("p (m t) -> p m t", t=4),
+                th[b][:, :, m0:m1].rearrange("p t m -> p m t"),
+                gain_cols[:, b : b + 1, 0:4].to_broadcast([P, m1 - m0, 4]),
+                ALU.mult,
             )
 
-        out_rows = out.rearrange("(b p t) m -> b t p m", b=2, t=4)
+        def make_x_rest():
+            for t in range(4):
+                nc.scalar.activation(x_rows[:, t, :], th[1][:, t, SPLIT:M], ACT.Copy, scale=col(gain_cols, 4 + t))
+            nc.scalar.copy(x_bf[1][:, 4 * SPLIT :].rearrange("p (m t) -> p m t", t=4), x_rows[:].rearrange("p t m -> p m t"))
 
-        def decode(j):
+        def cast_w2(nb, b, on_gpsimd):
+            dst = w2_bf[nb][:, :, b, :].rearrange("p t (m r) -> p m r t", r=4)
+            src = w2_raw[nb, b][:].rearrange("p r (m t) -> p m r t", t=4)
+            if on_gpsimd:
+                nc.gpsimd.tensor_scalar(dst.rearrange("p m r t -> p m t r"), src.rearrange("p m r t -> p m t r"), 1.0, 0.0, ALU.mult, ALU.add)
+            else:
+                nc.scalar.copy(dst, src)
+
+        def pick_skip(j, pool, offset):
+            g2[j] = pool.tile([P, M], F32, name="g2_%d" % j, align_bytes=64, offset=offset)
+            nc.vector.tensor_copy(g2[j][:], h[j][:].indirect(pos2_sb[:]))
+
+        def scale_skip(j, pool, offset):
+            enc[j] = pool.tile([P, M], F32, name="enc%d" % j, align_bytes=64, offset=offset)
+            if j < 2:
+                nc.gpsimd.tensor_scalar(enc[j][:], g2[j][:], col(skip_cols, j), 0.0, ALU.mult, ALU.add)
+            else:
+                nc.scalar.activation(enc[j][:], g2[j][:], ACT.Copy, scale=col(skip_cols, j))
+
+        def quantize_x(b):
+            x_s[b] = late.tile([P, M], U8, name="x_s%d" % b, align_bytes=64, offset=M * b)
+            nc.vector.quantize_mx(out=x_w[b][:].bitcast(FP8X4), scales=x_s[b][:], in_=x_bf[b][:])
+
+        def quantize_w2(nb, t0, t1):
+            if t0 == 0:
+                w2_s[nb] = late.tile([P, 2 * N], U8, name="w2_s%d" % nb, align_bytes=64, offset=KB + 2 * KB * nb)
+            cols = slice(2 * P * t0, 2 * P * t1)
+            nc.vector.quantize_mx(
+                out=w2_w[nb][:, cols].bitcast(FP8X4), scales=w2_s[nb][:, cols], in_=w2_bf[nb][:, t0:t1].rearrange("p t b n -> p (t b n)")
+            )
+
+        def project(j):
             nb, t = divmod(j, 4)
-            pair, e = divmod(j, 2)
-            acc = psum.tile([P, N], F32, name="acc", tag="bank")
+            banks[j] = psum.tile([P, N], F32, name="acc", tag="bank")
             for b in range(2):
+                cols = slice((2 * t + b) * P, (2 * t + b + 1) * P)
                 nc.tensor.matmul_mx(
-                    out=acc[:],
-                    lhsT=w2_w[pair][:, (2 * b + e) * P : (2 * b + e + 1) * P].bitcast(FP8X4),
-                    lhsT_scale=w2_s[pair][:, (2 * b + e) * P : (2 * b + e + 1) * P],
+                    out=banks[j][:],
+                    lhsT=w2_w[nb][:, cols].bitcast(FP8X4),
+                    lhsT_scale=w2_s[nb][:, cols],
                     rhs=x_w[b][:].bitcast(FP8X4),
                     rhs_scale=x_s[b][:],
                     start=(b == 0),
                     stop=(b == 1),
                 )
+
+        out_rows = out.rearrange("(b p t) m -> b t p m", b=2, t=4)
+
+        halves = (slice(0, M // 2), slice(M // 2, M))
+
+        def empty_y(j):
+            y[j] = keep.tile([P, M], F32, name="y%d" % j)
+            for ms in halves:
+                nc.scalar.activation(y[j][:, ms], banks[j][:, ms], ACT.Identity, bias=col(b2_cols, j))
+
+        def subtract(j):
+            diff[j] = keep.tile([P, M], F32, name="diff%d" % j)
+            for ms in halves:
+                nc.gpsimd.tensor_tensor(diff[j][:, ms], y[j][:, ms], enc[j][:, ms], ALU.subtract)
+
+        def rectify(j):
+            gap[j] = keep.tile([P, M], F32, name="gap%d" % j)
+            for ms in halves:
+                nc.scalar.activation(gap[j][:, ms], diff[j][:, ms], ACT.Relu)
+
+        def add_back(j):
+            res = keep.tile([P, M], F32, name="res%d" % j)
+            for ms in halves:
+                nc.gpsimd.tensor_tensor(res[:, ms], enc[j][:, ms], gap[j][:, ms], ALU.add)
+            nc.sync.dma_start(out_rows[j // 4, j % 4], res[:])
+
+        def finish(j):
+            res = keep.tile([P, M], F32, name="res%d" % j)
             for m0, m1 in ((0, 384), (384, M)) if j == 7 else ((0, M),):
                 ms = slice(m0, m1)
-                nc.vector.scalar_tensor_tensor(res[j][:, ms], acc[:, ms], col(b2_cols, j), enc[j][:, ms], ALU.add, ALU.max)
-                nc.sync.dma_start(out_rows[nb, t][:, ms], res[j][:, ms])
+                nc.vector.scalar_tensor_tensor(res[:, ms], banks[j][:, ms], col(b2_cols, j), enc[j][:, ms], ALU.add, ALU.max)
+                nc.sync.dma_start(out_rows[j // 4, j % 4][:, ms], res[:, ms])
 
-        for b in range(2):
-            for j in range(4 * b, 4 * b + 4):
-                encode(j)
-            for j in range(4 * b, 4 * b + 4):
-                squash(j)
-                scale_row(j)
-            if b == 0:
-                for j in range(2):
-                    pick_skip(j)
-                    scale_skip(j)
-        pick_skip(7)
-        for j in range(2, 6):
-            pick_skip(j)
-        for pair in range(3):
-            if pair < 2:
-                quantize_x(pair)
-            else:
-                pick_skip(6)
-            cast_w2(pair, 0)
-            cast_w2(pair, 1)
-            quantize_w2(pair, 0, 2)
-        for b in range(2):
-            cast_w2(3, b)
-            quantize_w2(3, b, b + 1)
-        for j in range(2, 8):
-            scale_skip(j)
+        cast_w2(0, 0, True)
+        cast_w2(0, 1, True)
+        cast_w2(1, 0, True)
+        for j in range(4):
+            encode(j)
+        for j in range(4):
+            squash(j)
+        make_x(0, 0, M)
+        for j in range(3):
+            pick_skip(j, picks, 2 * KB * j)
+        for j in range(2):
+            scale_skip(j, stage0, 2 * KB * j)
+        for j in range(4, 8):
+            encode(j)
+        for j in range(4, 8):
+            squash(j)
+        make_x(1, 0, SPLIT)
+        make_x_rest()
+        for j in range(3, 6):
+            pick_skip(j, picks, 2 * KB * (j + 1))
+        quantize_w2(0, 0, 2)
+        quantize_x(0)
+        quantize_x(1)
+        quantize_w2(0, 2, 4)
+        cast_w2(1, 1, False)
+        scale_skip(2, picks, 14 * KB)
+        quantize_w2(1, 0, 4)
+        pick_skip(6, late, 8 * KB)
         for j in range(8):
-            decode(j)
+            project(j)
+        empty_y(0)
+        subtract(0)
+        scale_skip(3, stage1, 17 * KB)
+        rectify(0)
+        add_back(0)
+        for j in range(4, 7):
+            scale_skip(j, stage1, 17 * KB + 2 * KB * (j - 3))
+        for j in range(1, 5):
+            finish(j)
+        pick_skip(7, stage1, 17 * KB)
+        scale_skip(7, stage0, 4 * KB)
+        for j in range(5, 8):
+            finish(j)

@@ -162,23 +162,24 @@ def tile_list_dental_unet_skip_kernel(
         load_channels(b2_cols, b2)
         load_w2(1, 1, stage1, 17 * KB)
         h = [keep.tile([P, S], F32, name="h%d" % j) for j in range(8)]
-        g1 = [picks.tile([P, M], F32, name="g1_%d" % j, align_bytes=64, offset=2 * KB * j) for j in range(8)]
+        g1 = [picks.tile([P, M], F32, name="g1_%d" % j, align_bytes=64, offset=2 * KB * j if j < 7 else 20 * KB) for j in range(8)]
         th = [after.tile([P, 4, M], F32, name="th0", align_bytes=64, offset=0), late.tile([P, 4, M], F32, name="th1", align_bytes=64, offset=0)]
-        x_rows = picks.tile([P, 4, M - SPLIT], BF16, name="x_rows", align_bytes=64, offset=14 * KB)
+        x_rows = picks.tile([P, 4, M - SPLIT], BF16, name="x_rows", align_bytes=64, offset=20 * KB)
         x_bf0 = stage1.tile([P, 4 * M], BF16, name="x_bf0", align_bytes=64, offset=9 * KB)
         x_bf1 = late.tile([P, 4 * M], BF16, name="x_bf1", align_bytes=64, offset=8 * KB)
         x_bf = [x_bf0, x_bf1]
         x_w = [keep.tile([P, M], U32, name="x_w%d" % b, align_bytes=64) for b in range(2)]
-        w2_bf = [keep.tile([P, 4, 2, N], BF16, name="w2_bf%d" % nb, align_bytes=64) for nb in range(2)]
+        w2_bf0 = keep.tile([P, 4, 2, N], BF16, name="w2_bf0", align_bytes=64)
+        w2_bf1 = [
+            keep.tile([P, 4, N], BF16, name="w2_bf10", align_bytes=64),
+            picks.tile([P, 4, N], BF16, name="w2_bf11", align_bytes=64, offset=21 * KB + 768),
+        ]
         w2_w = [keep.tile([P, 2 * N], U32, name="w2_w%d" % nb, align_bytes=64) for nb in range(2)]
         g2 = {}
         enc = {}
         x_s = {}
         w2_s = {}
         banks = {}
-        y = {}
-        diff = {}
-        gap = {}
 
         def encode(j):
             for c0, c1 in pieces if j == 0 else ((0, N), (N, S)):
@@ -216,7 +217,7 @@ def tile_list_dental_unet_skip_kernel(
             nc.scalar.copy(x_bf[1][:, 4 * SPLIT :].rearrange("p (m t) -> p m t", t=4), x_rows[:].rearrange("p t m -> p m t"))
 
         def cast_w2(nb, b, on_gpsimd):
-            dst = w2_bf[nb][:, :, b, :].rearrange("p t (m r) -> p m r t", r=4)
+            dst = (w2_bf0[:, :, b, :] if nb == 0 else w2_bf1[b][:]).rearrange("p t (m r) -> p m r t", r=4)
             src = w2_raw[nb, b][:].rearrange("p r (m t) -> p m r t", t=4)
             if on_gpsimd:
                 nc.gpsimd.tensor_scalar(dst.rearrange("p m r t -> p m t r"), src.rearrange("p m r t -> p m t r"), 1.0, 0.0, ALU.mult, ALU.add)
@@ -229,28 +230,28 @@ def tile_list_dental_unet_skip_kernel(
 
         def scale_skip(j, pool, offset):
             enc[j] = pool.tile([P, M], F32, name="enc%d" % j, align_bytes=64, offset=offset)
-            if j < 2:
+            if j < 1:
                 nc.gpsimd.tensor_scalar(enc[j][:], g2[j][:], col(skip_cols, j), 0.0, ALU.mult, ALU.add)
             else:
                 nc.scalar.activation(enc[j][:], g2[j][:], ACT.Copy, scale=col(skip_cols, j))
 
         def quantize_x(b):
-            x_s[b] = late.tile([P, M], U8, name="x_s%d" % b, align_bytes=64, offset=M * b)
+            x_s[b] = picks.tile([P, M], U8, name="x_s%d" % b, align_bytes=64, offset=20 * KB + 64 if b == 0 else 16 * KB)
             nc.vector.quantize_mx(out=x_w[b][:].bitcast(FP8X4), scales=x_s[b][:], in_=x_bf[b][:])
 
-        def quantize_w2(nb, t0, t1):
-            if t0 == 0:
-                w2_s[nb] = late.tile([P, 2 * N], U8, name="w2_s%d" % nb, align_bytes=64, offset=KB + 2 * KB * nb)
-            cols = slice(2 * P * t0, 2 * P * t1)
-            nc.vector.quantize_mx(
-                out=w2_w[nb][:, cols].bitcast(FP8X4), scales=w2_s[nb][:, cols], in_=w2_bf[nb][:, t0:t1].rearrange("p t b n -> p (t b n)")
-            )
+        def quantize_w2(nb, part):
+            if part == 0:
+                w2_s[nb] = picks.tile([P, 2 * N], U8, name="w2_s%d" % nb, align_bytes=64, offset=20 * KB + 704 if nb == 0 else 19 * KB + 64)
+            cols = slice(N * part, N * (part + 1))
+            rows_bf = w2_bf0[:, 2 * part : 2 * part + 2].rearrange("p t b n -> p (t b n)") if nb == 0 else w2_bf1[part][:].rearrange("p t n -> p (t n)")
+            nc.vector.quantize_mx(out=w2_w[nb][:, cols].bitcast(FP8X4), scales=w2_s[nb][:, cols], in_=rows_bf)
 
         def project(j):
             nb, t = divmod(j, 4)
             banks[j] = psum.tile([P, N], F32, name="acc", tag="bank")
             for b in range(2):
-                cols = slice((2 * t + b) * P, (2 * t + b + 1) * P)
+                first = 2 * t + b if nb == 0 else 4 * b + t
+                cols = slice(first * P, (first + 1) * P)
                 nc.tensor.matmul_mx(
                     out=banks[j][:],
                     lhsT=w2_w[nb][:, cols].bitcast(FP8X4),
@@ -265,33 +266,37 @@ def tile_list_dental_unet_skip_kernel(
 
         halves = (slice(0, M // 2), slice(M // 2, M))
 
-        def empty_y(j):
-            y[j] = keep.tile([P, M], F32, name="y%d" % j)
-            for ms in halves:
-                nc.scalar.activation(y[j][:, ms], banks[j][:, ms], ACT.Identity, bias=col(b2_cols, j))
-
-        def subtract(j):
-            diff[j] = keep.tile([P, M], F32, name="diff%d" % j)
-            for ms in halves:
-                nc.gpsimd.tensor_tensor(diff[j][:, ms], y[j][:, ms], enc[j][:, ms], ALU.subtract)
-
-        def rectify(j):
-            gap[j] = keep.tile([P, M], F32, name="gap%d" % j)
-            for ms in halves:
-                nc.scalar.activation(gap[j][:, ms], diff[j][:, ms], ACT.Relu)
-
-        def add_back(j):
+        def finish_aside(j):
+            y = keep.tile([P, M], F32, name="y")
+            diff = keep.tile([P, M], F32, name="diff")
+            gap = keep.tile([P, M], F32, name="gap")
             res = keep.tile([P, M], F32, name="res%d" % j)
-            for ms in halves:
-                nc.gpsimd.tensor_tensor(res[:, ms], enc[j][:, ms], gap[j][:, ms], ALU.add)
-            nc.sync.dma_start(out_rows[j // 4, j % 4], res[:])
+            nc.scalar.activation(y[:], banks[j][:], ACT.Identity, bias=col(b2_cols, j))
+            nc.gpsimd.tensor_tensor(diff[:], y[:], enc[j][:], ALU.subtract)
+            nc.scalar.activation(gap[:], diff[:], ACT.Relu)
+            nc.gpsimd.tensor_tensor(res[:], enc[j][:], gap[:], ALU.add)
+            return res
 
         def finish(j):
             res = keep.tile([P, M], F32, name="res%d" % j)
-            for m0, m1 in ((0, 384), (384, M)) if j == 7 else ((0, M),):
-                ms = slice(m0, m1)
-                nc.vector.scalar_tensor_tensor(res[:, ms], banks[j][:, ms], col(b2_cols, j), enc[j][:, ms], ALU.add, ALU.max)
-                nc.sync.dma_start(out_rows[j // 4, j % 4][:, ms], res[:, ms])
+            nc.vector.scalar_tensor_tensor(res[:], banks[j][:], col(b2_cols, j), enc[j][:], ALU.add, ALU.max)
+            nc.sync.dma_start(out_rows[j // 4, j % 4], res[:])
+
+        def spread_skip(j):
+            wide = keep.tile([P, M // 2], F32, name="skip_wide")
+            nc.gpsimd.tensor_scalar(wide[:], col(skip_cols, j).to_broadcast([P, M // 2]), 1.0, 0.0, ALU.mult, ALU.add)
+            return wide
+
+        def pick_scaled(j, half, wide, pool, offset):
+            enc[j, half] = pool.tile([P, M // 2], F32, name="enc%d_%d" % (j, half), align_bytes=64, offset=offset)
+            offsets = pos2_sb[:, half * M // 32 : (half + 1) * M // 32]
+            nc.vector.tensor_tensor(enc[j, half][:], h[j][:].indirect(offsets), wide[:], ALU.mult)
+
+        def finish_half(j, half):
+            res = keep.tile([P, M // 2], F32, name="res%d_%d" % (j, half))
+            ms = halves[half]
+            nc.vector.scalar_tensor_tensor(res[:], banks[j][:, ms], col(b2_cols, j), enc[j, half][:], ALU.add, ALU.max)
+            nc.sync.dma_start(out_rows[j // 4, j % 4][:, ms], res[:])
 
         cast_w2(0, 0, True)
         cast_w2(0, 1, True)
@@ -303,8 +308,8 @@ def tile_list_dental_unet_skip_kernel(
         make_x(0, 0, M)
         for j in range(3):
             pick_skip(j, picks, 2 * KB * j)
-        for j in range(2):
-            scale_skip(j, stage0, 2 * KB * j)
+        scale_skip(0, stage0, 0)
+        wide = spread_skip(7)
         for j in range(4, 8):
             encode(j)
         for j in range(4, 8):
@@ -313,26 +318,25 @@ def tile_list_dental_unet_skip_kernel(
         make_x_rest()
         for j in range(3, 6):
             pick_skip(j, picks, 2 * KB * (j + 1))
-        quantize_w2(0, 0, 2)
+        quantize_w2(0, 0)
         quantize_x(0)
         quantize_x(1)
-        quantize_w2(0, 2, 4)
+        quantize_w2(0, 1)
         cast_w2(1, 1, False)
-        scale_skip(2, picks, 14 * KB)
-        quantize_w2(1, 0, 4)
+        scale_skip(1, late, 4 * KB)
+        quantize_w2(1, 0)
+        quantize_w2(1, 1)
         pick_skip(6, late, 8 * KB)
         for j in range(8):
             project(j)
-        empty_y(0)
-        subtract(0)
-        scale_skip(3, stage1, 17 * KB)
-        rectify(0)
-        add_back(0)
-        for j in range(4, 7):
-            scale_skip(j, stage1, 17 * KB + 2 * KB * (j - 3))
-        for j in range(1, 5):
+        first = finish_aside(0)
+        for j in range(2, 6):
+            scale_skip(j, stage1, 17 * KB + 2 * KB * (j - 2))
+        scale_skip(6, stage1, 0)
+        nc.scalar.dma_start(out_rows[0, 0], first[:])
+        for j in range(1, 7):
             finish(j)
-        pick_skip(7, stage1, 17 * KB)
-        scale_skip(7, stage0, 4 * KB)
-        for j in range(5, 8):
-            finish(j)
+        for half in range(2):
+            pick_scaled(7, half, wide, stage1, (23 + half) * KB)
+        finish_half(7, 0)
+        finish_half(7, 1)

@@ -19,8 +19,8 @@ ACT = mybir.ActivationFunctionType
 P = 128
 N = 512
 KB = 1024
-SPLIT = 256
-SHARED = 1
+SPLIT = 160
+LAST = 256
 
 
 def tile_list_dental_unet_skip_kernel(
@@ -181,24 +181,33 @@ def tile_list_dental_unet_skip_kernel(
         w2_s = {}
         banks = {}
 
+        def multiply(j, c0, c1):
+            bank = psum.tile([P, N], F32, name="acc", tag="bank")
+            acc = bank[:, 0 : c1 - c0]
+            cols = slice(c0, c1)
+            for a in range(2):
+                words = v_w0[:, cols] if a == 0 else v_w1[c0 // N][:, c0 % N : c0 % N + c1 - c0]
+                nc.tensor.matmul_mx(
+                    out=acc,
+                    lhsT=w1w[j][a].bitcast(FP4X4),
+                    lhsT_scale=scales[:, a, S + P * j : S + P * (j + 1)] if j < 4 else scales_late[:, a, P * (j - 4) : P * (j - 3)],
+                    rhs=words.bitcast(FP8X4),
+                    rhs_scale=scales[:, a, cols],
+                    start=(a == 0),
+                    stop=(a == 1),
+                )
+            return acc
+
+        def empty(j, c0, c1, acc):
+            nc.scalar.activation(h[j][:, c0:c1], acc, ACT.Identity, bias=col(b1_cols, j))
+
+        def pick_coarse(j):
+            nc.vector.tensor_copy(g1[j][:], h[j][:].indirect(pos1_sb[:]))
+
         def encode(j):
             for c0, c1 in pieces if j == 0 else ((0, N), (N, S)):
-                bank = psum.tile([P, N], F32, name="acc", tag="bank")
-                acc = bank[:, 0 : c1 - c0]
-                cols = slice(c0, c1)
-                for a in range(2):
-                    words = v_w0[:, cols] if a == 0 else v_w1[c0 // N][:, c0 % N : c0 % N + c1 - c0]
-                    nc.tensor.matmul_mx(
-                        out=acc,
-                        lhsT=w1w[j][a].bitcast(FP4X4),
-                        lhsT_scale=scales[:, a, S + P * j : S + P * (j + 1)] if j < 4 else scales_late[:, a, P * (j - 4) : P * (j - 3)],
-                        rhs=words.bitcast(FP8X4),
-                        rhs_scale=scales[:, a, cols],
-                        start=(a == 0),
-                        stop=(a == 1),
-                    )
-                nc.scalar.activation(h[j][:, cols], acc, ACT.Identity, bias=col(b1_cols, j))
-            nc.vector.tensor_copy(g1[j][:], h[j][:].indirect(pos1_sb[:]))
+                empty(j, c0, c1, multiply(j, c0, c1))
+            pick_coarse(j)
 
         def squash(j):
             nc.scalar.activation(th[j // 4][:, j % 4, :], g1[j][:], ACT.Tanh, bias=zero[:, 0:1])
@@ -230,21 +239,21 @@ def tile_list_dental_unet_skip_kernel(
 
         def scale_skip(j, pool, offset):
             enc[j] = pool.tile([P, M], F32, name="enc%d" % j, align_bytes=64, offset=offset)
-            if j < 1:
+            if j < 2:
                 nc.gpsimd.tensor_scalar(enc[j][:], g2[j][:], col(skip_cols, j), 0.0, ALU.mult, ALU.add)
             else:
                 nc.scalar.activation(enc[j][:], g2[j][:], ACT.Copy, scale=col(skip_cols, j))
 
         def quantize_x(b):
-            x_s[b] = picks.tile([P, M], U8, name="x_s%d" % b, align_bytes=64, offset=20 * KB + 64 if b == 0 else 16 * KB)
+            x_s[b] = late.tile([P, M], U8, name="x_s%d" % b, align_bytes=64, offset=M * b)
             nc.vector.quantize_mx(out=x_w[b][:].bitcast(FP8X4), scales=x_s[b][:], in_=x_bf[b][:])
 
         def quantize_w2(nb, part):
-            if part == 0:
-                w2_s[nb] = picks.tile([P, 2 * N], U8, name="w2_s%d" % nb, align_bytes=64, offset=20 * KB + 704 if nb == 0 else 19 * KB + 64)
+            pool, offset = (late, KB) if nb + part == 0 else (picks, 20 * KB + N * (2 * nb + part - 1))
+            w2_s[nb, part] = pool.tile([P, N], U8, name="w2_s%d%d" % (nb, part), align_bytes=64, offset=offset)
             cols = slice(N * part, N * (part + 1))
             rows_bf = w2_bf0[:, 2 * part : 2 * part + 2].rearrange("p t b n -> p (t b n)") if nb == 0 else w2_bf1[part][:].rearrange("p t n -> p (t n)")
-            nc.vector.quantize_mx(out=w2_w[nb][:, cols].bitcast(FP8X4), scales=w2_s[nb][:, cols], in_=rows_bf)
+            nc.vector.quantize_mx(out=w2_w[nb][:, cols].bitcast(FP8X4), scales=w2_s[nb, part][:], in_=rows_bf)
 
         def project(j):
             nb, t = divmod(j, 4)
@@ -255,7 +264,7 @@ def tile_list_dental_unet_skip_kernel(
                 nc.tensor.matmul_mx(
                     out=banks[j][:],
                     lhsT=w2_w[nb][:, cols].bitcast(FP8X4),
-                    lhsT_scale=w2_s[nb][:, cols],
+                    lhsT_scale=w2_s[nb, first // 4][:, first % 4 * P : (first % 4 + 1) * P],
                     rhs=x_w[b][:].bitcast(FP8X4),
                     rhs_scale=x_s[b][:],
                     start=(b == 0),
@@ -264,7 +273,7 @@ def tile_list_dental_unet_skip_kernel(
 
         out_rows = out.rearrange("(b p t) m -> b t p m", b=2, t=4)
 
-        halves = (slice(0, M // 2), slice(M // 2, M))
+        halves = (slice(0, LAST), slice(LAST, M))
 
         def finish_aside(j):
             y = keep.tile([P, M], F32, name="y")
@@ -283,18 +292,19 @@ def tile_list_dental_unet_skip_kernel(
             nc.sync.dma_start(out_rows[j // 4, j % 4], res[:])
 
         def spread_skip(j):
-            wide = keep.tile([P, M // 2], F32, name="skip_wide")
-            nc.gpsimd.tensor_scalar(wide[:], col(skip_cols, j).to_broadcast([P, M // 2]), 1.0, 0.0, ALU.mult, ALU.add)
+            wide = late.tile([P, LAST], F32, name="skip_wide", align_bytes=64, offset=6 * KB)
+            nc.scalar.copy(wide[:], col(skip_cols, j).to_broadcast([P, LAST]))
             return wide
 
         def pick_scaled(j, half, wide, pool, offset):
-            enc[j, half] = pool.tile([P, M // 2], F32, name="enc%d_%d" % (j, half), align_bytes=64, offset=offset)
-            offsets = pos2_sb[:, half * M // 32 : (half + 1) * M // 32]
-            nc.vector.tensor_tensor(enc[j, half][:], h[j][:].indirect(offsets), wide[:], ALU.mult)
+            ms = halves[half]
+            enc[j, half] = pool.tile([P, ms.stop - ms.start], F32, name="enc%d_%d" % (j, half), align_bytes=64, offset=offset)
+            offsets = pos2_sb[:, ms.start // 16 : ms.stop // 16]
+            nc.vector.tensor_tensor(enc[j, half][:], h[j][:].indirect(offsets), wide[:, 0 : ms.stop - ms.start], ALU.mult)
 
         def finish_half(j, half):
-            res = keep.tile([P, M // 2], F32, name="res%d_%d" % (j, half))
             ms = halves[half]
+            res = keep.tile([P, ms.stop - ms.start], F32, name="res%d_%d" % (j, half))
             nc.vector.scalar_tensor_tensor(res[:], banks[j][:, ms], col(b2_cols, j), enc[j, half][:], ALU.add, ALU.max)
             nc.sync.dma_start(out_rows[j // 4, j % 4][:, ms], res[:])
 
@@ -308,8 +318,8 @@ def tile_list_dental_unet_skip_kernel(
         make_x(0, 0, M)
         for j in range(3):
             pick_skip(j, picks, 2 * KB * j)
-        scale_skip(0, stage0, 0)
-        wide = spread_skip(7)
+        for j in range(2):
+            scale_skip(j, stage0, 2 * KB * j)
         for j in range(4, 8):
             encode(j)
         for j in range(4, 8):
@@ -323,7 +333,6 @@ def tile_list_dental_unet_skip_kernel(
         quantize_x(1)
         quantize_w2(0, 1)
         cast_w2(1, 1, False)
-        scale_skip(1, late, 4 * KB)
         quantize_w2(1, 0)
         quantize_w2(1, 1)
         pick_skip(6, late, 8 * KB)
@@ -333,10 +342,11 @@ def tile_list_dental_unet_skip_kernel(
         for j in range(2, 6):
             scale_skip(j, stage1, 17 * KB + 2 * KB * (j - 2))
         scale_skip(6, stage1, 0)
+        wide = spread_skip(7)
         nc.scalar.dma_start(out_rows[0, 0], first[:])
         for j in range(1, 7):
             finish(j)
         for half in range(2):
-            pick_scaled(7, half, wide, stage1, (23 + half) * KB)
+            pick_scaled(7, half, wide, stage1, 23 * KB + 4 * LAST * half)
         finish_half(7, 0)
         finish_half(7, 1)

@@ -19,7 +19,7 @@ ACT = mybir.ActivationFunctionType
 P = 128
 N = 512
 KB = 1024
-SPLIT = 160
+SPLIT = 168
 LAST = 256
 
 
@@ -172,7 +172,8 @@ def tile_list_dental_unet_skip_kernel(
         w2_bf0 = keep.tile([P, 4, 2, N], BF16, name="w2_bf0", align_bytes=64)
         w2_bf1 = [
             keep.tile([P, 4, N], BF16, name="w2_bf10", align_bytes=64),
-            picks.tile([P, 4, N], BF16, name="w2_bf11", align_bytes=64, offset=21 * KB + 768),
+            keep.tile([P, 2, N], BF16, name="w2_bf11", align_bytes=64),
+            picks.tile([P, 2, N], BF16, name="w2_bf12", align_bytes=64, offset=22 * KB),
         ]
         w2_w = [keep.tile([P, 2 * N], U32, name="w2_w%d" % nb, align_bytes=64) for nb in range(2)]
         g2 = {}
@@ -225,13 +226,13 @@ def tile_list_dental_unet_skip_kernel(
                 nc.scalar.activation(x_rows[:, t, :], th[1][:, t, SPLIT:M], ACT.Copy, scale=col(gain_cols, 4 + t))
             nc.scalar.copy(x_bf[1][:, 4 * SPLIT :].rearrange("p (m t) -> p m t", t=4), x_rows[:].rearrange("p t m -> p m t"))
 
-        def cast_w2(nb, b, on_gpsimd):
-            dst = (w2_bf0[:, :, b, :] if nb == 0 else w2_bf1[b][:]).rearrange("p t (m r) -> p m r t", r=4)
-            src = w2_raw[nb, b][:].rearrange("p r (m t) -> p m r t", t=4)
+        def cast_w2(dst, nb, b, t0, t1, on_gpsimd):
+            src = w2_raw[nb, b][:].rearrange("p r (m t) -> p m t r", t=4)[:, :, t0:t1, :]
+            dst = dst.rearrange("p t (m r) -> p m t r", r=4)
             if on_gpsimd:
-                nc.gpsimd.tensor_scalar(dst.rearrange("p m r t -> p m t r"), src.rearrange("p m r t -> p m t r"), 1.0, 0.0, ALU.mult, ALU.add)
+                nc.gpsimd.tensor_scalar(dst, src, 1.0, 0.0, ALU.mult, ALU.add)
             else:
-                nc.scalar.copy(dst, src)
+                nc.scalar.copy(dst.rearrange("p m t r -> p m r t"), src.rearrange("p m t r -> p m r t"))
 
         def pick_skip(j, pool, offset):
             g2[j] = pool.tile([P, M], F32, name="g2_%d" % j, align_bytes=64, offset=offset)
@@ -239,21 +240,17 @@ def tile_list_dental_unet_skip_kernel(
 
         def scale_skip(j, pool, offset):
             enc[j] = pool.tile([P, M], F32, name="enc%d" % j, align_bytes=64, offset=offset)
-            if j < 2:
-                nc.gpsimd.tensor_scalar(enc[j][:], g2[j][:], col(skip_cols, j), 0.0, ALU.mult, ALU.add)
-            else:
-                nc.scalar.activation(enc[j][:], g2[j][:], ACT.Copy, scale=col(skip_cols, j))
+            nc.scalar.activation(enc[j][:], g2[j][:], ACT.Copy, scale=col(skip_cols, j))
 
         def quantize_x(b):
             x_s[b] = late.tile([P, M], U8, name="x_s%d" % b, align_bytes=64, offset=M * b)
             nc.vector.quantize_mx(out=x_w[b][:].bitcast(FP8X4), scales=x_s[b][:], in_=x_bf[b][:])
 
-        def quantize_w2(nb, part):
-            pool, offset = (late, KB) if nb + part == 0 else (picks, 20 * KB + N * (2 * nb + part - 1))
-            w2_s[nb, part] = pool.tile([P, N], U8, name="w2_s%d%d" % (nb, part), align_bytes=64, offset=offset)
-            cols = slice(N * part, N * (part + 1))
-            rows_bf = w2_bf0[:, 2 * part : 2 * part + 2].rearrange("p t b n -> p (t b n)") if nb == 0 else w2_bf1[part][:].rearrange("p t n -> p (t n)")
-            nc.vector.quantize_mx(out=w2_w[nb][:, cols].bitcast(FP8X4), scales=w2_s[nb, part][:], in_=rows_bf)
+        def quantize_w2(nb, c0, c1, rows_bf, pool, offset):
+            plane = pool.tile([P, (c1 - c0) * P], U8, name="w2_s%d%d" % (nb, c0), align_bytes=64, offset=offset)
+            nc.vector.quantize_mx(out=w2_w[nb][:, c0 * P : c1 * P].bitcast(FP8X4), scales=plane[:], in_=rows_bf)
+            for c in range(c0, c1):
+                w2_s[nb, c] = plane[:, (c - c0) * P : (c - c0 + 1) * P]
 
         def project(j):
             nb, t = divmod(j, 4)
@@ -264,7 +261,7 @@ def tile_list_dental_unet_skip_kernel(
                 nc.tensor.matmul_mx(
                     out=banks[j][:],
                     lhsT=w2_w[nb][:, cols].bitcast(FP8X4),
-                    lhsT_scale=w2_s[nb, first // 4][:, first % 4 * P : (first % 4 + 1) * P],
+                    lhsT_scale=w2_s[nb, first],
                     rhs=x_w[b][:].bitcast(FP8X4),
                     rhs_scale=x_s[b][:],
                     start=(b == 0),
@@ -308,18 +305,17 @@ def tile_list_dental_unet_skip_kernel(
             nc.vector.scalar_tensor_tensor(res[:], banks[j][:, ms], col(b2_cols, j), enc[j, half][:], ALU.add, ALU.max)
             nc.sync.dma_start(out_rows[j // 4, j % 4][:, ms], res[:])
 
-        cast_w2(0, 0, True)
-        cast_w2(0, 1, True)
-        cast_w2(1, 0, True)
+        for b in range(2):
+            cast_w2(w2_bf0[:, :, b, :], 0, b, 0, 4, True)
+        cast_w2(w2_bf1[0][:], 1, 0, 0, 4, True)
         for j in range(4):
             encode(j)
         for j in range(4):
             squash(j)
         make_x(0, 0, M)
+        cast_w2(w2_bf1[1][:], 1, 1, 0, 2, True)
         for j in range(3):
             pick_skip(j, picks, 2 * KB * j)
-        for j in range(2):
-            scale_skip(j, stage0, 2 * KB * j)
         for j in range(4, 8):
             encode(j)
         for j in range(4, 8):
@@ -328,13 +324,15 @@ def tile_list_dental_unet_skip_kernel(
         make_x_rest()
         for j in range(3, 6):
             pick_skip(j, picks, 2 * KB * (j + 1))
-        quantize_w2(0, 0)
+        quantize_w2(0, 0, 4, w2_bf0[:, 0:2].rearrange("p t b n -> p (t b n)"), late, KB)
         quantize_x(0)
         quantize_x(1)
-        quantize_w2(0, 1)
-        cast_w2(1, 1, False)
-        quantize_w2(1, 0)
-        quantize_w2(1, 1)
+        quantize_w2(0, 4, 8, w2_bf0[:, 2:4].rearrange("p t b n -> p (t b n)"), picks, 20 * KB)
+        cast_w2(w2_bf1[2][:], 1, 1, 2, 4, False)
+        for j in range(2):
+            scale_skip(j, late, 2 * KB * (j + 1))
+        for part, (c0, c1) in enumerate(((0, 4), (4, 6), (6, 8))):
+            quantize_w2(1, c0, c1, w2_bf1[part][:].rearrange("p t n -> p (t n)"), picks, 20 * KB + N + P * c0)
         pick_skip(6, late, 8 * KB)
         for j in range(8):
             project(j)

@@ -116,7 +116,7 @@ def tile_list_dental_unet_skip_kernel(
         nc.gpsimd.memset(warm[:], 0)
         warm_s = warm[:, N : N + N // 4].bitcast(U8)
         nc.vector.quantize_mx(out=warm[:, 0 : P // 4].bitcast(FP8X4), scales=warm_s[:, 0 : P // 4], in_=warm[:, N + N // 4 :].bitcast(BF16))
-        warm_lhs = stage0.tile([P, P], U32, name="warm_lhs", align_bytes=64, offset=8 * KB)
+        warm_lhs = stage0.tile([P, P], U32, name="warm_lhs", align_bytes=64, offset=10 * KB)
         nc.scalar.copy(warm_lhs[:], warm[:, 0:P])
         warm_acc = psum.tile([P, N], F32, name="acc", tag="bank")
         for step in range(4):
@@ -137,9 +137,11 @@ def tile_list_dental_unet_skip_kernel(
             w2_raw[nb, b] = pool.tile([P, 4, N], F32, name="w2_raw%d%d" % (nb, b), align_bytes=64, offset=offset)
             nc.sync.dma_start(w2_raw[nb, b][:], w2_rows[nb, b])
 
-        load_w2(0, 0, stage0, 0)
+        w2_first = [stage0.tile([P, 4, N // 2], F32, name="w2_first%d" % half, align_bytes=64, offset=(1 + 4 * half) * KB) for half in range(2)]
+        for half in range(2):
+            nc.sync.dma_start(w2_first[half][:], w2_rows[0, 0][:, :, half * N // 2 : (half + 1) * N // 2])
         load_w2(0, 1, stage0, 12 * KB)
-        scales_late = stage0.tile([P, 2, N], U8, name="scales_late", align_bytes=64, offset=9 * KB)
+        scales_late = stage0.tile([P, 2, N], U8, name="scales_late", align_bytes=64, offset=11 * KB)
         nc.vector.memset(scales_late[:].rearrange("p a n -> p (a n)").bitcast(I32), 0)
         move_rows(scales_late, slice(S + N, S + H))
 
@@ -166,10 +168,10 @@ def tile_list_dental_unet_skip_kernel(
         th = [after.tile([P, 4, M], F32, name="th0", align_bytes=64, offset=0), late.tile([P, 4, M], F32, name="th1", align_bytes=64, offset=0)]
         x_rows = picks.tile([P, 4, M - SPLIT], BF16, name="x_rows", align_bytes=64, offset=20 * KB)
         x_bf0 = stage1.tile([P, 4 * M], BF16, name="x_bf0", align_bytes=64, offset=9 * KB)
-        x_bf1 = late.tile([P, 4 * M], BF16, name="x_bf1", align_bytes=64, offset=8 * KB)
+        x_bf1 = late.tile([P, 4 * M], BF16, name="x_bf1", align_bytes=64, offset=18 * KB)
         x_bf = [x_bf0, x_bf1]
         x_w = [keep.tile([P, M], U32, name="x_w%d" % b, align_bytes=64) for b in range(2)]
-        w2_bf0 = keep.tile([P, 4, 2, N], BF16, name="w2_bf0", align_bytes=64)
+        w2_bf0 = late.tile([P, 4, 2, N], BF16, name="w2_bf0", align_bytes=64, offset=9 * KB)
         w2_bf1 = [
             keep.tile([P, 4, N], BF16, name="w2_bf10", align_bytes=64),
             keep.tile([P, 2, N], BF16, name="w2_bf11", align_bytes=64),
@@ -226,8 +228,8 @@ def tile_list_dental_unet_skip_kernel(
                 nc.scalar.activation(x_rows[:, t, :], th[1][:, t, SPLIT:M], ACT.Copy, scale=col(gain_cols, 4 + t))
             nc.scalar.copy(x_bf[1][:, 4 * SPLIT :].rearrange("p (m t) -> p m t", t=4), x_rows[:].rearrange("p t m -> p m t"))
 
-        def cast_w2(dst, nb, b, t0, t1, on_gpsimd):
-            src = w2_raw[nb, b][:].rearrange("p r (m t) -> p m t r", t=4)[:, :, t0:t1, :]
+        def cast_w2(dst, raw, t0, t1, on_gpsimd):
+            src = raw[:].rearrange("p r (m t) -> p m t r", t=4)[:, :, t0:t1, :]
             dst = dst.rearrange("p t (m r) -> p m t r", r=4)
             if on_gpsimd:
                 nc.gpsimd.tensor_scalar(dst, src, 1.0, 0.0, ALU.mult, ALU.add)
@@ -272,21 +274,33 @@ def tile_list_dental_unet_skip_kernel(
 
         halves = (slice(0, LAST), slice(LAST, M))
 
-        def finish_aside(j):
-            y = keep.tile([P, M], F32, name="y")
-            diff = keep.tile([P, M], F32, name="diff")
-            gap = keep.tile([P, M], F32, name="gap")
-            res = keep.tile([P, M], F32, name="res%d" % j)
-            nc.scalar.activation(y[:], banks[j][:], ACT.Identity, bias=col(b2_cols, j))
-            nc.gpsimd.tensor_tensor(diff[:], y[:], enc[j][:], ALU.subtract)
-            nc.scalar.activation(gap[:], diff[:], ACT.Relu)
-            nc.gpsimd.tensor_tensor(res[:], enc[j][:], gap[:], ALU.add)
-            return res
+        y = {}
+        diff = {}
+        gap = {}
+        done = {}
 
-        def finish(j):
-            res = keep.tile([P, M], F32, name="res%d" % j)
-            nc.vector.scalar_tensor_tensor(res[:], banks[j][:], col(b2_cols, j), enc[j][:], ALU.add, ALU.max)
-            nc.sync.dma_start(out_rows[j // 4, j % 4], res[:])
+        def subtract_aside(j, ms):
+            y[j] = keep.tile([P, ms.stop - ms.start], F32, name="y%d" % j)
+            nc.scalar.activation(y[j][:], banks[j][:, ms], ACT.Identity, bias=col(b2_cols, j))
+            diff[j] = keep.tile([P, ms.stop - ms.start], F32, name="diff%d" % j)
+            nc.gpsimd.tensor_tensor(diff[j][:], y[j][:], enc[j][:, ms], ALU.subtract)
+
+        def add_aside(j, ms):
+            gap[j] = keep.tile([P, ms.stop - ms.start], F32, name="gap%d" % j)
+            nc.scalar.activation(gap[j][:], diff[j][:], ACT.Relu)
+            done[j] = keep.tile([P, ms.stop - ms.start], F32, name="done%d" % j)
+            nc.gpsimd.tensor_tensor(done[j][:], enc[j][:, ms], gap[j][:], ALU.add)
+
+        def finish(j, ms):
+            res = keep.tile([P, ms.stop - ms.start], F32, name="res%d" % j)
+            nc.vector.scalar_tensor_tensor(res[:], banks[j][:, ms], col(b2_cols, j), enc[j][:, ms], ALU.add, ALU.max)
+            nc.sync.dma_start(out_rows[j // 4, j % 4][:, ms], res[:])
+
+        def pick_first_half(j, offset):
+            picked = stage1.tile([P, LAST], F32, name="g2_%d" % j, align_bytes=64, offset=offset)
+            nc.vector.tensor_copy(picked[:], h[j][:].indirect(pos2_sb[:, 0 : LAST // 16]))
+            enc[j, 0] = keep.tile([P, LAST], F32, name="enc%d_0" % j)
+            nc.scalar.activation(enc[j, 0][:], picked[:], ACT.Copy, scale=col(skip_cols, j))
 
         def spread_skip(j):
             wide = late.tile([P, LAST], F32, name="skip_wide", align_bytes=64, offset=6 * KB)
@@ -305,15 +319,16 @@ def tile_list_dental_unet_skip_kernel(
             nc.vector.scalar_tensor_tensor(res[:], banks[j][:, ms], col(b2_cols, j), enc[j, half][:], ALU.add, ALU.max)
             nc.sync.dma_start(out_rows[j // 4, j % 4][:, ms], res[:])
 
-        for b in range(2):
-            cast_w2(w2_bf0[:, :, b, :], 0, b, 0, 4, True)
-        cast_w2(w2_bf1[0][:], 1, 0, 0, 4, True)
+        for half in range(2):
+            cast_w2(w2_bf0[:, :, 0, half * N // 2 : (half + 1) * N // 2], w2_first[half], 0, 4, True)
+        cast_w2(w2_bf0[:, :, 1, :], w2_raw[0, 1], 0, 4, True)
+        cast_w2(w2_bf1[0][:], w2_raw[1, 0], 0, 4, True)
         for j in range(4):
             encode(j)
         for j in range(4):
             squash(j)
         make_x(0, 0, M)
-        cast_w2(w2_bf1[1][:], 1, 1, 0, 2, True)
+        cast_w2(w2_bf1[1][:], w2_raw[1, 1], 0, 2, True)
         for j in range(3):
             pick_skip(j, picks, 2 * KB * j)
         for j in range(4, 8):
@@ -328,23 +343,34 @@ def tile_list_dental_unet_skip_kernel(
         quantize_x(0)
         quantize_x(1)
         quantize_w2(0, 4, 8, w2_bf0[:, 2:4].rearrange("p t b n -> p (t b n)"), picks, 20 * KB)
-        cast_w2(w2_bf1[2][:], 1, 1, 2, 4, False)
+        cast_w2(w2_bf1[2][:], w2_raw[1, 1], 2, 4, False)
         for j in range(2):
             scale_skip(j, late, 2 * KB * (j + 1))
         for part, (c0, c1) in enumerate(((0, 4), (4, 6), (6, 8))):
             quantize_w2(1, c0, c1, w2_bf1[part][:].rearrange("p t n -> p (t n)"), picks, 20 * KB + N + P * c0)
-        pick_skip(6, late, 8 * KB)
+        pick_skip(6, late, 18 * KB)
         for j in range(8):
             project(j)
-        first = finish_aside(0)
-        for j in range(2, 6):
+        whole = slice(0, M)
+        aside = ((0, whole), (1, halves[0]))
+        for j, ms in aside:
+            subtract_aside(j, ms)
+        for j in range(2, 4):
             scale_skip(j, stage1, 17 * KB + 2 * KB * (j - 2))
+        add_aside(0, whole)
+        scale_skip(4, stage1, 21 * KB)
+        add_aside(1, halves[0])
+        scale_skip(5, stage1, 23 * KB)
         scale_skip(6, stage1, 0)
         wide = spread_skip(7)
-        nc.scalar.dma_start(out_rows[0, 0], first[:])
-        for j in range(1, 7):
-            finish(j)
-        for half in range(2):
-            pick_scaled(7, half, wide, stage1, 23 * KB + 4 * LAST * half)
+        finish(1, halves[1])
+        for j in range(2, 4):
+            finish(j, whole)
+        pick_first_half(7, 17 * KB)
+        for j, ms in aside:
+            nc.scalar.dma_start(out_rows[0, j][:, ms], done[j][:])
+        for j in range(4, 7):
+            finish(j, whole)
+        pick_scaled(7, 1, wide, stage1, 23 * KB)
         finish_half(7, 0)
         finish_half(7, 1)

@@ -19,7 +19,7 @@ ACT = mybir.ActivationFunctionType
 P = 128
 N = 512
 KB = 1024
-SPLIT = 168
+SPLIT = 136
 LAST = 256
 
 
@@ -158,11 +158,11 @@ def tile_list_dental_unet_skip_kernel(
         gain_cols = stage1.tile([P, 2, 8], F32, name="gain_cols", align_bytes=64, offset=8 * KB)
         skip_cols = stage1.tile([P, 2, 8], F32, name="skip_cols", align_bytes=64, offset=8 * KB + 64)
         b2_cols = stage1.tile([P, 2, 8], F32, name="b2_cols", align_bytes=64, offset=8 * KB + 128)
-        load_channels(gain_cols, gain)
         load_w2(1, 0, stage1, 9 * KB)
+        load_channels(gain_cols, gain)
+        load_w2(1, 1, stage1, 17 * KB)
         load_channels(skip_cols, skip)
         load_channels(b2_cols, b2)
-        load_w2(1, 1, stage1, 17 * KB)
         h = [keep.tile([P, S], F32, name="h%d" % j) for j in range(8)]
         g1 = [picks.tile([P, M], F32, name="g1_%d" % j, align_bytes=64, offset=2 * KB * j if j < 7 else 20 * KB) for j in range(8)]
         th = [after.tile([P, 4, M], F32, name="th0", align_bytes=64, offset=0), late.tile([P, 4, M], F32, name="th1", align_bytes=64, offset=0)]
@@ -202,7 +202,10 @@ def tile_list_dental_unet_skip_kernel(
             return acc
 
         def empty(j, c0, c1, acc):
-            nc.scalar.activation(h[j][:, c0:c1], acc, ACT.Identity, bias=col(b1_cols, j))
+            if (j, c1) == (0, S):
+                nc.vector.tensor_scalar(h[j][:, c0:c1], acc, col(b1_cols, j), None, ALU.add)
+            else:
+                nc.scalar.activation(h[j][:, c0:c1], acc, ACT.Identity, bias=col(b1_cols, j))
 
         def pick_coarse(j):
             nc.vector.tensor_copy(g1[j][:], h[j][:].indirect(pos1_sb[:]))
@@ -226,7 +229,10 @@ def tile_list_dental_unet_skip_kernel(
         def make_x_rest():
             for t in range(4):
                 nc.scalar.activation(x_rows[:, t, :], th[1][:, t, SPLIT:M], ACT.Copy, scale=col(gain_cols, 4 + t))
-            nc.scalar.copy(x_bf[1][:, 4 * SPLIT :].rearrange("p (m t) -> p m t", t=4), x_rows[:].rearrange("p t m -> p m t"))
+            nc.scalar.copy(
+                x_bf[1][:, 4 * SPLIT :].rearrange("p (c i t) -> p c t i", i=4, t=4),
+                x_rows[:].rearrange("p t (c i) -> p c t i", i=4),
+            )
 
         def cast_w2(dst, raw, t0, t1, on_gpsimd):
             src = raw[:].rearrange("p r (m t) -> p m t r", t=4)[:, :, t0:t1, :]
@@ -282,7 +288,7 @@ def tile_list_dental_unet_skip_kernel(
         def subtract_aside(j, ms):
             y[j] = keep.tile([P, ms.stop - ms.start], F32, name="y%d" % j)
             nc.scalar.activation(y[j][:], banks[j][:, ms], ACT.Identity, bias=col(b2_cols, j))
-            diff[j] = keep.tile([P, ms.stop - ms.start], F32, name="diff%d" % j)
+            diff[j] = picks.tile([P, ms.stop - ms.start], F32, name="diff%d" % j, align_bytes=64, offset=(22 + 2 * j) * KB)
             nc.gpsimd.tensor_tensor(diff[j][:], y[j][:], enc[j][:, ms], ALU.subtract)
 
         def add_aside(j, ms):

@@ -303,7 +303,7 @@ def tile_list_dental_unet_skip_kernel(
             nc.sync.dma_start(out_rows[j // 4, j % 4][:, ms], res[:])
 
         def pick_first_half(j, offset):
-            picked = stage1.tile([P, LAST], F32, name="g2_%d" % j, align_bytes=64, offset=offset)
+            picked = picks.tile([P, LAST], F32, name="g2_%d" % j, align_bytes=64, offset=offset)
             nc.vector.tensor_copy(picked[:], h[j][:].indirect(pos2_sb[:, 0 : LAST // 16]))
             enc[j, 0] = keep.tile([P, LAST], F32, name="enc%d_0" % j)
             nc.scalar.activation(enc[j, 0][:], picked[:], ACT.Copy, scale=col(skip_cols, j))
@@ -361,21 +361,20 @@ def tile_list_dental_unet_skip_kernel(
         aside = ((0, whole), (1, halves[0]))
         for j, ms in aside:
             subtract_aside(j, ms)
-        for j in range(2, 4):
+        for j in range(2, 5):
             scale_skip(j, stage1, 17 * KB + 2 * KB * (j - 2))
         add_aside(0, whole)
-        scale_skip(4, stage1, 21 * KB)
         add_aside(1, halves[0])
         scale_skip(5, stage1, 23 * KB)
         scale_skip(6, stage1, 0)
         wide = spread_skip(7)
         finish(1, halves[1])
-        for j in range(2, 4):
+        for j in range(2, 5):
             finish(j, whole)
-        pick_first_half(7, 17 * KB)
+        pick_first_half(7, 10 * KB)
         for j, ms in aside:
             nc.scalar.dma_start(out_rows[0, j][:, ms], done[j][:])
-        for j in range(4, 7):
+        for j in range(5, 7):
             finish(j, whole)
         pick_scaled(7, 1, wide, stage1, 23 * KB)
         finish_half(7, 0)

@@ -19,7 +19,7 @@ ACT = mybir.ActivationFunctionType
 P = 128
 N = 512
 KB = 1024
-SPLIT = 136
+SPLIT = 72
 LAST = 256
 
 
@@ -164,7 +164,7 @@ def tile_list_dental_unet_skip_kernel(
         load_channels(skip_cols, skip)
         load_channels(b2_cols, b2)
         h = [keep.tile([P, S], F32, name="h%d" % j) for j in range(8)]
-        g1 = [picks.tile([P, M], F32, name="g1_%d" % j, align_bytes=64, offset=2 * KB * j if j < 7 else 20 * KB) for j in range(8)]
+        g1 = [picks.tile([P, M], F32, name="g1_%d" % j, align_bytes=64, offset=2 * KB * j) for j in range(8)]
         th = [after.tile([P, 4, M], F32, name="th0", align_bytes=64, offset=0), late.tile([P, 4, M], F32, name="th1", align_bytes=64, offset=0)]
         x_rows = picks.tile([P, 4, M - SPLIT], BF16, name="x_rows", align_bytes=64, offset=20 * KB)
         x_bf0 = stage1.tile([P, 4 * M], BF16, name="x_bf0", align_bytes=64, offset=9 * KB)
@@ -226,9 +226,10 @@ def tile_list_dental_unet_skip_kernel(
                 ALU.mult,
             )
 
-        def make_x_rest():
-            for t in range(4):
-                nc.scalar.activation(x_rows[:, t, :], th[1][:, t, SPLIT:M], ACT.Copy, scale=col(gain_cols, 4 + t))
+        def scale_row(t):
+            nc.scalar.activation(x_rows[:, t, :], th[1][:, t, SPLIT:M], ACT.Copy, scale=col(gain_cols, 4 + t))
+
+        def interleave_rows():
             nc.scalar.copy(
                 x_bf[1][:, 4 * SPLIT :].rearrange("p (c i t) -> p c t i", i=4, t=4),
                 x_rows[:].rearrange("p t (c i) -> p c t i", i=4),
@@ -339,41 +340,43 @@ def tile_list_dental_unet_skip_kernel(
             pick_skip(j, picks, 2 * KB * j)
         for j in range(4, 8):
             encode(j)
-        for j in range(4, 8):
+        for j in range(4, 7):
             squash(j)
+        scale_row(0)
+        squash(7)
         make_x(1, 0, SPLIT)
-        make_x_rest()
+        for t in range(1, 4):
+            scale_row(t)
+        interleave_rows()
         for j in range(3, 6):
             pick_skip(j, picks, 2 * KB * (j + 1))
         quantize_w2(0, 0, 4, w2_bf0[:, 0:2].rearrange("p t b n -> p (t b n)"), late, KB)
         quantize_x(0)
+        quantize_w2(1, 4, 6, w2_bf1[1][:].rearrange("p t n -> p (t n)"), late, KB + N)
         quantize_x(1)
         quantize_w2(0, 4, 8, w2_bf0[:, 2:4].rearrange("p t b n -> p (t b n)"), picks, 20 * KB)
         cast_w2(w2_bf1[2][:], w2_raw[1, 1], 2, 4, False)
         for j in range(2):
             scale_skip(j, late, 2 * KB * (j + 1))
-        for part, (c0, c1) in enumerate(((0, 4), (4, 6), (6, 8))):
+        for part, c0, c1 in ((0, 0, 4), (2, 6, 8)):
             quantize_w2(1, c0, c1, w2_bf1[part][:].rearrange("p t n -> p (t n)"), picks, 20 * KB + N + P * c0)
         pick_skip(6, late, 18 * KB)
         for j in range(8):
             project(j)
         whole = slice(0, M)
-        aside = ((0, whole), (1, halves[0]))
+        aside = ((0, whole),)
         for j, ms in aside:
             subtract_aside(j, ms)
         for j in range(2, 5):
             scale_skip(j, stage1, 17 * KB + 2 * KB * (j - 2))
         add_aside(0, whole)
-        add_aside(1, halves[0])
         scale_skip(5, stage1, 23 * KB)
         scale_skip(6, stage1, 0)
         wide = spread_skip(7)
-        finish(1, halves[1])
-        for j in range(2, 5):
+        nc.scalar.dma_start(out_rows[0, 0], done[0][:])
+        for j in range(1, 5):
             finish(j, whole)
         pick_first_half(7, 10 * KB)
-        for j, ms in aside:
-            nc.scalar.dma_start(out_rows[0, j][:, ms], done[j][:])
         for j in range(5, 7):
             finish(j, whole)
         pick_scaled(7, 1, wide, stage1, 23 * KB)

@@ -19,7 +19,7 @@ ACT = mybir.ActivationFunctionType
 P = 128
 N = 512
 KB = 1024
-SPLIT = 72
+SPLIT = 128
 LAST = 256
 
 
@@ -164,8 +164,10 @@ def tile_list_dental_unet_skip_kernel(
         load_channels(skip_cols, skip)
         load_channels(b2_cols, b2)
         h = [keep.tile([P, S], F32, name="h%d" % j) for j in range(8)]
-        g1 = [picks.tile([P, M], F32, name="g1_%d" % j, align_bytes=64, offset=2 * KB * j) for j in range(8)]
-        th = [after.tile([P, 4, M], F32, name="th0", align_bytes=64, offset=0), late.tile([P, 4, M], F32, name="th1", align_bytes=64, offset=0)]
+        g1_pair = [picks.tile([P, 2, M], F32, name="g1_pair%d" % u, align_bytes=64, offset=4 * KB * u) for u in range(2)]
+        g1 = [g1_pair[j // 2][:, j % 2, :] for j in range(4)]
+        g1 += [picks.tile([P, M], F32, name="g1_%d" % j, align_bytes=64, offset=2 * KB * j)[:] for j in range(4, 8)]
+        th = [after.tile([P, 2, M, 2], F32, name="th0", align_bytes=64, offset=0), late.tile([P, 4, M], F32, name="th1", align_bytes=64, offset=0)]
         x_rows = picks.tile([P, 4, M - SPLIT], BF16, name="x_rows", align_bytes=64, offset=20 * KB)
         x_bf0 = stage1.tile([P, 4 * M], BF16, name="x_bf0", align_bytes=64, offset=9 * KB)
         x_bf1 = late.tile([P, 4 * M], BF16, name="x_bf1", align_bytes=64, offset=18 * KB)
@@ -208,7 +210,7 @@ def tile_list_dental_unet_skip_kernel(
                 nc.scalar.activation(h[j][:, c0:c1], acc, ACT.Identity, bias=col(b1_cols, j))
 
         def pick_coarse(j):
-            nc.vector.tensor_copy(g1[j][:], h[j][:].indirect(pos1_sb[:]))
+            nc.vector.tensor_copy(g1[j], h[j][:].indirect(pos1_sb[:]))
 
         def encode(j):
             for c0, c1 in pieces if j == 0 else ((0, N), (N, S)):
@@ -216,7 +218,18 @@ def tile_list_dental_unet_skip_kernel(
             pick_coarse(j)
 
         def squash(j):
-            nc.scalar.activation(th[j // 4][:, j % 4, :], g1[j][:], ACT.Tanh, bias=zero[:, 0:1])
+            nc.scalar.activation(th[j // 4][:, j % 4, :], g1[j], ACT.Tanh, bias=zero[:, 0:1])
+
+        def squash_pair(u):
+            nc.scalar.activation(th[0][:, u], g1_pair[u][:].rearrange("p e m -> p m e"), ACT.Tanh, bias=zero[:, 0:1])
+
+        def make_x_first():
+            nc.gpsimd.tensor_tensor(
+                x_bf[0][:].rearrange("p (m u e) -> p m u e", u=2, e=2),
+                th[0][:].rearrange("p u m e -> p m u e"),
+                gain_cols[:, 0:1, 0:4].to_broadcast([P, M, 4]).rearrange("p m (u e) -> p m u e", u=2),
+                ALU.mult,
+            )
 
         def make_x(b, m0, m1):
             nc.gpsimd.tensor_tensor(
@@ -332,9 +345,9 @@ def tile_list_dental_unet_skip_kernel(
         cast_w2(w2_bf1[0][:], w2_raw[1, 0], 0, 4, True)
         for j in range(4):
             encode(j)
-        for j in range(4):
-            squash(j)
-        make_x(0, 0, M)
+        for u in range(2):
+            squash_pair(u)
+        make_x_first()
         cast_w2(w2_bf1[1][:], w2_raw[1, 1], 0, 2, True)
         for j in range(3):
             pick_skip(j, picks, 2 * KB * j)

@@ -19,7 +19,7 @@ ACT = mybir.ActivationFunctionType
 P = 128
 N = 512
 KB = 1024
-SPLIT = 128
+SPLIT = 72
 LAST = 256
 
 
@@ -74,10 +74,10 @@ def tile_list_dental_unet_skip_kernel(
         load_scale_rows(w1s_raw, w1_scales)
         tab_w0 = stage0.tile([P, T], I32, name="tab_w0", align_bytes=64, offset=4 * KB)
         nc.sync.dma_start(tab_w0[:], tab_words[0].rearrange("p n t -> p (n t)").bitcast(I32))
-        nc.sync.dma_start(pos1_sb[:], pos1)
-        nc.sync.dma_start(pos2_sb[:], pos2)
         tab_w1 = stage1.tile([P, T], I32, name="tab_w1", align_bytes=64, offset=4 * KB)
         nc.sync.dma_start(tab_w1[:], tab_words[1].rearrange("p n t -> p (n t)").bitcast(I32))
+        nc.sync.dma_start(pos1_sb[:], pos1)
+        nc.sync.dma_start(pos2_sb[:], pos2)
         load_w1_words(0, keep.tile([P, 2, 256], I32, name="w1w_raw0", align_bytes=64))
 
         zero_in = keep.tile([P, 8], F32, name="zero_in")
@@ -140,7 +140,9 @@ def tile_list_dental_unet_skip_kernel(
         w2_first = [stage0.tile([P, 4, N // 2], F32, name="w2_first%d" % half, align_bytes=64, offset=(1 + 4 * half) * KB) for half in range(2)]
         for half in range(2):
             nc.sync.dma_start(w2_first[half][:], w2_rows[0, 0][:, :, half * N // 2 : (half + 1) * N // 2])
-        load_w2(0, 1, stage0, 12 * KB)
+        w2_second = [stage0.tile([P, 4, N // 2], F32, name="w2_second%d" % half, align_bytes=64, offset=(12 + 4 * half) * KB) for half in range(2)]
+        for half in range(2):
+            nc.sync.dma_start(w2_second[half][:], w2_rows[0, 1][:, :, half * N // 2 : (half + 1) * N // 2])
         scales_late = stage0.tile([P, 2, N], U8, name="scales_late", align_bytes=64, offset=11 * KB)
         nc.vector.memset(scales_late[:].rearrange("p a n -> p (a n)").bitcast(I32), 0)
         move_rows(scales_late, slice(S + N, S + H))
@@ -341,7 +343,8 @@ def tile_list_dental_unet_skip_kernel(
 
         for half in range(2):
             cast_w2(w2_bf0[:, :, 0, half * N // 2 : (half + 1) * N // 2], w2_first[half], 0, 4, True)
-        cast_w2(w2_bf0[:, :, 1, :], w2_raw[0, 1], 0, 4, True)
+        for half in range(2):
+            cast_w2(w2_bf0[:, :, 1, half * N // 2 : (half + 1) * N // 2], w2_second[half], 0, 4, True)
         cast_w2(w2_bf1[0][:], w2_raw[1, 0], 0, 4, True)
         for j in range(4):
             encode(j)

@@ -20,6 +20,7 @@ P = 128
 N = 512
 KB = 1024
 SPLIT = 72
+EARLY = 2
 LAST = 256
 
 
@@ -74,7 +75,7 @@ def tile_list_dental_unet_skip_kernel(
         load_scale_rows(w1s_raw, w1_scales)
         tab_w0 = stage0.tile([P, T], I32, name="tab_w0", align_bytes=64, offset=4 * KB)
         nc.sync.dma_start(tab_w0[:], tab_words[0].rearrange("p n t -> p (n t)").bitcast(I32))
-        tab_w1 = stage1.tile([P, T], I32, name="tab_w1", align_bytes=64, offset=4 * KB)
+        tab_w1 = stage1.tile([P, T], I32, name="tab_w1", align_bytes=64, offset=8 * KB)
         nc.sync.dma_start(tab_w1[:], tab_words[1].rearrange("p n t -> p (n t)").bitcast(I32))
         nc.sync.dma_start(pos1_sb[:], pos1)
         nc.sync.dma_start(pos2_sb[:], pos2)
@@ -85,7 +86,7 @@ def tile_list_dental_unet_skip_kernel(
         nc.vector.memset(zero_in[:], 0.0)
         nc.scalar.activation(zero[:, 0:1], zero_in[:, 0:1], ACT.Tanh)
 
-        scales = keep.tile([P, 2, S + N], U8, name="scales", align_bytes=64)
+        scales = keep.tile([P, 2, S + EARLY * P], U8, name="scales", align_bytes=64)
         nc.vector.memset(scales[:].rearrange("p a n -> p (a n)").bitcast(I32), 0)
 
         picked_s = keep.tile([P, S], U8, name="picked_s", align_bytes=64)
@@ -101,7 +102,7 @@ def tile_list_dental_unet_skip_kernel(
             for q in (0, 2, 1, 3):
                 nc.sync.dma_start(tile[32 * q : 32 * q + 4, :, :].bitcast(I32), rows[8 * q : 8 * q + 8, cols].bitcast(I32))
 
-        move_rows(scales, slice(0, S + N))
+        move_rows(scales, slice(0, S + EARLY * P))
         b1_cols = late.tile([P, 2, 8], F32, name="b1_cols", align_bytes=64, offset=7 * KB)
         load_channels(b1_cols, b1)
         load_w1_words(1, late.tile([P, 2, 256], I32, name="w1w_raw1", align_bytes=64, offset=7 * KB + 64))
@@ -137,15 +138,18 @@ def tile_list_dental_unet_skip_kernel(
             w2_raw[nb, b] = pool.tile([P, 4, N], F32, name="w2_raw%d%d" % (nb, b), align_bytes=64, offset=offset)
             nc.sync.dma_start(w2_raw[nb, b][:], w2_rows[nb, b])
 
-        w2_first = [stage0.tile([P, 4, N // 2], F32, name="w2_first%d" % half, align_bytes=64, offset=(1 + 4 * half) * KB) for half in range(2)]
-        for half in range(2):
-            nc.sync.dma_start(w2_first[half][:], w2_rows[0, 0][:, :, half * N // 2 : (half + 1) * N // 2])
-        w2_second = [stage0.tile([P, 4, N // 2], F32, name="w2_second%d" % half, align_bytes=64, offset=(12 + 4 * half) * KB) for half in range(2)]
-        for half in range(2):
-            nc.sync.dma_start(w2_second[half][:], w2_rows[0, 1][:, :, half * N // 2 : (half + 1) * N // 2])
-        scales_late = stage0.tile([P, 2, N], U8, name="scales_late", align_bytes=64, offset=11 * KB)
+        w2_half = {}
+
+        def load_w2_half(b, half, pool, offset):
+            w2_half[b, half] = pool.tile([P, 4, N // 2], F32, name="w2_half%d%d" % (b, half), align_bytes=64, offset=offset)
+            nc.sync.dma_start(w2_half[b, half][:], w2_rows[0, b][:, :, half * N // 2 : (half + 1) * N // 2])
+
+        load_w2_half(0, 0, stage0, KB)
+        scales_late = stage0.tile([P, 2, H - EARLY * P], U8, name="scales_late", align_bytes=64, offset=11 * KB)
         nc.vector.memset(scales_late[:].rearrange("p a n -> p (a n)").bitcast(I32), 0)
-        move_rows(scales_late, slice(S + N, S + H))
+        move_rows(scales_late, slice(S + EARLY * P, S + H))
+        for piece in range(1, 4):
+            load_w2_half(piece // 2, piece % 2, stage1, 4 * KB * piece + 64)
 
         v_w1 = [keep.tile([P, N], I32, name="v_w1_%d" % half, align_bytes=64) for half in range(2)]
         pieces = ((0, 512), (512, 768), (768, 1024))
@@ -157,12 +161,12 @@ def tile_list_dental_unet_skip_kernel(
 
         order_w1_words(nc.vector.tensor_copy, keep.tile([P, 2, 256], I32, name="w1w_last", align_bytes=64), 1, 0, 4)
 
-        gain_cols = stage1.tile([P, 2, 8], F32, name="gain_cols", align_bytes=64, offset=8 * KB)
-        skip_cols = stage1.tile([P, 2, 8], F32, name="skip_cols", align_bytes=64, offset=8 * KB + 64)
-        b2_cols = stage1.tile([P, 2, 8], F32, name="b2_cols", align_bytes=64, offset=8 * KB + 128)
-        load_w2(1, 0, stage1, 9 * KB)
+        gain_cols = stage1.tile([P, 2, 8], F32, name="gain_cols", align_bytes=64, offset=16 * KB + 64)
+        skip_cols = stage1.tile([P, 2, 8], F32, name="skip_cols", align_bytes=64, offset=16 * KB + 128)
+        b2_cols = stage1.tile([P, 2, 8], F32, name="b2_cols", align_bytes=64, offset=16 * KB + 192)
+        load_w2(1, 0, stage1, 17 * KB)
         load_channels(gain_cols, gain)
-        load_w2(1, 1, stage1, 17 * KB)
+        load_w2(1, 1, stage0, 0)
         load_channels(skip_cols, skip)
         load_channels(b2_cols, b2)
         h = [keep.tile([P, S], F32, name="h%d" % j) for j in range(8)]
@@ -171,7 +175,7 @@ def tile_list_dental_unet_skip_kernel(
         g1 += [picks.tile([P, M], F32, name="g1_%d" % j, align_bytes=64, offset=2 * KB * j)[:] for j in range(4, 8)]
         th = [after.tile([P, 2, M, 2], F32, name="th0", align_bytes=64, offset=0), late.tile([P, 4, M], F32, name="th1", align_bytes=64, offset=0)]
         x_rows = picks.tile([P, 4, M - SPLIT], BF16, name="x_rows", align_bytes=64, offset=20 * KB)
-        x_bf0 = stage1.tile([P, 4 * M], BF16, name="x_bf0", align_bytes=64, offset=9 * KB)
+        x_bf0 = stage1.tile([P, 4 * M], BF16, name="x_bf0", align_bytes=64, offset=17 * KB)
         x_bf1 = late.tile([P, 4 * M], BF16, name="x_bf1", align_bytes=64, offset=18 * KB)
         x_bf = [x_bf0, x_bf1]
         x_w = [keep.tile([P, M], U32, name="x_w%d" % b, align_bytes=64) for b in range(2)]
@@ -197,7 +201,7 @@ def tile_list_dental_unet_skip_kernel(
                 nc.tensor.matmul_mx(
                     out=acc,
                     lhsT=w1w[j][a].bitcast(FP4X4),
-                    lhsT_scale=scales[:, a, S + P * j : S + P * (j + 1)] if j < 4 else scales_late[:, a, P * (j - 4) : P * (j - 3)],
+                    lhsT_scale=scales[:, a, S + P * j : S + P * (j + 1)] if j < EARLY else scales_late[:, a, P * (j - EARLY) : P * (j - EARLY + 1)],
                     rhs=words.bitcast(FP8X4),
                     rhs_scale=scales[:, a, cols],
                     start=(a == 0),
@@ -341,10 +345,9 @@ def tile_list_dental_unet_skip_kernel(
             nc.vector.scalar_tensor_tensor(res[:], banks[j][:, ms], col(b2_cols, j), enc[j, half][:], ALU.add, ALU.max)
             nc.sync.dma_start(out_rows[j // 4, j % 4][:, ms], res[:])
 
-        for half in range(2):
-            cast_w2(w2_bf0[:, :, 0, half * N // 2 : (half + 1) * N // 2], w2_first[half], 0, 4, True)
-        for half in range(2):
-            cast_w2(w2_bf0[:, :, 1, half * N // 2 : (half + 1) * N // 2], w2_second[half], 0, 4, True)
+        for b in range(2):
+            for half in range(2):
+                cast_w2(w2_bf0[:, :, b, half * N // 2 : (half + 1) * N // 2], w2_half[b, half], 0, 4, True)
         cast_w2(w2_bf1[0][:], w2_raw[1, 0], 0, 4, True)
         for j in range(4):
             encode(j)
@@ -384,9 +387,9 @@ def tile_list_dental_unet_skip_kernel(
         for j, ms in aside:
             subtract_aside(j, ms)
         for j in range(2, 5):
-            scale_skip(j, stage1, 17 * KB + 2 * KB * (j - 2))
+            scale_skip(j, stage0, 2 * KB * (j - 2))
         add_aside(0, whole)
-        scale_skip(5, stage1, 23 * KB)
+        scale_skip(5, stage0, 6 * KB)
         scale_skip(6, stage1, 0)
         wide = spread_skip(7)
         nc.scalar.dma_start(out_rows[0, 0], done[0][:])
@@ -395,6 +398,6 @@ def tile_list_dental_unet_skip_kernel(
         pick_first_half(7, 10 * KB)
         for j in range(5, 7):
             finish(j, whole)
-        pick_scaled(7, 1, wide, stage1, 23 * KB)
+        pick_scaled(7, 1, wide, stage0, 6 * KB)
         finish_half(7, 0)
         finish_half(7, 1)

from contextlib import ExitStack

import concourse.mybir as mybir

K, H, T, S, M = 1024, 1024, 4096, 1024, 512
FLOPS = 2 * K * H * S + 2 * H * H * M

F32 = mybir.dt.float32
BF16 = mybir.dt.bfloat16
I32 = mybir.dt.int32
U32 = mybir.dt.uint32
U16 = mybir.dt.uint16
U8 = mybir.dt.uint8
FP8X4 = mybir.dt.float8_e4m3fn_x4
FP4X4 = mybir.dt.float4_e2m1fn_x4
ALU = mybir.AluOpType
ACT = mybir.ActivationFunctionType

P = 128
N = 512
KB = 1024
SPLIT = 72
EARLY = 2
LAST = 256


def tile_list_dental_unet_skip_kernel(
    tc, tab_words, tab_scales, offs, w1_words, w1_scales, b1, pos1, gain, w2, b2, pos2, skip, out
):
    nc = tc.nc
    with ExitStack() as ctx:
        keep = ctx.enter_context(tc.tile_pool(name="keep", bufs=1))
        stage0 = ctx.enter_context(tc.tile_pool(name="stage0", bufs=1))
        stage1 = ctx.enter_context(tc.tile_pool(name="stage1", bufs=1))
        after = ctx.enter_context(tc.tile_pool(name="after", bufs=1))
        picks = ctx.enter_context(tc.tile_pool(name="picks", bufs=1))
        late = ctx.enter_context(tc.tile_pool(name="late", bufs=1))
        psum = ctx.enter_context(tc.psum_pool(name="psum", bufs=8))

        offs_sb = keep.tile([P, S // 16], U16, name="offs_sb")
        pos1_sb = keep.tile([P, M // 16], U16, name="pos1_sb")
        pos2_sb = keep.tile([P, M // 16], U16, name="pos2_sb")

        def load_channels(tile, vec):
            nc.sync.dma_start(tile[:, :, 0:4], vec.rearrange("(b p t) -> p b t", b=2, t=4))

        def col(cols, j):
            return cols[:, j // 4, j % 4 : j % 4 + 1]

        def load_scale_rows(tile, scales):
            nc.sync.dma_start(tile[0:32, :].bitcast(I32), scales.rearrange("a q n -> q a n").bitcast(I32))
            nc.vector.memset(tile[32:64, :].bitcast(I32), 0)
            nc.vector.memset(tile[64:128, :].bitcast(I32), 0)

        w1w_raw = {}
        w1w = {}

        def load_w1_words(b, tile):
            w1w_raw[b] = tile
            words = w1_words.rearrange("a p n -> p a n").bitcast(I32)
            nc.sync.dma_start(w1w_raw[b][:], words[:, :, 256 * b : 256 * (b + 1)])

        def order_w1_words(copy, tile, b, t0, t1):
            copy(
                tile[:].bitcast(U16).rearrange("p a (t m) -> p a t m", m=P),
                w1w_raw[b][:].bitcast(U16).rearrange("p a (m t) -> p a t m", t=4)[:, :, t0:t1],
            )
            for t in range(t0, t1):
                w1w[4 * b + t] = [tile[:, a, 64 * (t - t0) : 64 * (t - t0 + 1)] for a in range(2)]

        nc.sync.dma_start(offs_sb[:], offs)
        tab_s = keep.tile([P, T], U8, name="tab_s", align_bytes=64)
        load_scale_rows(tab_s, tab_scales)
        w1s_raw = late.tile([P, H], U8, name="w1s_raw", align_bytes=64, offset=7 * KB)
        load_scale_rows(w1s_raw, w1_scales)
        tab_w0 = stage0.tile([P, T], I32, name="tab_w0", align_bytes=64, offset=4 * KB)
        nc.sync.dma_start(tab_w0[:], tab_words[0].rearrange("p n t -> p (n t)").bitcast(I32))
        tab_w1 = stage1.tile([P, T], I32, name="tab_w1", align_bytes=64, offset=8 * KB)
        nc.sync.dma_start(tab_w1[:], tab_words[1].rearrange("p n t -> p (n t)").bitcast(I32))
        nc.sync.dma_start(pos1_sb[:], pos1)
        nc.sync.dma_start(pos2_sb[:], pos2)
        load_w1_words(0, keep.tile([P, 2, 256], I32, name="w1w_raw0", align_bytes=64))

        zero_in = keep.tile([P, 8], F32, name="zero_in")
        zero = keep.tile([P, 8], F32, name="zero")
        nc.vector.memset(zero_in[:], 0.0)
        nc.scalar.activation(zero[:, 0:1], zero_in[:, 0:1], ACT.Tanh)

        scales = keep.tile([P, 2, S + EARLY * P], U8, name="scales", align_bytes=64)
        nc.vector.memset(scales[:].rearrange("p a n -> p (a n)").bitcast(I32), 0)

        picked_s = keep.tile([P, S], U8, name="picked_s", align_bytes=64)
        nc.vector.tensor_copy(picked_s[:], tab_s[:].indirect(offs_sb[:]))
        rows = keep.tile([P, S + H], U8, name="rows", align_bytes=64)
        nc.vector.tensor_copy(rows[:, 0:S].bitcast(I32), picked_s[:].bitcast(I32))
        nc.vector.tensor_copy(
            rows[:, S : S + H].rearrange("p (c t m) -> p c t m", c=2, t=4),
            w1s_raw[:].rearrange("p (c m t) -> p c t m", c=2, t=4),
        )

        def move_rows(tile, cols):
            for q in (0, 2, 1, 3):
                nc.sync.dma_start(tile[32 * q : 32 * q + 4, :, :].bitcast(I32), rows[8 * q : 8 * q + 8, cols].bitcast(I32))

        move_rows(scales, slice(0, S + EARLY * P))
        b1_cols = late.tile([P, 2, 8], F32, name="b1_cols", align_bytes=64, offset=7 * KB)
        load_channels(b1_cols, b1)
        load_w1_words(1, late.tile([P, 2, 256], I32, name="w1w_raw1", align_bytes=64, offset=7 * KB + 64))

        order_w1_words(nc.scalar.copy, keep.tile([P, 2, 64], I32, name="w1w_tile0", align_bytes=64), 0, 0, 1)
        order_w1_words(nc.scalar.copy, after.tile([P, 2, 192], I32, name="w1w_tiles123", align_bytes=64, offset=0), 0, 1, 4)

        v_w0 = keep.tile([P, S], I32, name="v_w0", align_bytes=64)
        nc.vector.tensor_copy(v_w0[:].bitcast(U32), tab_w0[:].bitcast(U32).indirect(offs_sb[:]))

        warm = keep.tile([P, N + N // 4 + P // 2], U32, name="warm", align_bytes=64)
        nc.gpsimd.memset(warm[:], 0)
        warm_s = warm[:, N : N + N // 4].bitcast(U8)
        nc.vector.quantize_mx(out=warm[:, 0 : P // 4].bitcast(FP8X4), scales=warm_s[:, 0 : P // 4], in_=warm[:, N + N // 4 :].bitcast(BF16))
        warm_lhs = stage0.tile([P, P], U32, name="warm_lhs", align_bytes=64, offset=10 * KB)
        nc.scalar.copy(warm_lhs[:], warm[:, 0:P])
        warm_acc = psum.tile([P, N], F32, name="acc", tag="bank")
        for step in range(4):
            nc.tensor.matmul_mx(
                out=warm_acc[:],
                lhsT=warm_lhs[:].bitcast(FP8X4),
                lhsT_scale=warm_s[:, 0:P],
                rhs=warm[:, 0:N].bitcast(FP8X4),
                rhs_scale=warm_s[:],
                start=True,
                stop=True,
            )

        w2_rows = w2.rearrange("(b p r) (nb n) -> nb b p r n", b=2, r=4, nb=2)
        w2_raw = {}

        def load_w2(nb, b, pool, offset):
            w2_raw[nb, b] = pool.tile([P, 4, N], F32, name="w2_raw%d%d" % (nb, b), align_bytes=64, offset=offset)
            nc.sync.dma_start(w2_raw[nb, b][:], w2_rows[nb, b])

        w2_half = {}

        def load_w2_half(b, half, pool, offset):
            w2_half[b, half] = pool.tile([P, 4, N // 2], F32, name="w2_half%d%d" % (b, half), align_bytes=64, offset=offset)
            nc.sync.dma_start(w2_half[b, half][:], w2_rows[0, b][:, :, half * N // 2 : (half + 1) * N // 2])

        load_w2_half(0, 0, stage0, KB)
        scales_late = stage0.tile([P, 2, H - EARLY * P], U8, name="scales_late", align_bytes=64, offset=11 * KB)
        nc.vector.memset(scales_late[:].rearrange("p a n -> p (a n)").bitcast(I32), 0)
        move_rows(scales_late, slice(S + EARLY * P, S + H))
        for piece in range(1, 4):
            load_w2_half(piece // 2, piece % 2, stage1, 4 * KB * piece + 64)

        v_w1 = [keep.tile([P, N], I32, name="v_w1_%d" % half, align_bytes=64) for half in range(2)]
        pieces = ((0, 512), (512, 768), (768, 1024))
        for c0, c1 in pieces:
            nc.vector.tensor_copy(
                v_w1[c0 // N][:, c0 % N : c0 % N + c1 - c0].bitcast(U32),
                tab_w1[:].bitcast(U32).indirect(offs_sb[:, c0 // 16 : c1 // 16]),
            )

        order_w1_words(nc.vector.tensor_copy, keep.tile([P, 2, 256], I32, name="w1w_last", align_bytes=64), 1, 0, 4)

        gain_cols = stage1.tile([P, 2, 8], F32, name="gain_cols", align_bytes=64, offset=16 * KB + 64)
        skip_cols = stage1.tile([P, 2, 8], F32, name="skip_cols", align_bytes=64, offset=16 * KB + 128)
        b2_cols = stage1.tile([P, 2, 8], F32, name="b2_cols", align_bytes=64, offset=16 * KB + 192)
        load_w2(1, 0, stage1, 17 * KB)
        load_channels(gain_cols, gain)
        load_w2(1, 1, stage0, 0)
        load_channels(skip_cols, skip)
        load_channels(b2_cols, b2)
        h = [keep.tile([P, S], F32, name="h%d" % j) for j in range(8)]
        g1_pair = [picks.tile([P, 2, M], F32, name="g1_pair%d" % u, align_bytes=64, offset=4 * KB * u) for u in range(2)]
        g1 = [g1_pair[j // 2][:, j % 2, :] for j in range(4)]
        g1 += [picks.tile([P, M], F32, name="g1_%d" % j, align_bytes=64, offset=2 * KB * j)[:] for j in range(4, 8)]
        th = [after.tile([P, 2, M, 2], F32, name="th0", align_bytes=64, offset=0), late.tile([P, 4, M], F32, name="th1", align_bytes=64, offset=0)]
        x_rows = picks.tile([P, 4, M - SPLIT], BF16, name="x_rows", align_bytes=64, offset=20 * KB)
        x_bf0 = stage1.tile([P, 4 * M], BF16, name="x_bf0", align_bytes=64, offset=17 * KB)
        x_bf1 = late.tile([P, 4 * M], BF16, name="x_bf1", align_bytes=64, offset=18 * KB)
        x_bf = [x_bf0, x_bf1]
        x_w = [keep.tile([P, M], U32, name="x_w%d" % b, align_bytes=64) for b in range(2)]
        w2_bf0 = late.tile([P, 4, 2, N], BF16, name="w2_bf0", align_bytes=64, offset=9 * KB)
        w2_bf1 = [
            keep.tile([P, 4, N], BF16, name="w2_bf10", align_bytes=64),
            keep.tile([P, 2, N], BF16, name="w2_bf11", align_bytes=64),
            picks.tile([P, 2, N], BF16, name="w2_bf12", align_bytes=64, offset=22 * KB),
        ]
        w2_w = [keep.tile([P, 2 * N], U32, name="w2_w%d" % nb, align_bytes=64) for nb in range(2)]
        g2 = {}
        enc = {}
        x_s = {}
        w2_s = {}
        banks = {}

        def multiply(j, c0, c1):
            bank = psum.tile([P, N], F32, name="acc", tag="bank")
            acc = bank[:, 0 : c1 - c0]
            cols = slice(c0, c1)
            for a in range(2):
                words = v_w0[:, cols] if a == 0 else v_w1[c0 // N][:, c0 % N : c0 % N + c1 - c0]
                nc.tensor.matmul_mx(
                    out=acc,
                    lhsT=w1w[j][a].bitcast(FP4X4),
                    lhsT_scale=scales[:, a, S + P * j : S + P * (j + 1)] if j < EARLY else scales_late[:, a, P * (j - EARLY) : P * (j - EARLY + 1)],
                    rhs=words.bitcast(FP8X4),
                    rhs_scale=scales[:, a, cols],
                    start=(a == 0),
                    stop=(a == 1),
                )
            return acc

        def empty(j, c0, c1, acc):
            if (j, c1) == (0, S):
                nc.vector.tensor_scalar(h[j][:, c0:c1], acc, col(b1_cols, j), None, ALU.add)
            else:
                nc.scalar.activation(h[j][:, c0:c1], acc, ACT.Identity, bias=col(b1_cols, j))

        def pick_coarse(j):
            nc.vector.tensor_copy(g1[j], h[j][:].indirect(pos1_sb[:]))

        def encode(j):
            for c0, c1 in pieces if j == 0 else ((0, N), (N, S)):
                empty(j, c0, c1, multiply(j, c0, c1))
            pick_coarse(j)

        def squash(j):
            nc.scalar.activation(th[j // 4][:, j % 4, :], g1[j], ACT.Tanh, bias=zero[:, 0:1])

        def squash_pair(u):
            nc.scalar.activation(th[0][:, u], g1_pair[u][:].rearrange("p e m -> p m e"), ACT.Tanh, bias=zero[:, 0:1])

        def make_x_first():
            nc.gpsimd.tensor_tensor(
                x_bf[0][:].rearrange("p (m u e) -> p m u e", u=2, e=2),
                th[0][:].rearrange("p u m e -> p m u e"),
                gain_cols[:, 0:1, 0:4].to_broadcast([P, M, 4]).rearrange("p m (u e) -> p m u e", u=2),
                ALU.mult,
            )

        def make_x(b, m0, m1):
            nc.gpsimd.tensor_tensor(
                x_bf[b][:, 4 * m0 : 4 * m1].rearrange("p (m t) -> p m t", t=4),
                th[b][:, :, m0:m1].rearrange("p t m -> p m t"),
                gain_cols[:, b : b + 1, 0:4].to_broadcast([P, m1 - m0, 4]),
                ALU.mult,
            )

        def scale_row(t):
            nc.scalar.activation(x_rows[:, t, :], th[1][:, t, SPLIT:M], ACT.Copy, scale=col(gain_cols, 4 + t))

        def interleave_rows():
            nc.scalar.copy(
                x_bf[1][:, 4 * SPLIT :].rearrange("p (c i t) -> p c t i", i=4, t=4),
                x_rows[:].rearrange("p t (c i) -> p c t i", i=4),
            )

        def cast_w2(dst, raw, t0, t1, on_gpsimd):
            src = raw[:].rearrange("p r (m t) -> p m t r", t=4)[:, :, t0:t1, :]
            dst = dst.rearrange("p t (m r) -> p m t r", r=4)
            if on_gpsimd:
                nc.gpsimd.tensor_scalar(dst, src, 1.0, 0.0, ALU.mult, ALU.add)
            else:
                nc.scalar.copy(dst.rearrange("p m t r -> p m r t"), src.rearrange("p m t r -> p m r t"))

        def pick_skip(j, pool, offset):
            g2[j] = pool.tile([P, M], F32, name="g2_%d" % j, align_bytes=64, offset=offset)
            nc.vector.tensor_copy(g2[j][:], h[j][:].indirect(pos2_sb[:]))

        def scale_skip(j, pool, offset):
            enc[j] = pool.tile([P, M], F32, name="enc%d" % j, align_bytes=64, offset=offset)
            nc.scalar.activation(enc[j][:], g2[j][:], ACT.Copy, scale=col(skip_cols, j))

        def quantize_x(b):
            x_s[b] = late.tile([P, M], U8, name="x_s%d" % b, align_bytes=64, offset=M * b)
            nc.vector.quantize_mx(out=x_w[b][:].bitcast(FP8X4), scales=x_s[b][:], in_=x_bf[b][:])

        def quantize_w2(nb, c0, c1, rows_bf, pool, offset):
            plane = pool.tile([P, (c1 - c0) * P], U8, name="w2_s%d%d" % (nb, c0), align_bytes=64, offset=offset)
            nc.vector.quantize_mx(out=w2_w[nb][:, c0 * P : c1 * P].bitcast(FP8X4), scales=plane[:], in_=rows_bf)
            for c in range(c0, c1):
                w2_s[nb, c] = plane[:, (c - c0) * P : (c - c0 + 1) * P]

        def project(j):
            nb, t = divmod(j, 4)
            banks[j] = psum.tile([P, N], F32, name="acc", tag="bank")
            for b in range(2):
                first = 2 * t + b if nb == 0 else 4 * b + t
                cols = slice(first * P, (first + 1) * P)
                nc.tensor.matmul_mx(
                    out=banks[j][:],
                    lhsT=w2_w[nb][:, cols].bitcast(FP8X4),
                    lhsT_scale=w2_s[nb, first],
                    rhs=x_w[b][:].bitcast(FP8X4),
                    rhs_scale=x_s[b][:],
                    start=(b == 0),
                    stop=(b == 1),
                )

        out_rows = out.rearrange("(b p t) m -> b t p m", b=2, t=4)

        halves = (slice(0, LAST), slice(LAST, M))

        y = {}
        diff = {}
        gap = {}
        done = {}

        def subtract_aside(j, ms):
            y[j] = keep.tile([P, ms.stop - ms.start], F32, name="y%d" % j)
            nc.scalar.activation(y[j][:], banks[j][:, ms], ACT.Identity, bias=col(b2_cols, j))
            diff[j] = picks.tile([P, ms.stop - ms.start], F32, name="diff%d" % j, align_bytes=64, offset=(22 + 2 * j) * KB)
            nc.gpsimd.tensor_tensor(diff[j][:], y[j][:], enc[j][:, ms], ALU.subtract)

        def add_aside(j, ms):
            gap[j] = keep.tile([P, ms.stop - ms.start], F32, name="gap%d" % j)
            nc.scalar.activation(gap[j][:], diff[j][:], ACT.Relu)
            done[j] = keep.tile([P, ms.stop - ms.start], F32, name="done%d" % j)
            nc.gpsimd.tensor_tensor(done[j][:], enc[j][:, ms], gap[j][:], ALU.add)

        def finish(j, ms):
            res = keep.tile([P, ms.stop - ms.start], F32, name="res%d" % j)
            nc.vector.scalar_tensor_tensor(res[:], banks[j][:, ms], col(b2_cols, j), enc[j][:, ms], ALU.add, ALU.max)
            nc.sync.dma_start(out_rows[j // 4, j % 4][:, ms], res[:])

        def pick_first_half(j, offset):
            picked = picks.tile([P, LAST], F32, name="g2_%d" % j, align_bytes=64, offset=offset)
            nc.vector.tensor_copy(picked[:], h[j][:].indirect(pos2_sb[:, 0 : LAST // 16]))
            enc[j, 0] = keep.tile([P, LAST], F32, name="enc%d_0" % j)
            nc.scalar.activation(enc[j, 0][:], picked[:], ACT.Copy, scale=col(skip_cols, j))

        def spread_skip(j):
            wide = late.tile([P, LAST], F32, name="skip_wide", align_bytes=64, offset=6 * KB)
            nc.scalar.copy(wide[:], col(skip_cols, j).to_broadcast([P, LAST]))
            return wide

        def pick_scaled(j, half, wide, pool, offset):
            ms = halves[half]
            enc[j, half] = pool.tile([P, ms.stop - ms.start], F32, name="enc%d_%d" % (j, half), align_bytes=64, offset=offset)
            offsets = pos2_sb[:, ms.start // 16 : ms.stop // 16]
            nc.vector.tensor_tensor(enc[j, half][:], h[j][:].indirect(offsets), wide[:, 0 : ms.stop - ms.start], ALU.mult)

        def finish_half(j, half):
            ms = halves[half]
            res = keep.tile([P, ms.stop - ms.start], F32, name="res%d_%d" % (j, half))
            nc.vector.scalar_tensor_tensor(res[:], banks[j][:, ms], col(b2_cols, j), enc[j, half][:], ALU.add, ALU.max)
            nc.sync.dma_start(out_rows[j // 4, j % 4][:, ms], res[:])

        for b in range(2):
            for half in range(2):
                cast_w2(w2_bf0[:, :, b, half * N // 2 : (half + 1) * N // 2], w2_half[b, half], 0, 4, True)
        cast_w2(w2_bf1[0][:], w2_raw[1, 0], 0, 4, True)
        for j in range(4):
            encode(j)
        for u in range(2):
            squash_pair(u)
        make_x_first()
        cast_w2(w2_bf1[1][:], w2_raw[1, 1], 0, 2, True)
        for j in range(3):
            pick_skip(j, picks, 2 * KB * j)
        for j in range(4, 8):
            encode(j)
        for j in range(4, 7):
            squash(j)
        scale_row(0)
        squash(7)
        make_x(1, 0, SPLIT)
        for t in range(1, 4):
            scale_row(t)
        interleave_rows()
        for j in range(3, 6):
            pick_skip(j, picks, 2 * KB * (j + 1))
        quantize_w2(0, 0, 4, w2_bf0[:, 0:2].rearrange("p t b n -> p (t b n)"), late, KB)
        quantize_x(0)
        quantize_w2(1, 4, 6, w2_bf1[1][:].rearrange("p t n -> p (t n)"), late, KB + N)
        quantize_x(1)
        quantize_w2(0, 4, 8, w2_bf0[:, 2:4].rearrange("p t b n -> p (t b n)"), picks, 20 * KB)
        cast_w2(w2_bf1[2][:], w2_raw[1, 1], 2, 4, False)
        for j in range(2):
            scale_skip(j, late, 2 * KB * (j + 1))
        for part, c0, c1 in ((0, 0, 4), (2, 6, 8)):
            quantize_w2(1, c0, c1, w2_bf1[part][:].rearrange("p t n -> p (t n)"), picks, 20 * KB + N + P * c0)
        pick_skip(6, late, 18 * KB)
        for j in range(8):
            project(j)
        whole = slice(0, M)
        aside = ((0, whole),)
        for j, ms in aside:
            subtract_aside(j, ms)
        for j in range(2, 5):
            scale_skip(j, stage0, 2 * KB * (j - 2))
        add_aside(0, whole)
        scale_skip(5, stage0, 6 * KB)
        scale_skip(6, stage1, 0)
        wide = spread_skip(7)
        nc.scalar.dma_start(out_rows[0, 0], done[0][:])
        for j in range(1, 5):
            finish(j, whole)
        pick_first_half(7, 10 * KB)
        for j in range(5, 7):
            finish(j, whole)
        pick_scaled(7, 1, wide, stage0, 6 * KB)
        finish_half(7, 0)
        finish_half(7, 1)
